import numpy as np
import ml_dtypes


def mxq(x, axis, fmt="e4m3"):
    dtype, down = {"e4m3": (ml_dtypes.float8_e4m3fn, 7), "e5m2": (ml_dtypes.float8_e5m2, 14)}[fmt]
    v = np.moveaxis(np.asarray(x, np.float32).astype(ml_dtypes.bfloat16).astype(np.float64), axis, -1)
    blocks = v.reshape(v.shape[:-1] + (-1, 32))
    amax = np.abs(blocks).max(-1, keepdims=True)
    byte = np.maximum(np.where(amax > 0, np.frexp(amax)[1] - 1 + 127, 0) - down, 1)
    scale = np.exp2(byte - 127.0)
    codes = (blocks / scale).astype(np.float32).astype(dtype).astype(np.float64)
    return np.moveaxis((codes * scale).reshape(v.shape), -1, axis)


WIDE = False


def mx_kscale(k):
    if not WIDE:
        return np.ones(k)
    levels = np.array([18, -18])
    if k % 512:
        return np.exp2(np.random.permutation(np.resize(levels, k // 32))).repeat(32)
    a = np.empty((k // 512, 16))
    for p in range(k // 512):
        a[p, :8] = np.random.permutation(np.resize(levels, 8))
        for g in range(8):
            far = levels[np.abs(levels - a[p, g]) >= 10]
            a[p, g + 8] = far[np.random.randint(len(far))]
    return np.exp2(a.ravel()).repeat(32)


def f64(x):
    return np.asarray(x).astype(np.float64)


def striped(idx):
    return np.tile(np.asarray(idx).reshape(-1, 16).T, (8, 1)).astype(np.uint16)


def unstriped(offs):
    return offs[:16].T.reshape(-1).astype(np.int64)


E2M1 = np.array([0.0, 0.5, 1.0, 1.5, 2.0, 3.0, 4.0, 6.0, -0.0, -0.5, -1.0, -1.5, -2.0, -3.0, -4.0, -6.0])


def pack_weight(w, fmt):
    k, n = w.shape
    w = f64(np.asarray(w, np.float32).astype(ml_dtypes.bfloat16)).reshape(k // 32, 32, n)
    amax = np.abs(w).max(1)
    if fmt == "e4m3":
        byte = np.frexp(amax)[1] - 1 + 127 - 7
    else:
        mant, ex = np.frexp(amax / 6.0)
        byte = np.where(mant > 0.5, ex, ex - 1) + 127
    byte = np.clip(np.where(amax > 0, byte, 1), 1, 254)
    scaled = (w * np.exp2(127.0 - byte)[:, None, :]).reshape(k, n).astype(np.float32)
    by_word = np.ascontiguousarray(scaled.reshape(k // 512, 128, 4, n).transpose(0, 1, 3, 2))
    if fmt == "e4m3":
        words = by_word.astype(ml_dtypes.float8_e4m3fn).view(np.uint8)
    else:
        c = by_word.astype(ml_dtypes.float4_e2m1fn).view(np.uint8) & 0xF
        words = (c[..., 0::2] | (c[..., 1::2] << 4)).reshape(k // 512, 128, 2 * n)
    return np.ascontiguousarray(words), np.ascontiguousarray(byte.astype(np.uint8).reshape(k // 512, 16, n))


def unpack_weight(words, scales, fmt):
    g, _, n = scales.shape
    words = np.ascontiguousarray(words).reshape(g, 128, n, -1)
    if fmt == "e4m3":
        vals = words.view(ml_dtypes.float8_e4m3fn).astype(np.float64)
    else:
        nib = np.empty((g, 128, n, 4), np.uint8)
        nib[..., 0::2] = words & 0xF
        nib[..., 1::2] = words >> 4
        vals = E2M1[nib]
    vals = vals * np.repeat(np.exp2(scales.astype(np.float64) - 127.0), 8, axis=1)[..., None]
    return vals.transpose(0, 1, 3, 2).reshape(g * 512, n)


B, N, T, D, R = 1, 512, 2048, 1024, 512


def setup_inputs():
    n = np.random.standard_normal
    idx = np.random.permutation(T)[:B * N]
    s = mx_kscale(D)[:, None]
    z = mx_kscale(R)[:, None]
    x = n((B, D, R))
    teach = np.exp(n((B, R, N)))
    teach = teach / teach.sum(-1, keepdims=True)
    wp = pack_weight(n((D, T)) * (0.50 / np.sqrt(D)) / s, "e2m1")
    return {
        "xT": (x * s).astype(np.float32),
        "w_words": np.ascontiguousarray(wp[0].reshape(1, 2, 128, T, 2).transpose(0, 2, 3, 1, 4)).reshape(1, 128, T, 4),
        "w_scales": wp[1],
        "y": teach.astype(np.float32),
        "wt": (np.random.uniform(0.5, 1.5, (B, R, 1)) * N / np.sqrt(R) * z).astype(np.float32),
        "kb": np.tile(0.5 * n(T), (128, 1)).astype(np.float32),
        "xm": (x.transpose(0, 2, 1) / z).astype(np.float32),
        "offs": striped(idx),
    }


def reference(xT, w_words, w_scales, y, wt, kb, xm, offs):
    idx = unstriped(offs)
    w = unpack_weight(w_words.reshape(1, 128, T, 2, 2).transpose(0, 3, 1, 2, 4).reshape(2, 128, 2 * T), w_scales, "e2m1")
    pick = lambda x: x[:, idx].reshape(x.shape[0], B, N).transpose(1, 0, 2)
    a = mxq(f64(xT), 1, "e4m3").transpose(0, 2, 1) @ pick(w)
    a = a + pick(f64(kb))[:, :1, :]
    e = np.exp(a - a.max(-1, keepdims=True))
    g = f64(wt) * (e / e.sum(-1, keepdims=True) - f64(y))
    dw = mxq(f64(xm), 1, "e4m3").transpose(0, 2, 1) @ mxq(g, 1, "e5m2")
    gw = np.zeros((D, T))
    gw[:, idx] = dw.transpose(1, 0, 2).reshape(D, B * N)
    return gw

@@ -1,0 +1,205 @@
+from contextlib import ExitStack
+
+import concourse.mybir as mybir
+from concourse.masks import make_identity
+
+F32 = mybir.dt.float32
+BF16 = mybir.dt.bfloat16
+I32 = mybir.dt.int32
+U32 = mybir.dt.uint32
+U16 = mybir.dt.uint16
+U8 = mybir.dt.uint8
+E4M3 = mybir.dt.float8_e4m3fn_x4
+E5M2 = mybir.dt.float8_e5m2_x4
+E2M1 = mybir.dt.float4_e2m1fn_x4
+ALU = mybir.AluOpType
+ACT = mybir.ActivationFunctionType
+AX = mybir.AxisListType
+
+P = 128
+PACK = 4
+N, T, D, R = 512, 2048, 1024, 512
+PASSES = D // (P * PACK)
+WINDOWS = 3
+XM_LOADS = 2
+XM_PIECE = 256
+G_SPLIT = 88
+
+FLOPS = 2 * 2 * R * D * N
+
+
+def tile_attend_gkl_w_kb_kernel(tc, xT, w_words, w_scales, y, wt, kb, xm, offs, out):
+    nc = tc.nc
+    with ExitStack() as ctx:
+        keep = ctx.enter_context(tc.tile_pool(name="keep", bufs=1))
+        ring = ctx.enter_context(tc.tile_pool(name="ring", bufs=3))
+        psum = ctx.enter_context(tc.psum_pool(name="psum", bufs=1))
+
+        offsets = keep.tile([P, N // 16], U16, name="offsets")
+        nc.sync.dma_start(offsets[:], offs)
+
+        scale_pool = keep.tile([P, T // 4], I32, name="scale_pool", align_bytes=64)
+        for q in range(4):
+            nc.sync.dma_start(scale_pool[32 * q + 24 : 32 * q + 32, :], w_scales.bitcast(I32)[:, 4 * q : 4 * q + 4, :])
+            nc.gpsimd.memset(scale_pool[32 * q : 32 * q + 24, :], 0)
+        kb_pool = keep.tile([P, T], F32, name="kb_pool", tag="kb_xm", align_bytes=64)
+        nc.sync.dma_start(kb_pool[P - 1 : P, :], kb[0:1, :])
+        nc.gpsimd.memset(kb_pool[0 : P - 1, :], 0.0)
+        word_pool = keep.tile([P, T], I32, name="word_pool", tag="words_y", align_bytes=64)
+        nc.sync.dma_start(word_pool[:], w_words[0].rearrange("p n t -> p (n t)").bitcast(I32))
+        x_raw = []
+        for o in range(PASSES):
+            raw = keep.tile([P, PACK, R], F32, name=f"x_raw{o}", tag=f"x{o}_xm", align_bytes=64)
+            nc.sync.dma_start(raw[:], xT[0, 512 * o : 512 * (o + 1), :].rearrange("(p j) r -> p j r", j=PACK))
+            x_raw.append(raw)
+        wt_sb = keep.tile([P, PACK], F32, name="wt_sb")
+        nc.scalar.dma_start(wt_sb[:], wt[0].rearrange("(p t) one -> p (t one)", t=PACK))
+        identity = keep.tile([P, P], F32, name="identity")
+        make_identity(nc, identity[:])
+
+        warm2 = keep.tile([P, 1], F32, name="warm2")
+        nc.scalar.activation(warm2[:], wt_sb[:, 0:1], ACT.Exp, scale=0.0)
+
+        planes = keep.tile([P, PASSES, N // 4], I32, name="planes", align_bytes=64)
+        nc.vector.memset(planes[96:P], 0)
+
+        both = keep.tile([P, N], U8, name="both", align_bytes=64)
+        nc.vector.tensor_copy(both[:], scale_pool[:].bitcast(U8).indirect(offsets[:]))
+        for o in range(PASSES):
+            nc.scalar.dma_start(planes[0:100, o, :], both[24 + 4 * o : 124 + 4 * o, :].bitcast(I32))
+        w_planes = [planes[:, o, :].bitcast(U8) for o in range(PASSES)]
+        windows = [keep.tile([P, T], F32, name="window0")]
+        nc.vector.memset(windows[0][:], 0.0)
+
+        pairs = keep.tile([P, N], U32, name="pairs", align_bytes=64)
+        nc.vector.tensor_copy(pairs[:], word_pool[:].bitcast(U32).indirect(offsets[:]))
+        w_codes = keep.tile([P, PASSES * 2 * N], U8, name="w_codes", align_bytes=64)
+        nc.vector.tensor_copy(
+            w_codes[:].bitcast(U16).rearrange("p (o n) -> p o n", o=PASSES),
+            pairs[:].bitcast(U16).rearrange("p (n o) -> p o n", o=PASSES),
+        )
+        y_sb = keep.tile([P, PACK, N], F32, name="y_sb", tag="words_y", align_bytes=64)
+        nc.sync.dma_start(y_sb[:], y[0].rearrange("(p t) i -> p t i", t=PACK))
+        kb_g = keep.tile([P, N], F32, name="kb_g")
+        nc.vector.tensor_copy(kb_g[:], kb_pool[:].indirect(offsets[:]))
+        xm_raw = []
+        xm_w = D // XM_LOADS
+        for h, tag in enumerate(("kb_xm", "x0_xm")):
+            raw = keep.tile([P, PACK, xm_w], F32, name=f"xm_raw{h}", tag=tag, align_bytes=64)
+            nc.sync.dma_start(raw[:], xm[0, :, h * xm_w : (h + 1) * xm_w].rearrange("(p t) d -> p t d", t=PACK))
+            xm_raw.append(raw)
+
+        acc = [psum.tile([P, N], F32, name=f"acc{k}") for k in range(4)]
+        for c in range(N // P):
+            nc.tensor.transpose(acc[0][:, c * P : (c + 1) * P], kb_g[:, c * P : (c + 1) * P], identity[:])
+        kb_col = keep.tile([P, N // P], F32, name="kb_col")
+        nc.scalar.copy(kb_col[:], acc[0][:, P - 1 : N : P])
+        for c in range(N // P):
+            nc.tensor.transpose(acc[1][:, c * P : (c + 1) * P], kb_col[:, c : c + 1].to_broadcast([P, P]), identity[:])
+        kb_all = keep.tile([P, N], F32, name="kb_all")
+        nc.scalar.copy(kb_all[:], acc[1][:])
+
+        x_codes, x_planes = {}, {}
+        for o in range(PASSES):
+            for h in range(2):
+                grouped = keep.tile([P, 2 * P * PACK], BF16, name=f"x_grouped{o}{h}", tag=f"xg{o}{h}", align_bytes=64)
+                dst = grouped[:].rearrange("p (t m j) -> p m t j", t=2, j=PACK)
+                src = x_raw[o][:].rearrange("p j (m t) -> p m t j", t=PACK)[:, :, 2 * h : 2 * h + 2, :]
+                if h == 0:
+                    nc.vector.tensor_copy(dst, src)
+                else:
+                    nc.scalar.copy(dst, src)
+                codes = keep.tile([P, 2 * P], U32, name=f"x_codes{o}{h}", align_bytes=64)
+                plane = keep.tile([P, 2 * P], U8, name=f"x_plane{o}{h}", align_bytes=64)
+                nc.vector.quantize_mx(out=codes[:].bitcast(E4M3), scales=plane[:], in_=grouped[:])
+                x_codes[o, h], x_planes[o, h] = codes, plane
+
+        scores = [psum.tile([P, N], F32, name=f"scores{t}") for t in range(PACK)]
+        for o in range(PASSES):
+            for t in range(PACK):
+                cols = slice((t % 2) * P, (t % 2 + 1) * P)
+                nc.tensor.matmul_mx(
+                    out=scores[t][:],
+                    lhsT=x_codes[o, t // 2][:, cols].bitcast(E4M3),
+                    lhsT_scale=x_planes[o, t // 2][:, cols],
+                    rhs=w_codes[:, o * 2 * N : (o + 1) * 2 * N].bitcast(E2M1),
+                    rhs_scale=w_planes[o],
+                    start=(o == 0),
+                    stop=(o == PASSES - 1),
+                )
+
+        for k in range(1, WINDOWS):
+            win = keep.tile([P, T], F32, name=f"window{k}", tag="xg11" if k == 1 else "xg10", align_bytes=64)
+            nc.gpsimd.memset(win[:], 0.0)
+            windows.append(win)
+
+        neg_z = [keep.tile([P, N], F32, name=f"neg_z{t}") for t in range(PACK)]
+        neg_m = [keep.tile([P, 1], F32, name=f"neg_m{t}") for t in range(PACK)]
+        e = [keep.tile([P, N], F32, name=f"e{t}") for t in range(PACK)]
+        wy = [keep.tile([P, N], F32, name=f"wy{t}") for t in range(PACK)]
+        sums = [keep.tile([P, 2], F32, name=f"sums{h}") for h in range(2)]
+
+        def add_bias(t):
+            nc.vector.scalar_tensor_tensor(neg_z[t][:], scores[t][:], -1.0, kb_all[:], ALU.mult, ALU.subtract)
+
+        def exp_row(t):
+            nc.vector.tensor_reduce(neg_m[t][:], neg_z[t][:], AX.X, ALU.min)
+            nc.scalar.activation(
+                e[t][:], neg_z[t][:], ACT.Exp, bias=neg_m[t][:], scale=-1.0,
+                accum_out=sums[t // 2][:, t % 2 : t % 2 + 1],
+            )
+
+        for t in range(PACK):
+            nc.scalar.activation(wy[t][:], y_sb[:, t, :], ACT.Copy, scale=wt_sb[:, t : t + 1])
+        add_bias(0)
+        for t in range(PACK):
+            if t + 1 < PACK:
+                add_bias(t + 1)
+            exp_row(t)
+
+        g_rows = keep.tile([P, PACK, N], BF16, name="g_rows", align_bytes=64)
+        for h in range(2):
+            inv = keep.tile([P, 2], F32, name=f"inv{h}")
+            nc.vector.reciprocal(inv[:], sums[h][:])
+            coef = keep.tile([P, 2], F32, name=f"coef{h}")
+            nc.vector.tensor_tensor(coef[:], inv[:], wt_sb[:, 2 * h : 2 * h + 2], ALU.mult)
+            for u in range(2):
+                t = 2 * h + u
+                nc.vector.scalar_tensor_tensor(g_rows[:, t, :], e[t][:], coef[:, u : u + 1], wy[t][:], ALU.mult, ALU.subtract)
+        g_grouped = keep.tile([P, N * PACK], BF16, name="g_grouped", align_bytes=64)
+        g_dst = g_grouped[:].rearrange("p (c i t) -> p c t i", i=4, t=PACK)
+        g_src = g_rows[:].rearrange("p t (c i) -> p c t i", i=4)
+        nc.vector.tensor_copy(g_dst[:, :G_SPLIT], g_src[:, :G_SPLIT])
+        nc.scalar.copy(g_dst[:, G_SPLIT:], g_src[:, G_SPLIT:])
+        g_codes = keep.tile([P, N], U32, name="g_codes", align_bytes=64)
+        g_plane = keep.tile([P, N], U8, name="g_plane", align_bytes=64)
+        nc.vector.quantize_mx(out=g_codes[:].bitcast(E5M2), scales=g_plane[:], in_=g_grouped[:])
+
+        per_load = xm_w // XM_PIECE
+        for c in range(D // XM_PIECE):
+            h, u = divmod(c, per_load)
+            grouped = keep.tile([P, XM_PIECE * PACK], BF16, name=f"xm_grouped{c}", align_bytes=64)
+            nc.scalar.copy(
+                grouped[:].rearrange("p (d t) -> p d t", t=PACK),
+                xm_raw[h][:, :, u * XM_PIECE : (u + 1) * XM_PIECE].rearrange("p t d -> p d t"),
+            )
+            codes = keep.tile([P, XM_PIECE], U32, name=f"xm_codes{c}", align_bytes=64)
+            plane = keep.tile([P, XM_PIECE], U8, name=f"xm_plane{c}", align_bytes=64)
+            nc.vector.quantize_mx(out=codes[:].bitcast(E4M3), scales=plane[:], in_=grouped[:])
+            for v in range(XM_PIECE // P):
+                b = c * (XM_PIECE // P) + v
+                cols = slice(v * P, (v + 1) * P)
+                nc.tensor.matmul_mx(
+                    out=acc[b % 4][:],
+                    lhsT=codes[:, cols].bitcast(E4M3),
+                    lhsT_scale=plane[:, cols],
+                    rhs=g_codes[:].bitcast(E5M2),
+                    rhs_scale=g_plane[:],
+                    start=True,
+                    stop=True,
+                )
+                dense = ring.tile([P, N], F32, name="dense")
+                nc.scalar.copy(dense[:], acc[b % 4][:])
+                win = windows[b % WINDOWS]
+                nc.vector.tensor_copy(win[:].indirect(offsets[:]), dense[:])
+                nc.sync.dma_start(out[b * P : (b + 1) * P, :], win[:])

@@ -22,7 +22,8 @@ N, T, D, R = 512, 2048, 1024, 512
 PASSES = D // (P * PACK)
 WINDOWS = 3
 XM_LOADS = 2
-XM_PIECE = 256
+X_LOADS = (1, 2)
+XM_GROUPS = (1, 1, 2, 4)
 G_SPLIT = 88
 
 FLOPS = 2 * 2 * R * D * N
@@ -38,56 +39,63 @@ def tile_attend_gkl_w_kb_kernel(tc, xT, w_words, w_scales, y, wt, kb, xm, offs, 
         offsets = keep.tile([P, N // 16], U16, name="offsets")
         nc.sync.dma_start(offsets[:], offs)
 
-        scale_pool = keep.tile([P, T // 4], I32, name="scale_pool", align_bytes=64)
+        warm = keep.tile([P, 1], F32, name="warm")
+        nc.vector.memset(warm[:], 0.0)
+        kb_pool = keep.tile([P, T], F32, name="kb_pool", align_bytes=64)
+        nc.scalar.dma_start(kb_pool[P - 1 : P, :], kb[0:1, :])
+        nc.vector.memset(kb_pool[0 : P - 1, :], 0.0)
+        scale_pool = keep.tile([P, T // 4], I32, name="scale_pool", tag="scales_pairs", align_bytes=64)
         for q in range(4):
-            nc.sync.dma_start(scale_pool[32 * q + 24 : 32 * q + 32, :], w_scales.bitcast(I32)[:, 4 * q : 4 * q + 4, :])
-            nc.gpsimd.memset(scale_pool[32 * q : 32 * q + 24, :], 0)
-        kb_pool = keep.tile([P, T], F32, name="kb_pool", tag="kb_xm", align_bytes=64)
-        nc.sync.dma_start(kb_pool[P - 1 : P, :], kb[0:1, :])
-        nc.gpsimd.memset(kb_pool[0 : P - 1, :], 0.0)
+            nc.scalar.dma_start(scale_pool[32 * q + 24 : 32 * q + 32, :], w_scales.bitcast(I32)[:, 4 * q : 4 * q + 4, :])
+            nc.vector.memset(scale_pool[32 * q : 32 * q + 24, :], 0)
         word_pool = keep.tile([P, T], I32, name="word_pool", tag="words_y", align_bytes=64)
         nc.sync.dma_start(word_pool[:], w_words[0].rearrange("p n t -> p (n t)").bitcast(I32))
         x_raw = []
-        for o in range(PASSES):
-            raw = keep.tile([P, PACK, R], F32, name=f"x_raw{o}", tag=f"x{o}_xm", align_bytes=64)
-            nc.sync.dma_start(raw[:], xT[0, 512 * o : 512 * (o + 1), :].rearrange("(p j) r -> p j r", j=PACK))
-            x_raw.append(raw)
+        for o, pieces in enumerate(X_LOADS):
+            rows = xT[0, 512 * o : 512 * (o + 1), :].rearrange("(p j) r -> p j r", j=PACK)
+            width = R // pieces
+            for u in range(pieces):
+                raw = keep.tile([P, PACK, width], F32, name=f"x_raw{o}{u}", tag=f"x{o}{u}_xm", align_bytes=64)
+                nc.sync.dma_start(raw[:], rows[:, :, u * width : (u + 1) * width])
+                x_raw.append((o, u * width // PACK, width // PACK, raw))
         wt_sb = keep.tile([P, PACK], F32, name="wt_sb")
-        nc.scalar.dma_start(wt_sb[:], wt[0].rearrange("(p t) one -> p (t one)", t=PACK))
+        nc.gpsimd.dma_start(wt_sb[:], wt[0].rearrange("(p t) one -> p (t one)", t=PACK))
         identity = keep.tile([P, P], F32, name="identity")
         make_identity(nc, identity[:])
 
         warm2 = keep.tile([P, 1], F32, name="warm2")
-        nc.scalar.activation(warm2[:], wt_sb[:, 0:1], ACT.Exp, scale=0.0)
+        nc.scalar.activation(warm2[:], warm[:], ACT.Exp)
 
         planes = keep.tile([P, PASSES, N // 4], I32, name="planes", align_bytes=64)
         nc.vector.memset(planes[96:P], 0)
 
+        windows = [keep.tile([P, T], F32, name="window0")]
+        nc.vector.memset(windows[0][:], 0.0)
+        kb_g = keep.tile([P, N], F32, name="kb_g")
+        nc.vector.tensor_copy(kb_g[:], kb_pool[:].indirect(offsets[:]))
         both = keep.tile([P, N], U8, name="both", align_bytes=64)
         nc.vector.tensor_copy(both[:], scale_pool[:].bitcast(U8).indirect(offsets[:]))
         for o in range(PASSES):
             nc.scalar.dma_start(planes[0:100, o, :], both[24 + 4 * o : 124 + 4 * o, :].bitcast(I32))
         w_planes = [planes[:, o, :].bitcast(U8) for o in range(PASSES)]
-        windows = [keep.tile([P, T], F32, name="window0")]
-        nc.vector.memset(windows[0][:], 0.0)
 
-        pairs = keep.tile([P, N], U32, name="pairs", align_bytes=64)
+        pairs = keep.tile([P, N], U32, name="pairs", tag="scales_pairs", align_bytes=64)
         nc.vector.tensor_copy(pairs[:], word_pool[:].bitcast(U32).indirect(offsets[:]))
         w_codes = keep.tile([P, PASSES * 2 * N], U8, name="w_codes", align_bytes=64)
         nc.vector.tensor_copy(
             w_codes[:].bitcast(U16).rearrange("p (o n) -> p o n", o=PASSES),
             pairs[:].bitcast(U16).rearrange("p (n o) -> p o n", o=PASSES),
         )
-        y_sb = keep.tile([P, PACK, N], F32, name="y_sb", tag="words_y", align_bytes=64)
-        nc.sync.dma_start(y_sb[:], y[0].rearrange("(p t) i -> p t i", t=PACK))
-        kb_g = keep.tile([P, N], F32, name="kb_g")
-        nc.vector.tensor_copy(kb_g[:], kb_pool[:].indirect(offsets[:]))
-        xm_raw = []
         xm_w = D // XM_LOADS
-        for h, tag in enumerate(("kb_xm", "x0_xm")):
+        xm_raw = []
+
+        def load_xm(h, tag):
             raw = keep.tile([P, PACK, xm_w], F32, name=f"xm_raw{h}", tag=tag, align_bytes=64)
             nc.sync.dma_start(raw[:], xm[0, :, h * xm_w : (h + 1) * xm_w].rearrange("(p t) d -> p t d", t=PACK))
             xm_raw.append(raw)
+
+        y_sb = keep.tile([P, PACK, N], F32, name="y_sb", tag="words_y", align_bytes=64)
+        nc.sync.dma_start(y_sb[:], y[0].rearrange("(p t) i -> p t i", t=PACK))
 
         acc = [psum.tile([P, N], F32, name=f"acc{k}") for k in range(4)]
         for c in range(N // P):
@@ -103,17 +111,22 @@ def tile_attend_gkl_w_kb_kernel(tc, xT, w_words, w_scales, y, wt, kb, xm, offs, 
         for o in range(PASSES):
             for h in range(2):
                 grouped = keep.tile([P, 2 * P * PACK], BF16, name=f"x_grouped{o}{h}", tag=f"xg{o}{h}", align_bytes=64)
-                dst = grouped[:].rearrange("p (t m j) -> p m t j", t=2, j=PACK)
-                src = x_raw[o][:].rearrange("p j (m t) -> p m t j", t=PACK)[:, :, 2 * h : 2 * h + 2, :]
-                if h == 0:
-                    nc.vector.tensor_copy(dst, src)
-                else:
-                    nc.scalar.copy(dst, src)
+                for o_raw, m0, width, raw in x_raw:
+                    if o_raw != o:
+                        continue
+                    dst = grouped[:].rearrange("p (t m j) -> p m t j", t=2, j=PACK)[:, m0 : m0 + width]
+                    src = raw[:].rearrange("p j (m t) -> p m t j", t=PACK)[:, :, 2 * h : 2 * h + 2, :]
+                    if h == 0:
+                        nc.vector.tensor_copy(dst, src)
+                    else:
+                        nc.scalar.copy(dst, src)
                 codes = keep.tile([P, 2 * P], U32, name=f"x_codes{o}{h}", align_bytes=64)
                 plane = keep.tile([P, 2 * P], U8, name=f"x_plane{o}{h}", align_bytes=64)
                 nc.vector.quantize_mx(out=codes[:].bitcast(E4M3), scales=plane[:], in_=grouped[:])
                 x_codes[o, h], x_planes[o, h] = codes, plane
 
+        load_xm(0, "x00_xm")
+        load_xm(1, "x10_xm")
         scores = [psum.tile([P, N], F32, name=f"scores{t}") for t in range(PACK)]
         for o in range(PASSES):
             for t in range(PACK):
@@ -128,16 +141,19 @@ def tile_attend_gkl_w_kb_kernel(tc, xT, w_words, w_scales, y, wt, kb, xm, offs, 
                     stop=(o == PASSES - 1),
                 )
 
-        for k in range(1, WINDOWS):
-            win = keep.tile([P, T], F32, name=f"window{k}", tag="xg11" if k == 1 else "xg10", align_bytes=64)
+        def zeroed_window(k, tag):
+            win = keep.tile([P, T], F32, name=f"window{k}", tag=tag, align_bytes=64)
             nc.gpsimd.memset(win[:], 0.0)
             windows.append(win)
 
         neg_z = [keep.tile([P, N], F32, name=f"neg_z{t}") for t in range(PACK)]
         neg_m = [keep.tile([P, 1], F32, name=f"neg_m{t}") for t in range(PACK)]
-        e = [keep.tile([P, N], F32, name=f"e{t}") for t in range(PACK)]
-        wy = [keep.tile([P, N], F32, name=f"wy{t}") for t in range(PACK)]
+        e = [keep.tile([P, N], F32, name=f"e{t}", tag=f"e{t}", align_bytes=64) for t in range(PACK)]
+        wy = [keep.tile([P, N], F32, name=f"wy{t}", tag=f"wy{t}", align_bytes=64) for t in range(PACK)]
         sums = [keep.tile([P, 2], F32, name=f"sums{h}") for h in range(2)]
+        inv = [keep.tile([P, 2], F32, name=f"inv{h}") for h in range(2)]
+        coef = [keep.tile([P, 2], F32, name=f"coef{h}") for h in range(2)]
+        g_rows = keep.tile([P, PACK, N], BF16, name="g_rows", tag="g_rows", align_bytes=64)
 
         def add_bias(t):
             nc.vector.scalar_tensor_tensor(neg_z[t][:], scores[t][:], -1.0, kb_all[:], ALU.mult, ALU.subtract)
@@ -149,57 +165,81 @@ def tile_attend_gkl_w_kb_kernel(tc, xT, w_words, w_scales, y, wt, kb, xm, offs, 
                 accum_out=sums[t // 2][:, t % 2 : t % 2 + 1],
             )
 
-        for t in range(PACK):
-            nc.scalar.activation(wy[t][:], y_sb[:, t, :], ACT.Copy, scale=wt_sb[:, t : t + 1])
-        add_bias(0)
-        for t in range(PACK):
-            if t + 1 < PACK:
-                add_bias(t + 1)
-            exp_row(t)
+        def invert(h):
+            nc.vector.reciprocal(inv[h][:], sums[h][:])
 
-        g_rows = keep.tile([P, PACK, N], BF16, name="g_rows", align_bytes=64)
-        for h in range(2):
-            inv = keep.tile([P, 2], F32, name=f"inv{h}")
-            nc.vector.reciprocal(inv[:], sums[h][:])
-            coef = keep.tile([P, 2], F32, name=f"coef{h}")
-            nc.vector.tensor_tensor(coef[:], inv[:], wt_sb[:, 2 * h : 2 * h + 2], ALU.mult)
-            for u in range(2):
-                t = 2 * h + u
-                nc.vector.scalar_tensor_tensor(g_rows[:, t, :], e[t][:], coef[:, u : u + 1], wy[t][:], ALU.mult, ALU.subtract)
+        def weigh(h):
+            nc.vector.tensor_tensor(coef[h][:], inv[h][:], wt_sb[:, 2 * h : 2 * h + 2], ALU.mult)
+
+        def gradient(t):
+            nc.vector.scalar_tensor_tensor(
+                g_rows[:, t, :], e[t][:], coef[t // 2][:, t % 2 : t % 2 + 1], wy[t][:], ALU.mult, ALU.subtract
+            )
+
+        zeroed_window(1, "xg11")
+        for t in range(PACK):
+            nc.gpsimd.tensor_scalar(wy[t][:], y_sb[:, t, :], wt_sb[:, t : t + 1], 0.0, ALU.mult, ALU.add)
+        zeroed_window(2, "xg10")
+        add_bias(0)
+        add_bias(1)
+        exp_row(0)
+        add_bias(2)
+        exp_row(1)
+        add_bias(3)
+        exp_row(2)
+        invert(0)
+        exp_row(3)
+        weigh(0)
+        gradient(0)
+        invert(1)
+        gradient(1)
+        weigh(1)
+        gradient(2)
+        gradient(3)
+
         g_grouped = keep.tile([P, N * PACK], BF16, name="g_grouped", align_bytes=64)
         g_dst = g_grouped[:].rearrange("p (c i t) -> p c t i", i=4, t=PACK)
         g_src = g_rows[:].rearrange("p t (c i) -> p c t i", i=4)
         nc.vector.tensor_copy(g_dst[:, :G_SPLIT], g_src[:, :G_SPLIT])
         nc.scalar.copy(g_dst[:, G_SPLIT:], g_src[:, G_SPLIT:])
+
+        xm_q = []
+
+        def quantize_xm(first, count, tag):
+            grouped = keep.tile([P, count * P * PACK], BF16, name=f"xm_grouped{first}", align_bytes=64)
+            for u in range(count):
+                h, d0 = divmod((first + u) * P, xm_w)
+                nc.scalar.copy(
+                    grouped[:, u * P * PACK : (u + 1) * P * PACK].rearrange("p (d t) -> p d t", t=PACK),
+                    xm_raw[h][:, :, d0 : d0 + P].rearrange("p t d -> p d t"),
+                )
+            codes = keep.tile([P, count * P], U32, name=f"xm_codes{first}", tag=tag, align_bytes=64)
+            plane = keep.tile([P, count * P], U8, name=f"xm_plane{first}", align_bytes=64)
+            nc.vector.quantize_mx(out=codes[:].bitcast(E4M3), scales=plane[:], in_=grouped[:])
+            for u in range(count):
+                xm_q.append((codes[:, u * P : (u + 1) * P], plane[:, u * P : (u + 1) * P]))
+
+        quantize_xm(0, 1, "e3")
         g_codes = keep.tile([P, N], U32, name="g_codes", align_bytes=64)
         g_plane = keep.tile([P, N], U8, name="g_plane", align_bytes=64)
         nc.vector.quantize_mx(out=g_codes[:].bitcast(E5M2), scales=g_plane[:], in_=g_grouped[:])
+        quantize_xm(1, 1, "wy3")
+        quantize_xm(2, 2, "e2")
+        quantize_xm(4, 4, "g_rows")
 
-        per_load = xm_w // XM_PIECE
-        for c in range(D // XM_PIECE):
-            h, u = divmod(c, per_load)
-            grouped = keep.tile([P, XM_PIECE * PACK], BF16, name=f"xm_grouped{c}", align_bytes=64)
-            nc.scalar.copy(
-                grouped[:].rearrange("p (d t) -> p d t", t=PACK),
-                xm_raw[h][:, :, u * XM_PIECE : (u + 1) * XM_PIECE].rearrange("p t d -> p d t"),
+        for b in range(D // P):
+            codes, plane = xm_q[b]
+            nc.tensor.matmul_mx(
+                out=acc[b % 4][:],
+                lhsT=codes.bitcast(E4M3),
+                lhsT_scale=plane,
+                rhs=g_codes[:].bitcast(E5M2),
+                rhs_scale=g_plane[:],
+                start=True,
+                stop=True,
             )
-            codes = keep.tile([P, XM_PIECE], U32, name=f"xm_codes{c}", align_bytes=64)
-            plane = keep.tile([P, XM_PIECE], U8, name=f"xm_plane{c}", align_bytes=64)
-            nc.vector.quantize_mx(out=codes[:].bitcast(E4M3), scales=plane[:], in_=grouped[:])
-            for v in range(XM_PIECE // P):
-                b = c * (XM_PIECE // P) + v
-                cols = slice(v * P, (v + 1) * P)
-                nc.tensor.matmul_mx(
-                    out=acc[b % 4][:],
-                    lhsT=codes[:, cols].bitcast(E4M3),
-                    lhsT_scale=plane[:, cols],
-                    rhs=g_codes[:].bitcast(E5M2),
-                    rhs_scale=g_plane[:],
-                    start=True,
-                    stop=True,
-                )
-                dense = ring.tile([P, N], F32, name="dense")
-                nc.scalar.copy(dense[:], acc[b % 4][:])
-                win = windows[b % WINDOWS]
-                nc.vector.tensor_copy(win[:].indirect(offsets[:]), dense[:])
-                nc.sync.dma_start(out[b * P : (b + 1) * P, :], win[:])
+            dense = ring.tile([P, N], F32, name="dense")
+            nc.scalar.copy(dense[:], acc[b % 4][:])
+            win = windows[b % WINDOWS]
+            nc.vector.tensor_copy(win[:].indirect(offsets[:]), dense[:])
+            nc.sync.dma_start(out[b * P : (b + 1) * P, :], win[:])

@@ -41,25 +41,25 @@ def tile_attend_gkl_w_kb_kernel(tc, xT, w_words, w_scales, y, wt, kb, xm, offs, 
 
         warm = keep.tile([P, 1], F32, name="warm")
         nc.vector.memset(warm[:], 0.0)
-        kb_pool = keep.tile([P, T], F32, name="kb_pool", align_bytes=64)
+        kb_pool = keep.tile([P, T], F32, name="kb_pool", tag="x10", align_bytes=64)
         nc.scalar.dma_start(kb_pool[P - 1 : P, :], kb[0:1, :])
         nc.vector.memset(kb_pool[0 : P - 1, :], 0.0)
-        scale_pool = keep.tile([P, T // 4], I32, name="scale_pool", tag="scales_pairs", align_bytes=64)
+        scale_pool = keep.tile([P, T // 4], I32, name="scale_pool", tag="x11", align_bytes=64)
         for q in range(4):
             nc.scalar.dma_start(scale_pool[32 * q + 24 : 32 * q + 32, :], w_scales.bitcast(I32)[:, 4 * q : 4 * q + 4, :])
             nc.vector.memset(scale_pool[32 * q : 32 * q + 24, :], 0)
         word_pool = keep.tile([P, T], I32, name="word_pool", tag="words_y", align_bytes=64)
         nc.sync.dma_start(word_pool[:], w_words[0].rearrange("p n t -> p (n t)").bitcast(I32))
         x_raw = []
-        for o, pieces in enumerate(X_LOADS):
+
+        def load_x(o, u, pieces):
             rows = xT[0, 512 * o : 512 * (o + 1), :].rearrange("(p j) r -> p j r", j=PACK)
             width = R // pieces
-            for u in range(pieces):
-                raw = keep.tile([P, PACK, width], F32, name=f"x_raw{o}{u}", tag=f"x{o}{u}_xm", align_bytes=64)
-                nc.sync.dma_start(raw[:], rows[:, :, u * width : (u + 1) * width])
-                x_raw.append((o, u * width // PACK, width // PACK, raw))
-        wt_sb = keep.tile([P, PACK], F32, name="wt_sb")
-        nc.gpsimd.dma_start(wt_sb[:], wt[0].rearrange("(p t) one -> p (t one)", t=PACK))
+            raw = keep.tile([P, PACK, width], F32, name=f"x_raw{o}{u}", tag=f"x{o}{u}", align_bytes=64)
+            nc.sync.dma_start(raw[:], rows[:, :, u * width : (u + 1) * width])
+            x_raw.append((o, u * width // PACK, width // PACK, raw))
+
+        load_x(0, 0, 1)
         identity = keep.tile([P, P], F32, name="identity")
         make_identity(nc, identity[:])
 
@@ -73,13 +73,15 @@ def tile_attend_gkl_w_kb_kernel(tc, xT, w_words, w_scales, y, wt, kb, xm, offs, 
         nc.vector.memset(windows[0][:], 0.0)
         kb_g = keep.tile([P, N], F32, name="kb_g")
         nc.vector.tensor_copy(kb_g[:], kb_pool[:].indirect(offsets[:]))
+        load_x(1, 0, 2)
         both = keep.tile([P, N], U8, name="both", align_bytes=64)
         nc.vector.tensor_copy(both[:], scale_pool[:].bitcast(U8).indirect(offsets[:]))
         for o in range(PASSES):
             nc.scalar.dma_start(planes[0:100, o, :], both[24 + 4 * o : 124 + 4 * o, :].bitcast(I32))
         w_planes = [planes[:, o, :].bitcast(U8) for o in range(PASSES)]
 
-        pairs = keep.tile([P, N], U32, name="pairs", tag="scales_pairs", align_bytes=64)
+        load_x(1, 1, 2)
+        pairs = keep.tile([P, N], U32, name="pairs", tag="pairs_wt", align_bytes=64)
         nc.vector.tensor_copy(pairs[:], word_pool[:].bitcast(U32).indirect(offsets[:]))
         w_codes = keep.tile([P, PASSES * 2 * N], U8, name="w_codes", align_bytes=64)
         nc.vector.tensor_copy(
@@ -97,6 +99,15 @@ def tile_attend_gkl_w_kb_kernel(tc, xT, w_words, w_scales, y, wt, kb, xm, offs, 
         y_sb = keep.tile([P, PACK, N], F32, name="y_sb", tag="words_y", align_bytes=64)
         nc.sync.dma_start(y_sb[:], y[0].rearrange("(p t) i -> p t i", t=PACK))
 
+        wt_sb = keep.tile([P, PACK], F32, name="wt_sb", tag="pairs_wt", align_bytes=64)
+        nc.sync.dma_start(wt_sb[:], wt[0].rearrange("(p t) one -> p (t one)", t=PACK))
+
+        def zeroed_window(k):
+            win = keep.tile([P, T], F32, name=f"window{k}")
+            nc.vector.memset(win[:], 0.0)
+            windows.append(win)
+
+        zeroed_window(1)
         acc = [psum.tile([P, N], F32, name=f"acc{k}") for k in range(4)]
         for c in range(N // P):
             nc.tensor.transpose(acc[0][:, c * P : (c + 1) * P], kb_g[:, c * P : (c + 1) * P], identity[:])
@@ -110,7 +121,7 @@ def tile_attend_gkl_w_kb_kernel(tc, xT, w_words, w_scales, y, wt, kb, xm, offs, 
         x_codes, x_planes = {}, {}
         for o in range(PASSES):
             for h in range(2):
-                grouped = keep.tile([P, 2 * P * PACK], BF16, name=f"x_grouped{o}{h}", tag=f"xg{o}{h}", align_bytes=64)
+                grouped = keep.tile([P, 2 * P * PACK], BF16, name=f"x_grouped{o}{h}", align_bytes=64)
                 for o_raw, m0, width, raw in x_raw:
                     if o_raw != o:
                         continue
@@ -125,8 +136,8 @@ def tile_attend_gkl_w_kb_kernel(tc, xT, w_words, w_scales, y, wt, kb, xm, offs, 
                 nc.vector.quantize_mx(out=codes[:].bitcast(E4M3), scales=plane[:], in_=grouped[:])
                 x_codes[o, h], x_planes[o, h] = codes, plane
 
-        load_xm(0, "x00_xm")
-        load_xm(1, "x10_xm")
+        load_xm(0, "x00")
+        load_xm(1, "x10")
         scores = [psum.tile([P, N], F32, name=f"scores{t}") for t in range(PACK)]
         for o in range(PASSES):
             for t in range(PACK):
@@ -141,13 +152,8 @@ def tile_attend_gkl_w_kb_kernel(tc, xT, w_words, w_scales, y, wt, kb, xm, offs, 
                     stop=(o == PASSES - 1),
                 )
 
-        def zeroed_window(k, tag):
-            win = keep.tile([P, T], F32, name=f"window{k}", tag=tag, align_bytes=64)
-            nc.gpsimd.memset(win[:], 0.0)
-            windows.append(win)
-
-        neg_z = [keep.tile([P, N], F32, name=f"neg_z{t}") for t in range(PACK)]
-        neg_m = [keep.tile([P, 1], F32, name=f"neg_m{t}") for t in range(PACK)]
+        neg_z = [keep.tile([P, N], F32, name=f"neg_z{t}", tag=f"neg_z{t}", align_bytes=64) for t in range(PACK)]
+        neg_m = [keep.tile([P, 1], F32, name=f"neg_m{t}", tag=f"neg_m{t}", align_bytes=64) for t in range(PACK)]
         e = [keep.tile([P, N], F32, name=f"e{t}", tag=f"e{t}", align_bytes=64) for t in range(PACK)]
         wy = [keep.tile([P, N], F32, name=f"wy{t}", tag=f"wy{t}", align_bytes=64) for t in range(PACK)]
         sums = [keep.tile([P, 2], F32, name=f"sums{h}") for h in range(2)]
@@ -176,10 +182,8 @@ def tile_attend_gkl_w_kb_kernel(tc, xT, w_words, w_scales, y, wt, kb, xm, offs, 
                 g_rows[:, t, :], e[t][:], coef[t // 2][:, t % 2 : t % 2 + 1], wy[t][:], ALU.mult, ALU.subtract
             )
 
-        zeroed_window(1, "xg11")
         for t in range(PACK):
-            nc.gpsimd.tensor_scalar(wy[t][:], y_sb[:, t, :], wt_sb[:, t : t + 1], 0.0, ALU.mult, ALU.add)
-        zeroed_window(2, "xg10")
+            nc.scalar.activation(wy[t][:], y_sb[:, t, :], ACT.Copy, scale=wt_sb[:, t : t + 1])
         add_bias(0)
         add_bias(1)
         exp_row(0)
@@ -197,7 +201,7 @@ def tile_attend_gkl_w_kb_kernel(tc, xT, w_words, w_scales, y, wt, kb, xm, offs, 
         gradient(2)
         gradient(3)
 
-        g_grouped = keep.tile([P, N * PACK], BF16, name="g_grouped", align_bytes=64)
+        g_grouped = keep.tile([P, N * PACK], BF16, name="g_grouped", tag="g_grouped", align_bytes=64)
         g_dst = g_grouped[:].rearrange("p (c i t) -> p c t i", i=4, t=PACK)
         g_src = g_rows[:].rearrange("p t (c i) -> p c t i", i=4)
         nc.vector.tensor_copy(g_dst[:, :G_SPLIT], g_src[:, :G_SPLIT])
@@ -205,8 +209,8 @@ def tile_attend_gkl_w_kb_kernel(tc, xT, w_words, w_scales, y, wt, kb, xm, offs, 
 
         xm_q = []
 
-        def quantize_xm(first, count, tag):
-            grouped = keep.tile([P, count * P * PACK], BF16, name=f"xm_grouped{first}", align_bytes=64)
+        def quantize_xm(first, count, grouped_tag, tag):
+            grouped = keep.tile([P, count * P * PACK], BF16, name=f"xm_grouped{first}", tag=grouped_tag, align_bytes=64)
             for u in range(count):
                 h, d0 = divmod((first + u) * P, xm_w)
                 nc.scalar.copy(
@@ -219,15 +223,19 @@ def tile_attend_gkl_w_kb_kernel(tc, xT, w_words, w_scales, y, wt, kb, xm, offs, 
             for u in range(count):
                 xm_q.append((codes[:, u * P : (u + 1) * P], plane[:, u * P : (u + 1) * P]))
 
-        quantize_xm(0, 1, "e3")
+        quantize_xm(0, 1, "neg_z2", "e3")
         g_codes = keep.tile([P, N], U32, name="g_codes", align_bytes=64)
         g_plane = keep.tile([P, N], U8, name="g_plane", align_bytes=64)
         nc.vector.quantize_mx(out=g_codes[:].bitcast(E5M2), scales=g_plane[:], in_=g_grouped[:])
-        quantize_xm(1, 1, "wy3")
-        quantize_xm(2, 2, "e2")
-        quantize_xm(4, 4, "g_rows")
+        quantize_xm(1, 1, "neg_z3", "wy2")
+        quantize_xm(2, 2, "neg_m3", "e2")
+        win = keep.tile([P, T], F32, name="window2", tag="g_grouped", align_bytes=64)
+        nc.vector.memset(win[:], 0.0)
+        windows.append(win)
 
         for b in range(D // P):
+            if b == 1:
+                quantize_xm(4, 4, "wy3", "g_rows")
             codes, plane = xm_q[b]
             nc.tensor.matmul_mx(
                 out=acc[b % 4][:],

@@ -39,55 +39,84 @@ def tile_attend_gkl_w_kb_kernel(tc, xT, w_words, w_scales, y, wt, kb, xm, offs, 
         offsets = keep.tile([P, N // 16], U16, name="offsets")
         nc.sync.dma_start(offsets[:], offs)
 
-        warm = keep.tile([P, 1], F32, name="warm")
-        nc.vector.memset(warm[:], 0.0)
+        scale_pool = keep.tile([P, T // 4], I32, name="scale_pool", tag="x11", align_bytes=64)
+        nc.vector.memset(scale_pool[:], 0)
         kb_pool = keep.tile([P, T], F32, name="kb_pool", tag="x10", align_bytes=64)
         nc.scalar.dma_start(kb_pool[P - 1 : P, :], kb[0:1, :])
-        nc.vector.memset(kb_pool[0 : P - 1, :], 0.0)
-        scale_pool = keep.tile([P, T // 4], I32, name="scale_pool", tag="x11", align_bytes=64)
         for q in range(4):
-            nc.scalar.dma_start(scale_pool[32 * q + 24 : 32 * q + 32, :], w_scales.bitcast(I32)[:, 4 * q : 4 * q + 4, :])
-            nc.vector.memset(scale_pool[32 * q : 32 * q + 24, :], 0)
-        word_pool = keep.tile([P, T], I32, name="word_pool", tag="words_y", align_bytes=64)
-        nc.sync.dma_start(word_pool[:], w_words[0].rearrange("p n t -> p (n t)").bitcast(I32))
-        x_raw = []
+            nc.scalar.dma_start(scale_pool[32 * q : 32 * q + 8, :], w_scales.bitcast(I32)[:, 4 * q : 4 * q + 4, :])
+        x_raw = {}
 
         def load_x(o, u, pieces):
             rows = xT[0, 512 * o : 512 * (o + 1), :].rearrange("(p j) r -> p j r", j=PACK)
             width = R // pieces
             raw = keep.tile([P, PACK, width], F32, name=f"x_raw{o}{u}", tag=f"x{o}{u}", align_bytes=64)
             nc.sync.dma_start(raw[:], rows[:, :, u * width : (u + 1) * width])
-            x_raw.append((o, u * width // PACK, width // PACK, raw))
+            x_raw[o, u] = raw
 
         load_x(0, 0, 1)
+        word_pool = keep.tile([P, T], I32, name="word_pool", tag="words_xm", align_bytes=64)
+        nc.sync.dma_start(word_pool[:], w_words[0].rearrange("p n t -> p (n t)").bitcast(I32))
         identity = keep.tile([P, P], F32, name="identity")
         make_identity(nc, identity[:])
 
-        warm2 = keep.tile([P, 1], F32, name="warm2")
-        nc.scalar.activation(warm2[:], warm[:], ACT.Exp)
+        plane1 = keep.tile([P, N // 4], I32, name="plane1", align_bytes=64)
+        nc.vector.memset(plane1[96:P], 0)
+        warm = keep.tile([P, 1], F32, name="warm")
+        nc.scalar.activation(warm[:], identity[:, 0:1], ACT.Exp)
+        nc.vector.memset(kb_pool[0 : P - 1, :], 0.0)
+        windows = [keep.tile([P, T], F32, name=f"window{k}") for k in range(2)]
+        for win in windows:
+            nc.vector.memset(win[:], 0.0)
 
-        planes = keep.tile([P, PASSES, N // 4], I32, name="planes", align_bytes=64)
-        nc.vector.memset(planes[96:P], 0)
-
-        windows = [keep.tile([P, T], F32, name="window0")]
-        nc.vector.memset(windows[0][:], 0.0)
-        kb_g = keep.tile([P, N], F32, name="kb_g")
+        kb_g = keep.tile([P, N], F32, name="kb_g", tag="kb_wt", align_bytes=64)
         nc.vector.tensor_copy(kb_g[:], kb_pool[:].indirect(offsets[:]))
         load_x(1, 0, 2)
         both = keep.tile([P, N], U8, name="both", align_bytes=64)
         nc.vector.tensor_copy(both[:], scale_pool[:].bitcast(U8).indirect(offsets[:]))
-        for o in range(PASSES):
-            nc.scalar.dma_start(planes[0:100, o, :], both[24 + 4 * o : 124 + 4 * o, :].bitcast(I32))
-        w_planes = [planes[:, o, :].bitcast(U8) for o in range(PASSES)]
-
+        nc.sync.dma_start(plane1[0:112, :], both[4:116, :].bitcast(I32))
+        w_planes = [both[:], plane1[:].bitcast(U8)]
         load_x(1, 1, 2)
-        pairs = keep.tile([P, N], U32, name="pairs", tag="pairs_wt", align_bytes=64)
+
+        pairs = keep.tile([P, N], U32, name="pairs", align_bytes=64)
         nc.vector.tensor_copy(pairs[:], word_pool[:].bitcast(U32).indirect(offsets[:]))
         w_codes = keep.tile([P, PASSES * 2 * N], U8, name="w_codes", align_bytes=64)
         nc.vector.tensor_copy(
             w_codes[:].bitcast(U16).rearrange("p (o n) -> p o n", o=PASSES),
             pairs[:].bitcast(U16).rearrange("p (n o) -> p o n", o=PASSES),
         )
+
+        acc = [psum.tile([P, N], F32, name=f"acc{k}") for k in range(4)]
+        for c in range(N // P):
+            nc.tensor.transpose(acc[0][:, c * P : (c + 1) * P], kb_g[:, c * P : (c + 1) * P], identity[:])
+        wt_sb = keep.tile([P, PACK], F32, name="wt_sb", tag="kb_wt", align_bytes=64)
+        nc.sync.dma_start(wt_sb[:], wt[0].rearrange("(p t) one -> p (t one)", t=PACK))
+        kb_col = keep.tile([P, N // P], F32, name="kb_col")
+        nc.scalar.copy(kb_col[:], acc[0][:, P - 1 : N : P])
+        for c in range(N // P):
+            nc.tensor.transpose(acc[1][:, c * P : (c + 1) * P], kb_col[:, c : c + 1].to_broadcast([P, P]), identity[:])
+        kb_all = keep.tile([P, N], F32, name="kb_all")
+        nc.scalar.copy(kb_all[:], acc[1][:])
+
+        x_q = {}
+
+        def quantize_x(o, t0, count, copy):
+            grouped = keep.tile([P, count * P * PACK], BF16, name=f"x_grouped{o}{t0}", align_bytes=64)
+            pieces = X_LOADS[o]
+            width = P // pieces
+            for u in range(pieces):
+                dst = grouped[:].rearrange("p (t m j) -> p m t j", t=count, j=PACK)[:, u * width : (u + 1) * width]
+                src = x_raw[o, u][:].rearrange("p j (m t) -> p m t j", t=PACK)[:, :, t0 : t0 + count, :]
+                copy(dst, src)
+            codes = keep.tile([P, count * P], U32, name=f"x_codes{o}{t0}", align_bytes=64)
+            plane = keep.tile([P, count * P], U8, name=f"x_plane{o}{t0}", align_bytes=64)
+            nc.vector.quantize_mx(out=codes[:].bitcast(E4M3), scales=plane[:], in_=grouped[:])
+            for u in range(count):
+                x_q[o, t0 + u] = (codes[:, u * P : (u + 1) * P], plane[:, u * P : (u + 1) * P])
+
+        quantize_x(0, 0, 4, nc.scalar.copy)
+        y_sb = keep.tile([P, PACK, N], F32, name="y_sb", tag="x00", align_bytes=64)
+        nc.sync.dma_start(y_sb[:], y[0].rearrange("(p t) i -> p t i", t=PACK))
         xm_w = D // XM_LOADS
         xm_raw = []
 
@@ -96,56 +125,19 @@ def tile_attend_gkl_w_kb_kernel(tc, xT, w_words, w_scales, y, wt, kb, xm, offs, 
             nc.sync.dma_start(raw[:], xm[0, :, h * xm_w : (h + 1) * xm_w].rearrange("(p t) d -> p t d", t=PACK))
             xm_raw.append(raw)
 
-        y_sb = keep.tile([P, PACK, N], F32, name="y_sb", tag="words_y", align_bytes=64)
-        nc.sync.dma_start(y_sb[:], y[0].rearrange("(p t) i -> p t i", t=PACK))
-
-        wt_sb = keep.tile([P, PACK], F32, name="wt_sb", tag="pairs_wt", align_bytes=64)
-        nc.sync.dma_start(wt_sb[:], wt[0].rearrange("(p t) one -> p (t one)", t=PACK))
-
-        def zeroed_window(k):
-            win = keep.tile([P, T], F32, name=f"window{k}")
-            nc.vector.memset(win[:], 0.0)
-            windows.append(win)
-
-        zeroed_window(1)
-        acc = [psum.tile([P, N], F32, name=f"acc{k}") for k in range(4)]
-        for c in range(N // P):
-            nc.tensor.transpose(acc[0][:, c * P : (c + 1) * P], kb_g[:, c * P : (c + 1) * P], identity[:])
-        kb_col = keep.tile([P, N // P], F32, name="kb_col")
-        nc.scalar.copy(kb_col[:], acc[0][:, P - 1 : N : P])
-        for c in range(N // P):
-            nc.tensor.transpose(acc[1][:, c * P : (c + 1) * P], kb_col[:, c : c + 1].to_broadcast([P, P]), identity[:])
-        kb_all = keep.tile([P, N], F32, name="kb_all")
-        nc.scalar.copy(kb_all[:], acc[1][:])
-
-        x_codes, x_planes = {}, {}
-        for o in range(PASSES):
-            for h in range(2):
-                grouped = keep.tile([P, 2 * P * PACK], BF16, name=f"x_grouped{o}{h}", align_bytes=64)
-                for o_raw, m0, width, raw in x_raw:
-                    if o_raw != o:
-                        continue
-                    dst = grouped[:].rearrange("p (t m j) -> p m t j", t=2, j=PACK)[:, m0 : m0 + width]
-                    src = raw[:].rearrange("p j (m t) -> p m t j", t=PACK)[:, :, 2 * h : 2 * h + 2, :]
-                    if h == 0:
-                        nc.vector.tensor_copy(dst, src)
-                    else:
-                        nc.scalar.copy(dst, src)
-                codes = keep.tile([P, 2 * P], U32, name=f"x_codes{o}{h}", align_bytes=64)
-                plane = keep.tile([P, 2 * P], U8, name=f"x_plane{o}{h}", align_bytes=64)
-                nc.vector.quantize_mx(out=codes[:].bitcast(E4M3), scales=plane[:], in_=grouped[:])
-                x_codes[o, h], x_planes[o, h] = codes, plane
-
-        load_xm(0, "x00")
+        load_xm(0, "words_xm")
+        quantize_x(1, 0, 2, nc.vector.tensor_copy)
+        quantize_x(1, 2, 2, nc.scalar.copy)
         load_xm(1, "x10")
+
         scores = [psum.tile([P, N], F32, name=f"scores{t}") for t in range(PACK)]
-        for o in range(PASSES):
-            for t in range(PACK):
-                cols = slice((t % 2) * P, (t % 2 + 1) * P)
+        for t in range(PACK):
+            for o in range(PASSES):
+                codes, plane = x_q[o, t]
                 nc.tensor.matmul_mx(
                     out=scores[t][:],
-                    lhsT=x_codes[o, t // 2][:, cols].bitcast(E4M3),
-                    lhsT_scale=x_planes[o, t // 2][:, cols],
+                    lhsT=codes.bitcast(E4M3),
+                    lhsT_scale=plane,
                     rhs=w_codes[:, o * 2 * N : (o + 1) * 2 * N].bitcast(E2M1),
                     rhs_scale=w_planes[o],
                     start=(o == 0),
@@ -182,31 +174,6 @@ def tile_attend_gkl_w_kb_kernel(tc, xT, w_words, w_scales, y, wt, kb, xm, offs, 
                 g_rows[:, t, :], e[t][:], coef[t // 2][:, t % 2 : t % 2 + 1], wy[t][:], ALU.mult, ALU.subtract
             )
 
-        for t in range(PACK):
-            nc.scalar.activation(wy[t][:], y_sb[:, t, :], ACT.Copy, scale=wt_sb[:, t : t + 1])
-        add_bias(0)
-        add_bias(1)
-        exp_row(0)
-        add_bias(2)
-        exp_row(1)
-        add_bias(3)
-        exp_row(2)
-        invert(0)
-        exp_row(3)
-        weigh(0)
-        gradient(0)
-        invert(1)
-        gradient(1)
-        weigh(1)
-        gradient(2)
-        gradient(3)
-
-        g_grouped = keep.tile([P, N * PACK], BF16, name="g_grouped", tag="g_grouped", align_bytes=64)
-        g_dst = g_grouped[:].rearrange("p (c i t) -> p c t i", i=4, t=PACK)
-        g_src = g_rows[:].rearrange("p t (c i) -> p c t i", i=4)
-        nc.vector.tensor_copy(g_dst[:, :G_SPLIT], g_src[:, :G_SPLIT])
-        nc.scalar.copy(g_dst[:, G_SPLIT:], g_src[:, G_SPLIT:])
-
         xm_q = []
 
         def quantize_xm(first, count, grouped_tag, tag):
@@ -223,7 +190,32 @@ def tile_attend_gkl_w_kb_kernel(tc, xT, w_words, w_scales, y, wt, kb, xm, offs, 
             for u in range(count):
                 xm_q.append((codes[:, u * P : (u + 1) * P], plane[:, u * P : (u + 1) * P]))
 
-        quantize_xm(0, 1, "neg_z2", "e3")
+        for t in range(PACK):
+            nc.scalar.activation(wy[t][:], y_sb[:, t, :], ACT.Copy, scale=wt_sb[:, t : t + 1])
+        add_bias(0)
+        add_bias(1)
+        exp_row(0)
+        add_bias(2)
+        exp_row(1)
+        add_bias(3)
+        exp_row(2)
+        invert(0)
+        exp_row(3)
+        weigh(0)
+        gradient(0)
+        invert(1)
+        gradient(1)
+        weigh(1)
+        quantize_xm(0, 1, "neg_z2", "e0")
+        gradient(2)
+        gradient(3)
+
+        g_grouped = keep.tile([P, N * PACK], BF16, name="g_grouped", tag="g_grouped", align_bytes=64)
+        g_dst = g_grouped[:].rearrange("p (c i t) -> p c t i", i=4, t=PACK)
+        g_src = g_rows[:].rearrange("p t (c i) -> p c t i", i=4)
+        nc.vector.tensor_copy(g_dst[:, :G_SPLIT], g_src[:, :G_SPLIT])
+        nc.scalar.copy(g_dst[:, G_SPLIT:], g_src[:, G_SPLIT:])
+
         g_codes = keep.tile([P, N], U32, name="g_codes", align_bytes=64)
         g_plane = keep.tile([P, N], U8, name="g_plane", align_bytes=64)
         nc.vector.quantize_mx(out=g_codes[:].bitcast(E5M2), scales=g_plane[:], in_=g_grouped[:])

@@ -18,12 +18,16 @@ AX = mybir.AxisListType
 
 P = 128
 PACK = 4
+K_PASS = P * PACK
 N, T, D, R = 512, 2048, 1024, 512
-PASSES = D // (P * PACK)
+PASSES = D // K_PASS
+QUADRANT = 32
+SCALE_ROWS = 4
+SHIFT_ROWS = 112
 WINDOWS = 3
-XM_LOADS = 2
 X_LOADS = (1, 2)
-XM_GROUPS = (1, 1, 2, 4)
+XM_LOADS = 2
+RUN = 4
 G_SPLIT = 88
 
 FLOPS = 2 * 2 * R * D * N
@@ -43,40 +47,41 @@ def tile_attend_gkl_w_kb_kernel(tc, xT, w_words, w_scales, y, wt, kb, xm, offs, 
         nc.vector.memset(scale_pool[:], 0)
         kb_pool = keep.tile([P, T], F32, name="kb_pool", tag="x10", align_bytes=64)
         nc.scalar.dma_start(kb_pool[P - 1 : P, :], kb[0:1, :])
-        for q in range(4):
-            nc.scalar.dma_start(scale_pool[32 * q : 32 * q + 8, :], w_scales.bitcast(I32)[:, 4 * q : 4 * q + 4, :])
+        for q in range(P // QUADRANT):
+            nc.scalar.dma_start(
+                scale_pool[QUADRANT * q : QUADRANT * q + PASSES * SCALE_ROWS, :],
+                w_scales.bitcast(I32)[:, SCALE_ROWS * q : SCALE_ROWS * (q + 1), :],
+            )
         x_raw = {}
 
-        def load_x(o, u, pieces):
-            rows = xT[0, 512 * o : 512 * (o + 1), :].rearrange("(p j) r -> p j r", j=PACK)
-            width = R // pieces
+        def load_x(o, u):
+            rows = xT[0, K_PASS * o : K_PASS * (o + 1), :].rearrange("(p j) r -> p j r", j=PACK)
+            width = R // X_LOADS[o]
             raw = keep.tile([P, PACK, width], F32, name=f"x_raw{o}{u}", tag=f"x{o}{u}", align_bytes=64)
             nc.sync.dma_start(raw[:], rows[:, :, u * width : (u + 1) * width])
             x_raw[o, u] = raw
 
-        load_x(0, 0, 1)
+        load_x(0, 0)
         word_pool = keep.tile([P, T], I32, name="word_pool", tag="words_xm", align_bytes=64)
         nc.sync.dma_start(word_pool[:], w_words[0].rearrange("p n t -> p (n t)").bitcast(I32))
         identity = keep.tile([P, P], F32, name="identity")
         make_identity(nc, identity[:])
 
         plane1 = keep.tile([P, N // 4], I32, name="plane1", align_bytes=64)
-        nc.vector.memset(plane1[96:P], 0)
-        warm = keep.tile([P, 1], F32, name="warm")
-        nc.scalar.activation(warm[:], identity[:, 0:1], ACT.Exp)
+        nc.vector.memset(plane1[P - QUADRANT : P], 0)
         nc.vector.memset(kb_pool[0 : P - 1, :], 0.0)
-        windows = [keep.tile([P, T], F32, name=f"window{k}") for k in range(2)]
+        windows = [keep.tile([P, T], F32, name=f"window{k}") for k in range(WINDOWS - 1)]
         for win in windows:
             nc.vector.memset(win[:], 0.0)
 
         kb_g = keep.tile([P, N], F32, name="kb_g", tag="kb_wt", align_bytes=64)
         nc.vector.tensor_copy(kb_g[:], kb_pool[:].indirect(offsets[:]))
-        load_x(1, 0, 2)
+        load_x(1, 0)
         both = keep.tile([P, N], U8, name="both", align_bytes=64)
         nc.vector.tensor_copy(both[:], scale_pool[:].bitcast(U8).indirect(offsets[:]))
-        nc.sync.dma_start(plane1[0:112, :], both[4:116, :].bitcast(I32))
+        nc.sync.dma_start(plane1[0:SHIFT_ROWS, :], both[SCALE_ROWS : SCALE_ROWS + SHIFT_ROWS, :].bitcast(I32))
         w_planes = [both[:], plane1[:].bitcast(U8)]
-        load_x(1, 1, 2)
+        load_x(1, 1)
 
         pairs = keep.tile([P, N], U32, name="pairs", align_bytes=64)
         nc.vector.tensor_copy(pairs[:], word_pool[:].bitcast(U32).indirect(offsets[:]))
@@ -114,7 +119,7 @@ def tile_attend_gkl_w_kb_kernel(tc, xT, w_words, w_scales, y, wt, kb, xm, offs, 
             for u in range(count):
                 x_q[o, t0 + u] = (codes[:, u * P : (u + 1) * P], plane[:, u * P : (u + 1) * P])
 
-        quantize_x(0, 0, 4, nc.scalar.copy)
+        quantize_x(0, 0, PACK, nc.scalar.copy)
         y_sb = keep.tile([P, PACK, N], F32, name="y_sb", tag="x00", align_bytes=64)
         nc.sync.dma_start(y_sb[:], y[0].rearrange("(p t) i -> p t i", t=PACK))
         xm_w = D // XM_LOADS
@@ -126,8 +131,8 @@ def tile_attend_gkl_w_kb_kernel(tc, xT, w_words, w_scales, y, wt, kb, xm, offs, 
             xm_raw.append(raw)
 
         load_xm(0, "words_xm")
-        quantize_x(1, 0, 2, nc.vector.tensor_copy)
-        quantize_x(1, 2, 2, nc.scalar.copy)
+        quantize_x(1, 0, PACK // 2, nc.vector.tensor_copy)
+        quantize_x(1, PACK // 2, PACK // 2, nc.scalar.copy)
         load_xm(1, "x10")
 
         scores = [psum.tile([P, N], F32, name=f"scores{t}") for t in range(PACK)]
@@ -176,7 +181,7 @@ def tile_attend_gkl_w_kb_kernel(tc, xT, w_words, w_scales, y, wt, kb, xm, offs, 
 
         xm_q = []
 
-        def quantize_xm(first, count, grouped_tag, tag):
+        def quantize_xm(first, count, grouped_tag, codes_tag):
             grouped = keep.tile([P, count * P * PACK], BF16, name=f"xm_grouped{first}", tag=grouped_tag, align_bytes=64)
             for u in range(count):
                 h, d0 = divmod((first + u) * P, xm_w)
@@ -184,7 +189,7 @@ def tile_attend_gkl_w_kb_kernel(tc, xT, w_words, w_scales, y, wt, kb, xm, offs, 
                     grouped[:, u * P * PACK : (u + 1) * P * PACK].rearrange("p (d t) -> p d t", t=PACK),
                     xm_raw[h][:, :, d0 : d0 + P].rearrange("p t d -> p d t"),
                 )
-            codes = keep.tile([P, count * P], U32, name=f"xm_codes{first}", tag=tag, align_bytes=64)
+            codes = keep.tile([P, count * P], U32, name=f"xm_codes{first}", tag=codes_tag, align_bytes=64)
             plane = keep.tile([P, count * P], U8, name=f"xm_plane{first}", align_bytes=64)
             nc.vector.quantize_mx(out=codes[:].bitcast(E4M3), scales=plane[:], in_=grouped[:])
             for u in range(count):
@@ -193,14 +198,11 @@ def tile_attend_gkl_w_kb_kernel(tc, xT, w_words, w_scales, y, wt, kb, xm, offs, 
         for t in range(PACK):
             nc.scalar.activation(wy[t][:], y_sb[:, t, :], ACT.Copy, scale=wt_sb[:, t : t + 1])
         add_bias(0)
-        add_bias(1)
-        exp_row(0)
-        add_bias(2)
-        exp_row(1)
-        add_bias(3)
-        exp_row(2)
+        for t in range(PACK - 1):
+            add_bias(t + 1)
+            exp_row(t)
         invert(0)
-        exp_row(3)
+        exp_row(PACK - 1)
         weigh(0)
         gradient(0)
         invert(1)
@@ -211,8 +213,8 @@ def tile_attend_gkl_w_kb_kernel(tc, xT, w_words, w_scales, y, wt, kb, xm, offs, 
         gradient(3)
 
         g_grouped = keep.tile([P, N * PACK], BF16, name="g_grouped", tag="g_grouped", align_bytes=64)
-        g_dst = g_grouped[:].rearrange("p (c i t) -> p c t i", i=4, t=PACK)
-        g_src = g_rows[:].rearrange("p t (c i) -> p c t i", i=4)
+        g_dst = g_grouped[:].rearrange("p (c i t) -> p c t i", i=RUN, t=PACK)
+        g_src = g_rows[:].rearrange("p t (c i) -> p c t i", i=RUN)
         nc.vector.tensor_copy(g_dst[:, :G_SPLIT], g_src[:, :G_SPLIT])
         nc.scalar.copy(g_dst[:, G_SPLIT:], g_src[:, G_SPLIT:])
 
@@ -221,16 +223,15 @@ def tile_attend_gkl_w_kb_kernel(tc, xT, w_words, w_scales, y, wt, kb, xm, offs, 
         nc.vector.quantize_mx(out=g_codes[:].bitcast(E5M2), scales=g_plane[:], in_=g_grouped[:])
         quantize_xm(1, 1, "neg_z3", "wy2")
         quantize_xm(2, 2, "neg_m3", "e2")
-        win = keep.tile([P, T], F32, name="window2", tag="g_grouped", align_bytes=64)
-        nc.vector.memset(win[:], 0.0)
-        windows.append(win)
+        last_window = keep.tile([P, T], F32, name="window2", tag="g_grouped", align_bytes=64)
+        nc.vector.memset(last_window[:], 0.0)
+        windows.append(last_window)
 
-        for b in range(D // P):
-            if b == 1:
-                quantize_xm(4, 4, "wy3", "g_rows")
+        def output_block(b):
             codes, plane = xm_q[b]
+            bank = acc[b % len(acc)]
             nc.tensor.matmul_mx(
-                out=acc[b % 4][:],
+                out=bank[:],
                 lhsT=codes.bitcast(E4M3),
                 lhsT_scale=plane,
                 rhs=g_codes[:].bitcast(E5M2),
@@ -239,7 +240,12 @@ def tile_attend_gkl_w_kb_kernel(tc, xT, w_words, w_scales, y, wt, kb, xm, offs, 
                 stop=True,
             )
             dense = ring.tile([P, N], F32, name="dense")
-            nc.scalar.copy(dense[:], acc[b % 4][:])
-            win = windows[b % WINDOWS]
-            nc.vector.tensor_copy(win[:].indirect(offsets[:]), dense[:])
-            nc.sync.dma_start(out[b * P : (b + 1) * P, :], win[:])
+            nc.scalar.copy(dense[:], bank[:])
+            window = windows[b % WINDOWS]
+            nc.vector.tensor_copy(window[:].indirect(offsets[:]), dense[:])
+            nc.sync.dma_start(out[b * P : (b + 1) * P, :], window[:])
+
+        output_block(0)
+        quantize_xm(4, 4, "wy3", "g_rows")
+        for b in range(1, D // P):
+            output_block(b)

@@ -43,15 +43,13 @@ def tile_attend_gkl_w_kb_kernel(tc, xT, w_words, w_scales, y, wt, kb, xm, offs, 
         offsets = keep.tile([P, N // 16], U16, name="offsets")
         nc.sync.dma_start(offsets[:], offs)
 
-        scale_pool = keep.tile([P, T // 4], I32, name="scale_pool", tag="x11", align_bytes=64)
-        nc.vector.memset(scale_pool[:], 0)
+        scale_pool = keep.tile([P, T // 4], I32, name="scale_pool", align_bytes=64)
+        nc.gpsimd.memset(scale_pool[:], 0)
+        identity = keep.tile([P, P], F32, name="identity")
+        make_identity(nc, identity[:])
         kb_pool = keep.tile([P, T], F32, name="kb_pool", tag="x10", align_bytes=64)
         nc.scalar.dma_start(kb_pool[P - 1 : P, :], kb[0:1, :])
-        for q in range(P // QUADRANT):
-            nc.scalar.dma_start(
-                scale_pool[QUADRANT * q : QUADRANT * q + PASSES * SCALE_ROWS, :],
-                w_scales.bitcast(I32)[:, SCALE_ROWS * q : SCALE_ROWS * (q + 1), :],
-            )
+        nc.vector.memset(kb_pool[0 : P - 1, :], 0.0)
         x_raw = {}
 
         def load_x(o, u):
@@ -62,78 +60,80 @@ def tile_attend_gkl_w_kb_kernel(tc, xT, w_words, w_scales, y, wt, kb, xm, offs, 
             x_raw[o, u] = raw
 
         load_x(0, 0)
-        word_pool = keep.tile([P, T], I32, name="word_pool", tag="words_xm", align_bytes=64)
+        for q in range(P // QUADRANT):
+            nc.sync.dma_start(
+                scale_pool[QUADRANT * q : QUADRANT * q + PASSES * SCALE_ROWS, :],
+                w_scales.bitcast(I32)[:, SCALE_ROWS * q : SCALE_ROWS * (q + 1), :],
+            )
+        word_pool = keep.tile([P, T], I32, name="word_pool", tag="y", align_bytes=64)
         nc.sync.dma_start(word_pool[:], w_words[0].rearrange("p n t -> p (n t)").bitcast(I32))
-        identity = keep.tile([P, P], F32, name="identity")
-        make_identity(nc, identity[:])
-
         plane1 = keep.tile([P, N // 4], I32, name="plane1", align_bytes=64)
         nc.vector.memset(plane1[P - QUADRANT : P], 0)
-        nc.vector.memset(kb_pool[0 : P - 1, :], 0.0)
-        windows = [keep.tile([P, T], F32, name=f"window{k}") for k in range(WINDOWS - 1)]
-        for win in windows:
-            nc.vector.memset(win[:], 0.0)
+        windows = [keep.tile([P, T], F32, name="window0")]
+        nc.vector.memset(windows[0][:], 0.0)
 
-        kb_g = keep.tile([P, N], F32, name="kb_g", tag="kb_wt", align_bytes=64)
+        kb_g = keep.tile([P, N], F32, name="kb_g", tag="x11", align_bytes=64)
         nc.vector.tensor_copy(kb_g[:], kb_pool[:].indirect(offsets[:]))
         load_x(1, 0)
+        acc = [psum.tile([P, N], F32, name=f"acc{k}") for k in range(4)]
+        for c in range(N // P):
+            nc.tensor.transpose(acc[0][:, c * P : (c + 1) * P], kb_g[:, c * P : (c + 1) * P], identity[:])
+        load_x(1, 1)
         both = keep.tile([P, N], U8, name="both", align_bytes=64)
         nc.vector.tensor_copy(both[:], scale_pool[:].bitcast(U8).indirect(offsets[:]))
-        nc.sync.dma_start(plane1[0:SHIFT_ROWS, :], both[SCALE_ROWS : SCALE_ROWS + SHIFT_ROWS, :].bitcast(I32))
+        nc.gpsimd.dma_start(plane1[0:SHIFT_ROWS, :], both[SCALE_ROWS : SCALE_ROWS + SHIFT_ROWS, :].bitcast(I32))
         w_planes = [both[:], plane1[:].bitcast(U8)]
-        load_x(1, 1)
+        kb_col = keep.tile([P, N // P], F32, name="kb_col", tag="wt", align_bytes=64)
+        nc.vector.tensor_copy(kb_col[:], acc[0][:, P - 1 : N : P])
+        for c in range(N // P):
+            nc.tensor.transpose(acc[1][:, c * P : (c + 1) * P], kb_col[:, c : c + 1].to_broadcast([P, P]), identity[:])
+        kb_all = keep.tile([P, N], F32, name="kb_all")
+        nc.vector.tensor_copy(kb_all[:], acc[1][:])
+        wt_sb = keep.tile([P, PACK], F32, name="wt_sb", tag="wt", align_bytes=64)
+        nc.sync.dma_start(wt_sb[:], wt[0].rearrange("(p t) one -> p (t one)", t=PACK))
 
         pairs = keep.tile([P, N], U32, name="pairs", align_bytes=64)
         nc.vector.tensor_copy(pairs[:], word_pool[:].bitcast(U32).indirect(offsets[:]))
-        w_codes = keep.tile([P, PASSES * 2 * N], U8, name="w_codes", align_bytes=64)
+        y_sb = keep.tile([P, PACK, N], F32, name="y_sb", tag="y", align_bytes=64)
+        nc.sync.dma_start(y_sb[:], y[0].rearrange("(p t) i -> p t i", t=PACK))
+        w_codes = keep.tile([P, PASSES * 2 * N], U8, name="w_codes", tag="w_codes", align_bytes=64)
         nc.vector.tensor_copy(
             w_codes[:].bitcast(U16).rearrange("p (o n) -> p o n", o=PASSES),
             pairs[:].bitcast(U16).rearrange("p (n o) -> p o n", o=PASSES),
         )
 
-        acc = [psum.tile([P, N], F32, name=f"acc{k}") for k in range(4)]
-        for c in range(N // P):
-            nc.tensor.transpose(acc[0][:, c * P : (c + 1) * P], kb_g[:, c * P : (c + 1) * P], identity[:])
-        wt_sb = keep.tile([P, PACK], F32, name="wt_sb", tag="kb_wt", align_bytes=64)
-        nc.sync.dma_start(wt_sb[:], wt[0].rearrange("(p t) one -> p (t one)", t=PACK))
-        kb_col = keep.tile([P, N // P], F32, name="kb_col")
-        nc.scalar.copy(kb_col[:], acc[0][:, P - 1 : N : P])
-        for c in range(N // P):
-            nc.tensor.transpose(acc[1][:, c * P : (c + 1) * P], kb_col[:, c : c + 1].to_broadcast([P, P]), identity[:])
-        kb_all = keep.tile([P, N], F32, name="kb_all")
-        nc.scalar.copy(kb_all[:], acc[1][:])
-
         x_q = {}
 
-        def quantize_x(o, t0, count, copy):
-            grouped = keep.tile([P, count * P * PACK], BF16, name=f"x_grouped{o}{t0}", align_bytes=64)
-            pieces = X_LOADS[o]
-            width = P // pieces
-            for u in range(pieces):
-                dst = grouped[:].rearrange("p (t m j) -> p m t j", t=count, j=PACK)[:, u * width : (u + 1) * width]
-                src = x_raw[o, u][:].rearrange("p j (m t) -> p m t j", t=PACK)[:, :, t0 : t0 + count, :]
-                copy(dst, src)
-            codes = keep.tile([P, count * P], U32, name=f"x_codes{o}{t0}", align_bytes=64)
+        def group_x(grouped, o, u, t0, count, copy):
+            width = P // X_LOADS[o]
+            dst = grouped[:].rearrange("p (t m j) -> p m t j", t=count, j=PACK)[:, u * width : (u + 1) * width]
+            src = x_raw[o, u][:].rearrange("p j (m t) -> p m t j", t=PACK)[:, :, t0 : t0 + count, :]
+            copy(dst, src)
+
+        def quantize_x(grouped, o, t0, count):
+            codes = keep.tile([P, count * P], U32, name=f"x_codes{o}{t0}", tag=f"x_codes{o}{t0}", align_bytes=64)
             plane = keep.tile([P, count * P], U8, name=f"x_plane{o}{t0}", align_bytes=64)
             nc.vector.quantize_mx(out=codes[:].bitcast(E4M3), scales=plane[:], in_=grouped[:])
             for u in range(count):
                 x_q[o, t0 + u] = (codes[:, u * P : (u + 1) * P], plane[:, u * P : (u + 1) * P])
 
-        quantize_x(0, 0, PACK, nc.scalar.copy)
-        y_sb = keep.tile([P, PACK, N], F32, name="y_sb", tag="x00", align_bytes=64)
-        nc.sync.dma_start(y_sb[:], y[0].rearrange("(p t) i -> p t i", t=PACK))
+        grouped0 = keep.tile([P, PACK * P * PACK], BF16, name="x_grouped0", align_bytes=64)
+        group_x(grouped0, 0, 0, 0, PACK, nc.scalar.copy)
+        quantize_x(grouped0, 0, 0, PACK)
+        half = PACK // 2
+        grouped1 = [keep.tile([P, half * P * PACK], BF16, name=f"x_grouped1{h}", align_bytes=64) for h in range(2)]
+        for h in range(2):
+            group_x(grouped1[h], 1, 0, h * half, half, nc.scalar.copy)
         xm_w = D // XM_LOADS
         xm_raw = []
-
-        def load_xm(h, tag):
+        for h, tag in enumerate(("x00", "x10")):
             raw = keep.tile([P, PACK, xm_w], F32, name=f"xm_raw{h}", tag=tag, align_bytes=64)
             nc.sync.dma_start(raw[:], xm[0, :, h * xm_w : (h + 1) * xm_w].rearrange("(p t) d -> p t d", t=PACK))
             xm_raw.append(raw)
-
-        load_xm(0, "words_xm")
-        quantize_x(1, 0, PACK // 2, nc.vector.tensor_copy)
-        quantize_x(1, PACK // 2, PACK // 2, nc.scalar.copy)
-        load_xm(1, "x10")
+        group_x(grouped1[0], 1, 1, 0, half, nc.vector.tensor_copy)
+        group_x(grouped1[1], 1, 1, half, half, nc.scalar.copy)
+        for h in range(2):
+            quantize_x(grouped1[h], 1, h * half, half)
 
         scores = [psum.tile([P, N], F32, name=f"scores{t}") for t in range(PACK)]
         for t in range(PACK):
@@ -149,13 +149,17 @@ def tile_attend_gkl_w_kb_kernel(tc, xT, w_words, w_scales, y, wt, kb, xm, offs, 
                     stop=(o == PASSES - 1),
                 )
 
+        second_window = keep.tile([P, T], F32, name="window1", tag="w_codes", align_bytes=64)
+        nc.gpsimd.memset(second_window[:], 0.0)
+        windows.append(second_window)
+
         neg_z = [keep.tile([P, N], F32, name=f"neg_z{t}", tag=f"neg_z{t}", align_bytes=64) for t in range(PACK)]
         neg_m = [keep.tile([P, 1], F32, name=f"neg_m{t}", tag=f"neg_m{t}", align_bytes=64) for t in range(PACK)]
         e = [keep.tile([P, N], F32, name=f"e{t}", tag=f"e{t}", align_bytes=64) for t in range(PACK)]
         wy = [keep.tile([P, N], F32, name=f"wy{t}", tag=f"wy{t}", align_bytes=64) for t in range(PACK)]
-        sums = [keep.tile([P, 2], F32, name=f"sums{h}") for h in range(2)]
-        inv = [keep.tile([P, 2], F32, name=f"inv{h}") for h in range(2)]
-        coef = [keep.tile([P, 2], F32, name=f"coef{h}") for h in range(2)]
+        sums = [keep.tile([P, 1], F32, name=f"sums{t}") for t in range(PACK)]
+        inv = [keep.tile([P, 1], F32, name=f"inv{t}") for t in range(PACK)]
+        coef = [keep.tile([P, 1], F32, name=f"coef{t}") for t in range(PACK)]
         g_rows = keep.tile([P, PACK, N], BF16, name="g_rows", tag="g_rows", align_bytes=64)
 
         def add_bias(t):
@@ -165,18 +169,18 @@ def tile_attend_gkl_w_kb_kernel(tc, xT, w_words, w_scales, y, wt, kb, xm, offs, 
             nc.vector.tensor_reduce(neg_m[t][:], neg_z[t][:], AX.X, ALU.min)
             nc.scalar.activation(
                 e[t][:], neg_z[t][:], ACT.Exp, bias=neg_m[t][:], scale=-1.0,
-                accum_out=sums[t // 2][:, t % 2 : t % 2 + 1],
+                accum_out=sums[t][:],
             )
 
-        def invert(h):
-            nc.vector.reciprocal(inv[h][:], sums[h][:])
+        def invert(t):
+            nc.vector.reciprocal(inv[t][:], sums[t][:])
 
-        def weigh(h):
-            nc.vector.tensor_tensor(coef[h][:], inv[h][:], wt_sb[:, 2 * h : 2 * h + 2], ALU.mult)
+        def weigh(t):
+            nc.vector.tensor_tensor(coef[t][:], inv[t][:], wt_sb[:, t : t + 1], ALU.mult)
 
         def gradient(t):
             nc.vector.scalar_tensor_tensor(
-                g_rows[:, t, :], e[t][:], coef[t // 2][:, t % 2 : t % 2 + 1], wy[t][:], ALU.mult, ALU.subtract
+                g_rows[:, t, :], e[t][:], coef[t][:], wy[t][:], ALU.mult, ALU.subtract
             )
 
         xm_q = []
@@ -195,22 +199,20 @@ def tile_attend_gkl_w_kb_kernel(tc, xT, w_words, w_scales, y, wt, kb, xm, offs, 
             for u in range(count):
                 xm_q.append((codes[:, u * P : (u + 1) * P], plane[:, u * P : (u + 1) * P]))
 
-        for t in range(PACK):
-            nc.scalar.activation(wy[t][:], y_sb[:, t, :], ACT.Copy, scale=wt_sb[:, t : t + 1])
         add_bias(0)
         for t in range(PACK - 1):
             add_bias(t + 1)
             exp_row(t)
         invert(0)
         exp_row(PACK - 1)
-        weigh(0)
-        gradient(0)
-        invert(1)
-        gradient(1)
-        weigh(1)
-        quantize_xm(0, 1, "neg_z2", "e0")
-        gradient(2)
-        gradient(3)
+        for t in range(PACK):
+            nc.scalar.activation(wy[t][:], y_sb[:, t, :], ACT.Copy, scale=wt_sb[:, t : t + 1])
+        for t in range(PACK - 1):
+            weigh(t)
+            invert(t + 1)
+            gradient(t)
+        weigh(PACK - 1)
+        gradient(PACK - 1)
 
         g_grouped = keep.tile([P, N * PACK], BF16, name="g_grouped", tag="g_grouped", align_bytes=64)
         g_dst = g_grouped[:].rearrange("p (c i t) -> p c t i", i=RUN, t=PACK)
@@ -218,14 +220,14 @@ def tile_attend_gkl_w_kb_kernel(tc, xT, w_words, w_scales, y, wt, kb, xm, offs, 
         nc.vector.tensor_copy(g_dst[:, :G_SPLIT], g_src[:, :G_SPLIT])
         nc.scalar.copy(g_dst[:, G_SPLIT:], g_src[:, G_SPLIT:])
 
+        quantize_xm(0, 2, "neg_z3", "e3")
         g_codes = keep.tile([P, N], U32, name="g_codes", align_bytes=64)
         g_plane = keep.tile([P, N], U8, name="g_plane", align_bytes=64)
         nc.vector.quantize_mx(out=g_codes[:].bitcast(E5M2), scales=g_plane[:], in_=g_grouped[:])
-        quantize_xm(1, 1, "neg_z3", "wy2")
-        quantize_xm(2, 2, "neg_m3", "e2")
         last_window = keep.tile([P, T], F32, name="window2", tag="g_grouped", align_bytes=64)
         nc.vector.memset(last_window[:], 0.0)
         windows.append(last_window)
+        quantize_xm(2, 2, "g_rows", "e2")
 
         def output_block(b):
             codes, plane = xm_q[b]
@@ -246,6 +248,7 @@ def tile_attend_gkl_w_kb_kernel(tc, xT, w_words, w_scales, y, wt, kb, xm, offs, 
             nc.sync.dma_start(out[b * P : (b + 1) * P, :], window[:])
 
         output_block(0)
-        quantize_xm(4, 4, "wy3", "g_rows")
-        for b in range(1, D // P):
+        output_block(1)
+        quantize_xm(4, 4, "e3", "e1")
+        for b in range(2, D // P):
             output_block(b)

@@ -47,7 +47,7 @@ def tile_attend_gkl_w_kb_kernel(tc, xT, w_words, w_scales, y, wt, kb, xm, offs, 
         nc.gpsimd.memset(scale_pool[:], 0)
         identity = keep.tile([P, P], F32, name="identity")
         make_identity(nc, identity[:])
-        kb_pool = keep.tile([P, T], F32, name="kb_pool", tag="x10", align_bytes=64)
+        kb_pool = keep.tile([P, T], F32, name="kb_pool", align_bytes=64)
         nc.scalar.dma_start(kb_pool[P - 1 : P, :], kb[0:1, :])
         nc.vector.memset(kb_pool[0 : P - 1, :], 0.0)
         x_raw = {}
@@ -67,30 +67,50 @@ def tile_attend_gkl_w_kb_kernel(tc, xT, w_words, w_scales, y, wt, kb, xm, offs, 
             )
         word_pool = keep.tile([P, T], I32, name="word_pool", tag="y", align_bytes=64)
         nc.sync.dma_start(word_pool[:], w_words[0].rearrange("p n t -> p (n t)").bitcast(I32))
+        load_x(1, 0)
+        load_x(1, 1)
+        wt_sb = keep.tile([P, PACK], F32, name="wt_sb", align_bytes=64)
+        nc.sync.dma_start(wt_sb[:], wt[0].rearrange("(p t) one -> p (t one)", t=PACK))
         plane1 = keep.tile([P, N // 4], I32, name="plane1", align_bytes=64)
         nc.vector.memset(plane1[P - QUADRANT : P], 0)
-        windows = [keep.tile([P, T], F32, name="window0")]
-        nc.vector.memset(windows[0][:], 0.0)
 
-        kb_g = keep.tile([P, N], F32, name="kb_g", tag="x11", align_bytes=64)
+        kb_g = keep.tile([P, N], F32, name="kb_g", align_bytes=64)
         nc.vector.tensor_copy(kb_g[:], kb_pool[:].indirect(offsets[:]))
-        load_x(1, 0)
         acc = [psum.tile([P, N], F32, name=f"acc{k}") for k in range(4)]
         for c in range(N // P):
             nc.tensor.transpose(acc[0][:, c * P : (c + 1) * P], kb_g[:, c * P : (c + 1) * P], identity[:])
-        load_x(1, 1)
-        both = keep.tile([P, N], U8, name="both", align_bytes=64)
-        nc.vector.tensor_copy(both[:], scale_pool[:].bitcast(U8).indirect(offsets[:]))
-        nc.gpsimd.dma_start(plane1[0:SHIFT_ROWS, :], both[SCALE_ROWS : SCALE_ROWS + SHIFT_ROWS, :].bitcast(I32))
-        w_planes = [both[:], plane1[:].bitcast(U8)]
-        kb_col = keep.tile([P, N // P], F32, name="kb_col", tag="wt", align_bytes=64)
-        nc.vector.tensor_copy(kb_col[:], acc[0][:, P - 1 : N : P])
+
+        x_q = {}
+
+        def group_x(grouped, o, u, t0, count, copy):
+            width = P // X_LOADS[o]
+            dst = grouped.rearrange("p (t m j) -> p m t j", t=count, j=PACK)[:, u * width : (u + 1) * width]
+            src = x_raw[o, u][:].rearrange("p j (m t) -> p m t j", t=PACK)[:, :, t0 : t0 + count, :]
+            copy(dst, src)
+
+        def quantize_x(grouped, o, t0, count, tag=None):
+            codes = keep.tile([P, count * P], U32, name=f"x_codes{o}{t0}", tag=tag or f"x_codes{o}{t0}", align_bytes=64)
+            plane = keep.tile([P, count * P], U8, name=f"x_plane{o}{t0}", align_bytes=64)
+            nc.vector.quantize_mx(out=codes[:].bitcast(E4M3), scales=plane[:], in_=grouped)
+            for u in range(count):
+                x_q[o, t0 + u] = (codes[:, u * P : (u + 1) * P], plane[:, u * P : (u + 1) * P])
+
+        half = PACK // 2
+        grouped0 = keep.tile([P, PACK * K_PASS], BF16, name="x_grouped0", tag="x_grouped0", align_bytes=64)
+        group_x(grouped0[:, : half * K_PASS], 0, 0, 0, half, nc.scalar.copy)
+        group_x(grouped0[:, half * K_PASS :], 0, 0, half, half, nc.vector.tensor_copy)
+        kb_col = keep.tile([P, N // P], F32, name="kb_col", align_bytes=64)
+        nc.scalar.copy(kb_col[:], acc[0][:, P - 1 : N : P])
         for c in range(N // P):
             nc.tensor.transpose(acc[1][:, c * P : (c + 1) * P], kb_col[:, c : c + 1].to_broadcast([P, P]), identity[:])
         kb_all = keep.tile([P, N], F32, name="kb_all")
-        nc.vector.tensor_copy(kb_all[:], acc[1][:])
-        wt_sb = keep.tile([P, PACK], F32, name="wt_sb", tag="wt", align_bytes=64)
-        nc.sync.dma_start(wt_sb[:], wt[0].rearrange("(p t) one -> p (t one)", t=PACK))
+        nc.scalar.copy(kb_all[:], acc[1][:])
+
+        both = keep.tile([P, N], U8, name="both", align_bytes=64)
+        nc.vector.tensor_copy(both[:], scale_pool[:].bitcast(U8).indirect(offsets[:]))
+        nc.sync.dma_start(plane1[0:SHIFT_ROWS, :], both[SCALE_ROWS : SCALE_ROWS + SHIFT_ROWS, :].bitcast(I32))
+        w_planes = [both[:], plane1[:].bitcast(U8)]
+        quantize_x(grouped0[:, : half * K_PASS], 0, 0, half)
 
         pairs = keep.tile([P, N], U32, name="pairs", align_bytes=64)
         nc.vector.tensor_copy(pairs[:], word_pool[:].bitcast(U32).indirect(offsets[:]))
@@ -102,38 +122,24 @@ def tile_attend_gkl_w_kb_kernel(tc, xT, w_words, w_scales, y, wt, kb, xm, offs, 
             pairs[:].bitcast(U16).rearrange("p (n o) -> p o n", o=PASSES),
         )
 
-        x_q = {}
-
-        def group_x(grouped, o, u, t0, count, copy):
-            width = P // X_LOADS[o]
-            dst = grouped[:].rearrange("p (t m j) -> p m t j", t=count, j=PACK)[:, u * width : (u + 1) * width]
-            src = x_raw[o, u][:].rearrange("p j (m t) -> p m t j", t=PACK)[:, :, t0 : t0 + count, :]
-            copy(dst, src)
-
-        def quantize_x(grouped, o, t0, count):
-            codes = keep.tile([P, count * P], U32, name=f"x_codes{o}{t0}", tag=f"x_codes{o}{t0}", align_bytes=64)
-            plane = keep.tile([P, count * P], U8, name=f"x_plane{o}{t0}", align_bytes=64)
-            nc.vector.quantize_mx(out=codes[:].bitcast(E4M3), scales=plane[:], in_=grouped[:])
-            for u in range(count):
-                x_q[o, t0 + u] = (codes[:, u * P : (u + 1) * P], plane[:, u * P : (u + 1) * P])
-
-        grouped0 = keep.tile([P, PACK * P * PACK], BF16, name="x_grouped0", align_bytes=64)
-        group_x(grouped0, 0, 0, 0, PACK, nc.scalar.copy)
-        quantize_x(grouped0, 0, 0, PACK)
-        half = PACK // 2
-        grouped1 = [keep.tile([P, half * P * PACK], BF16, name=f"x_grouped1{h}", align_bytes=64) for h in range(2)]
+        grouped1 = [
+            keep.tile([P, half * P * PACK], BF16, name=f"x_grouped1{t0}", tag=f"x_grouped1{t0}", align_bytes=64)
+            for t0 in (0, half)
+        ]
         for h in range(2):
-            group_x(grouped1[h], 1, 0, h * half, half, nc.scalar.copy)
+            group_x(grouped1[h][:], 1, 0, h * half, half, nc.scalar.copy)
+        group_x(grouped1[0][:], 1, 1, 0, half, nc.vector.tensor_copy)
+        group_x(grouped1[1][:], 1, 1, half, half, nc.scalar.copy)
         xm_w = D // XM_LOADS
         xm_raw = []
-        for h, tag in enumerate(("x00", "x10")):
+        for h, tag in enumerate(("x10", "x11")):
             raw = keep.tile([P, PACK, xm_w], F32, name=f"xm_raw{h}", tag=tag, align_bytes=64)
             nc.sync.dma_start(raw[:], xm[0, :, h * xm_w : (h + 1) * xm_w].rearrange("(p t) d -> p t d", t=PACK))
             xm_raw.append(raw)
-        group_x(grouped1[0], 1, 1, 0, half, nc.vector.tensor_copy)
-        group_x(grouped1[1], 1, 1, half, half, nc.scalar.copy)
-        for h in range(2):
-            quantize_x(grouped1[h], 1, h * half, half)
+        for t in range(half):
+            quantize_x(grouped1[0][:, t * K_PASS : (t + 1) * K_PASS], 1, t, 1)
+        quantize_x(grouped1[1][:], 1, half, half)
+        quantize_x(grouped0[:, half * K_PASS :], 0, half, half, tag="x_grouped10")
 
         scores = [psum.tile([P, N], F32, name=f"scores{t}") for t in range(PACK)]
         for t in range(PACK):
@@ -149,9 +155,11 @@ def tile_attend_gkl_w_kb_kernel(tc, xT, w_words, w_scales, y, wt, kb, xm, offs, 
                     stop=(o == PASSES - 1),
                 )
 
-        second_window = keep.tile([P, T], F32, name="window1", tag="w_codes", align_bytes=64)
-        nc.gpsimd.memset(second_window[:], 0.0)
-        windows.append(second_window)
+        windows = []
+        for k, tag in enumerate(("x_grouped0", "w_codes", "x_codes12")):
+            win = keep.tile([P, T], F32, name=f"window{k}", tag=tag, align_bytes=64)
+            nc.gpsimd.memset(win[:], 0.0)
+            windows.append(win)
 
         neg_z = [keep.tile([P, N], F32, name=f"neg_z{t}", tag=f"neg_z{t}", align_bytes=64) for t in range(PACK)]
         neg_m = [keep.tile([P, 1], F32, name=f"neg_m{t}", tag=f"neg_m{t}", align_bytes=64) for t in range(PACK)]
@@ -224,9 +232,6 @@ def tile_attend_gkl_w_kb_kernel(tc, xT, w_words, w_scales, y, wt, kb, xm, offs, 
         g_codes = keep.tile([P, N], U32, name="g_codes", align_bytes=64)
         g_plane = keep.tile([P, N], U8, name="g_plane", align_bytes=64)
         nc.vector.quantize_mx(out=g_codes[:].bitcast(E5M2), scales=g_plane[:], in_=g_grouped[:])
-        last_window = keep.tile([P, T], F32, name="window2", tag="g_grouped", align_bytes=64)
-        nc.vector.memset(last_window[:], 0.0)
-        windows.append(last_window)
         quantize_xm(2, 2, "g_rows", "e2")
 
         def output_block(b):
@@ -242,9 +247,13 @@ def tile_attend_gkl_w_kb_kernel(tc, xT, w_words, w_scales, y, wt, kb, xm, offs, 
                 stop=True,
             )
             dense = ring.tile([P, N], F32, name="dense")
-            nc.scalar.copy(dense[:], bank[:])
             window = windows[b % WINDOWS]
-            nc.vector.tensor_copy(window[:].indirect(offsets[:]), dense[:])
+            pieces = 2 if b == 0 else 1
+            for u in range(pieces):
+                cols = slice(u * N // pieces, (u + 1) * N // pieces)
+                entries = slice(cols.start // 16, cols.stop // 16)
+                nc.scalar.copy(dense[:, cols], bank[:, cols])
+                nc.vector.tensor_copy(window[:].indirect(offsets[:, entries]), dense[:, cols])
             nc.sync.dma_start(out[b * P : (b + 1) * P, :], window[:])
 
         output_block(0)

@@ -24,11 +24,11 @@ PASSES = D // K_PASS
 QUADRANT = 32
 SCALE_ROWS = 4
 SHIFT_ROWS = 112
-WINDOWS = 3
+WINDOWS = 4
 X_LOADS = (1, 2)
 XM_LOADS = 2
 RUN = 4
-G_SPLIT = 88
+G_SPLIT = 288
 
 FLOPS = 2 * 2 * R * D * N
 
@@ -43,7 +43,7 @@ def tile_attend_gkl_w_kb_kernel(tc, xT, w_words, w_scales, y, wt, kb, xm, offs, 
         offsets = keep.tile([P, N // 16], U16, name="offsets")
         nc.sync.dma_start(offsets[:], offs)
 
-        scale_pool = keep.tile([P, T // 4], I32, name="scale_pool", align_bytes=64)
+        scale_pool = keep.tile([P, T // 4], I32, name="scale_pool", tag="y", align_bytes=64)
         nc.gpsimd.memset(scale_pool[:], 0)
         identity = keep.tile([P, P], F32, name="identity")
         make_identity(nc, identity[:])
@@ -65,7 +65,7 @@ def tile_attend_gkl_w_kb_kernel(tc, xT, w_words, w_scales, y, wt, kb, xm, offs, 
                 scale_pool[QUADRANT * q : QUADRANT * q + PASSES * SCALE_ROWS, :],
                 w_scales.bitcast(I32)[:, SCALE_ROWS * q : SCALE_ROWS * (q + 1), :],
             )
-        word_pool = keep.tile([P, T], I32, name="word_pool", tag="y", align_bytes=64)
+        word_pool = keep.tile([P, T], I32, name="word_pool", tag="xm0", align_bytes=64)
         nc.sync.dma_start(word_pool[:], w_words[0].rearrange("p n t -> p (n t)").bitcast(I32))
         load_x(1, 0)
         load_x(1, 1)
@@ -73,6 +73,9 @@ def tile_attend_gkl_w_kb_kernel(tc, xT, w_words, w_scales, y, wt, kb, xm, offs, 
         nc.sync.dma_start(wt_sb[:], wt[0].rearrange("(p t) one -> p (t one)", t=PACK))
         plane1 = keep.tile([P, N // 4], I32, name="plane1", align_bytes=64)
         nc.vector.memset(plane1[P - QUADRANT : P], 0)
+
+        windows = [keep.tile([P, T], F32, name="window0")]
+        nc.vector.memset(windows[0][:], 0.0)
 
         kb_g = keep.tile([P, N], F32, name="kb_g", align_bytes=64)
         nc.vector.tensor_copy(kb_g[:], kb_pool[:].indirect(offsets[:]))
@@ -110,12 +113,12 @@ def tile_attend_gkl_w_kb_kernel(tc, xT, w_words, w_scales, y, wt, kb, xm, offs, 
         nc.vector.tensor_copy(both[:], scale_pool[:].bitcast(U8).indirect(offsets[:]))
         nc.sync.dma_start(plane1[0:SHIFT_ROWS, :], both[SCALE_ROWS : SCALE_ROWS + SHIFT_ROWS, :].bitcast(I32))
         w_planes = [both[:], plane1[:].bitcast(U8)]
+        y_sb = keep.tile([P, PACK, N], F32, name="y_sb", tag="y", align_bytes=64)
+        nc.sync.dma_start(y_sb[:], y[0].rearrange("(p t) i -> p t i", t=PACK))
         quantize_x(grouped0[:, : half * K_PASS], 0, 0, half)
 
         pairs = keep.tile([P, N], U32, name="pairs", align_bytes=64)
         nc.vector.tensor_copy(pairs[:], word_pool[:].bitcast(U32).indirect(offsets[:]))
-        y_sb = keep.tile([P, PACK, N], F32, name="y_sb", tag="y", align_bytes=64)
-        nc.sync.dma_start(y_sb[:], y[0].rearrange("(p t) i -> p t i", t=PACK))
         w_codes = keep.tile([P, PASSES * 2 * N], U8, name="w_codes", tag="w_codes", align_bytes=64)
         nc.vector.tensor_copy(
             w_codes[:].bitcast(U16).rearrange("p (o n) -> p o n", o=PASSES),
@@ -132,7 +135,7 @@ def tile_attend_gkl_w_kb_kernel(tc, xT, w_words, w_scales, y, wt, kb, xm, offs, 
         group_x(grouped1[1][:], 1, 1, half, half, nc.scalar.copy)
         xm_w = D // XM_LOADS
         xm_raw = []
-        for h, tag in enumerate(("x10", "x11")):
+        for h, tag in enumerate(("xm0", "x10")):
             raw = keep.tile([P, PACK, xm_w], F32, name=f"xm_raw{h}", tag=tag, align_bytes=64)
             nc.sync.dma_start(raw[:], xm[0, :, h * xm_w : (h + 1) * xm_w].rearrange("(p t) d -> p t d", t=PACK))
             xm_raw.append(raw)
@@ -155,16 +158,10 @@ def tile_attend_gkl_w_kb_kernel(tc, xT, w_words, w_scales, y, wt, kb, xm, offs, 
                     stop=(o == PASSES - 1),
                 )
 
-        windows = []
-        for k, tag in enumerate(("x_grouped0", "w_codes", "x_codes12")):
-            win = keep.tile([P, T], F32, name=f"window{k}", tag=tag, align_bytes=64)
-            nc.gpsimd.memset(win[:], 0.0)
-            windows.append(win)
-
         neg_z = [keep.tile([P, N], F32, name=f"neg_z{t}", tag=f"neg_z{t}", align_bytes=64) for t in range(PACK)]
         neg_m = [keep.tile([P, 1], F32, name=f"neg_m{t}", tag=f"neg_m{t}", align_bytes=64) for t in range(PACK)]
         e = [keep.tile([P, N], F32, name=f"e{t}", tag=f"e{t}", align_bytes=64) for t in range(PACK)]
-        wy = [keep.tile([P, N], F32, name=f"wy{t}", tag=f"wy{t}", align_bytes=64) for t in range(PACK)]
+        wy = keep.tile([P, PACK, N], F32, name="wy", tag="x_grouped0", align_bytes=64)
         sums = [keep.tile([P, 1], F32, name=f"sums{t}") for t in range(PACK)]
         inv = [keep.tile([P, 1], F32, name=f"inv{t}") for t in range(PACK)]
         coef = [keep.tile([P, 1], F32, name=f"coef{t}") for t in range(PACK)]
@@ -184,25 +181,26 @@ def tile_attend_gkl_w_kb_kernel(tc, xT, w_words, w_scales, y, wt, kb, xm, offs, 
             nc.vector.reciprocal(inv[t][:], sums[t][:])
 
         def weigh(t):
-            nc.vector.tensor_tensor(coef[t][:], inv[t][:], wt_sb[:, t : t + 1], ALU.mult)
+            nc.vector.tensor_scalar(coef[t][:], inv[t][:], wt_sb[:, t : t + 1], None, ALU.mult)
 
-        def gradient(t):
+        def gradient(t, cols=slice(0, N)):
             nc.vector.scalar_tensor_tensor(
-                g_rows[:, t, :], e[t][:], coef[t][:], wy[t][:], ALU.mult, ALU.subtract
+                g_rows[:, t, cols], e[t][:, cols], coef[t][:], wy[:, t, cols], ALU.mult, ALU.subtract
             )
 
         xm_q = []
 
-        def quantize_xm(first, count, grouped_tag, codes_tag):
+        def quantize_xm(first, copies, grouped_tag, codes_tag):
+            count = len(copies)
             grouped = keep.tile([P, count * P * PACK], BF16, name=f"xm_grouped{first}", tag=grouped_tag, align_bytes=64)
-            for u in range(count):
+            for u, copy in enumerate(copies):
                 h, d0 = divmod((first + u) * P, xm_w)
-                nc.scalar.copy(
+                copy(
                     grouped[:, u * P * PACK : (u + 1) * P * PACK].rearrange("p (d t) -> p d t", t=PACK),
                     xm_raw[h][:, :, d0 : d0 + P].rearrange("p t d -> p d t"),
                 )
             codes = keep.tile([P, count * P], U32, name=f"xm_codes{first}", tag=codes_tag, align_bytes=64)
-            plane = keep.tile([P, count * P], U8, name=f"xm_plane{first}", align_bytes=64)
+            plane = keep.tile([P, count * P], U8, name=f"xm_plane{first}", tag=f"xm_plane{first}", align_bytes=64)
             nc.vector.quantize_mx(out=codes[:].bitcast(E4M3), scales=plane[:], in_=grouped[:])
             for u in range(count):
                 xm_q.append((codes[:, u * P : (u + 1) * P], plane[:, u * P : (u + 1) * P]))
@@ -214,31 +212,41 @@ def tile_attend_gkl_w_kb_kernel(tc, xT, w_words, w_scales, y, wt, kb, xm, offs, 
         invert(0)
         exp_row(PACK - 1)
         for t in range(PACK):
-            nc.scalar.activation(wy[t][:], y_sb[:, t, :], ACT.Copy, scale=wt_sb[:, t : t + 1])
-        for t in range(PACK - 1):
+            nc.gpsimd.tensor_scalar(wy[:, t, :], y_sb[:, t, :], wt_sb[:, t : t + 1], 0.0, ALU.mult, ALU.add)
+        low, high = slice(0, G_SPLIT), slice(G_SPLIT, N)
+        weigh(0)
+        invert(1)
+        gradient(0)
+        for t in range(1, PACK):
             weigh(t)
-            invert(t + 1)
-            gradient(t)
-        weigh(PACK - 1)
-        gradient(PACK - 1)
+            if t + 1 < PACK:
+                invert(t + 1)
+            gradient(t, low)
+        for t in range(1, PACK):
+            gradient(t, high)
 
         g_grouped = keep.tile([P, N * PACK], BF16, name="g_grouped", tag="g_grouped", align_bytes=64)
         g_dst = g_grouped[:].rearrange("p (c i t) -> p c t i", i=RUN, t=PACK)
         g_src = g_rows[:].rearrange("p t (c i) -> p c t i", i=RUN)
-        nc.vector.tensor_copy(g_dst[:, :G_SPLIT], g_src[:, :G_SPLIT])
-        nc.scalar.copy(g_dst[:, G_SPLIT:], g_src[:, G_SPLIT:])
+        nc.scalar.copy(g_dst[:, : G_SPLIT // RUN], g_src[:, : G_SPLIT // RUN])
+        nc.vector.tensor_copy(g_dst[:, G_SPLIT // RUN :], g_src[:, G_SPLIT // RUN :])
 
-        quantize_xm(0, 2, "neg_z3", "e3")
+        on_scalar, on_vector = nc.scalar.copy, nc.vector.tensor_copy
+        quantize_xm(0, [on_scalar] * 2, "neg_z1", "e3")
         g_codes = keep.tile([P, N], U32, name="g_codes", align_bytes=64)
         g_plane = keep.tile([P, N], U8, name="g_plane", align_bytes=64)
         nc.vector.quantize_mx(out=g_codes[:].bitcast(E5M2), scales=g_plane[:], in_=g_grouped[:])
-        quantize_xm(2, 2, "g_rows", "e2")
+        quantize_xm(2, [on_scalar] * 2 + [on_vector] * 2, "g_rows", "e2")
 
-        def output_block(b):
+        def zero_window(k, tag):
+            win = keep.tile([P, T], F32, name=f"window{k}", tag=tag, align_bytes=64)
+            nc.gpsimd.memset(win[:], 0.0)
+            windows.append(win)
+
+        def multiply(b):
             codes, plane = xm_q[b]
-            bank = acc[b % len(acc)]
             nc.tensor.matmul_mx(
-                out=bank[:],
+                out=acc[b % len(acc)][:],
                 lhsT=codes.bitcast(E4M3),
                 lhsT_scale=plane,
                 rhs=g_codes[:].bitcast(E5M2),
@@ -246,7 +254,9 @@ def tile_attend_gkl_w_kb_kernel(tc, xT, w_words, w_scales, y, wt, kb, xm, offs, 
                 start=True,
                 stop=True,
             )
-            dense = ring.tile([P, N], F32, name="dense")
+
+        def place(b, dense):
+            bank = acc[b % len(acc)]
             window = windows[b % WINDOWS]
             pieces = 2 if b == 0 else 1
             for u in range(pieces):
@@ -256,8 +266,17 @@ def tile_attend_gkl_w_kb_kernel(tc, xT, w_words, w_scales, y, wt, kb, xm, offs, 
                 nc.vector.tensor_copy(window[:].indirect(offsets[:, entries]), dense[:, cols])
             nc.sync.dma_start(out[b * P : (b + 1) * P, :], window[:])
 
-        output_block(0)
-        output_block(1)
-        quantize_xm(4, 4, "e3", "e1")
-        for b in range(2, D // P):
-            output_block(b)
+        zero_window(1, "g_rows")
+        for b in range(len(acc)):
+            multiply(b)
+        for b in range(2):
+            place(b, ring.tile([P, N], F32, name="dense"))
+            multiply(b + len(acc))
+        zero_window(2, "e2")
+        zero_window(3, "xm_plane2")
+        place(2, keep.tile([P, N], F32, name="dense2", tag="dense2", align_bytes=64))
+        quantize_xm(6, [on_scalar] * 2, "e3", "dense2")
+        for b in range(3, D // P):
+            if b >= 6:
+                multiply(b)
+            place(b, ring.tile([P, N], F32, name="dense"))

@@ -26,7 +26,6 @@ SCALE_ROWS = 4
 SHIFT_ROWS = 112
 WINDOWS = 4
 X_LOADS = (1, 2)
-XM_LOADS = 2
 RUN = 4
 G_SPLIT = 288
 
@@ -74,9 +73,6 @@ def tile_attend_gkl_w_kb_kernel(tc, xT, w_words, w_scales, y, wt, kb, xm, offs, 
         plane1 = keep.tile([P, N // 4], I32, name="plane1", align_bytes=64)
         nc.vector.memset(plane1[P - QUADRANT : P], 0)
 
-        windows = [keep.tile([P, T], F32, name="window0")]
-        nc.vector.memset(windows[0][:], 0.0)
-
         kb_g = keep.tile([P, N], F32, name="kb_g", align_bytes=64)
         nc.vector.tensor_copy(kb_g[:], kb_pool[:].indirect(offsets[:]))
         acc = [psum.tile([P, N], F32, name=f"acc{k}") for k in range(4)]
@@ -85,10 +81,9 @@ def tile_attend_gkl_w_kb_kernel(tc, xT, w_words, w_scales, y, wt, kb, xm, offs, 
 
         x_q = {}
 
-        def group_x(grouped, o, u, t0, count, copy):
-            width = P // X_LOADS[o]
-            dst = grouped.rearrange("p (t m j) -> p m t j", t=count, j=PACK)[:, u * width : (u + 1) * width]
-            src = x_raw[o, u][:].rearrange("p j (m t) -> p m t j", t=PACK)[:, :, t0 : t0 + count, :]
+        def group_x(grouped, raw, m0, count, first, copy):
+            dst = grouped[:].rearrange("p (t m j) -> p m t j", t=PACK, j=PACK)[:, first : first + count]
+            src = raw[:].rearrange("p j (m t) -> p m t j", t=PACK)[:, m0 : m0 + count]
             copy(dst, src)
 
         def quantize_x(grouped, o, t0, count, tag=None):
@@ -100,8 +95,8 @@ def tile_attend_gkl_w_kb_kernel(tc, xT, w_words, w_scales, y, wt, kb, xm, offs, 
 
         half = PACK // 2
         grouped0 = keep.tile([P, PACK * K_PASS], BF16, name="x_grouped0", tag="x_grouped0", align_bytes=64)
-        group_x(grouped0[:, : half * K_PASS], 0, 0, 0, half, nc.scalar.copy)
-        group_x(grouped0[:, half * K_PASS :], 0, 0, half, half, nc.vector.tensor_copy)
+        group_x(grouped0, x_raw[0, 0], 0, P // 2, 0, nc.scalar.copy)
+        group_x(grouped0, x_raw[0, 0], P // 2, P // 2, P // 2, nc.vector.tensor_copy)
         kb_col = keep.tile([P, N // P], F32, name="kb_col", align_bytes=64)
         nc.scalar.copy(kb_col[:], acc[0][:, P - 1 : N : P])
         for c in range(N // P):
@@ -113,36 +108,42 @@ def tile_attend_gkl_w_kb_kernel(tc, xT, w_words, w_scales, y, wt, kb, xm, offs, 
         nc.vector.tensor_copy(both[:], scale_pool[:].bitcast(U8).indirect(offsets[:]))
         nc.sync.dma_start(plane1[0:SHIFT_ROWS, :], both[SCALE_ROWS : SCALE_ROWS + SHIFT_ROWS, :].bitcast(I32))
         w_planes = [both[:], plane1[:].bitcast(U8)]
-        y_sb = keep.tile([P, PACK, N], F32, name="y_sb", tag="y", align_bytes=64)
-        nc.sync.dma_start(y_sb[:], y[0].rearrange("(p t) i -> p t i", t=PACK))
+        y_sb = []
+
+        def load_y(h, tag):
+            raw = keep.tile([P, half, N], F32, name=f"y_sb{h}", tag=tag, align_bytes=64)
+            nc.sync.dma_start(raw[:], y[0].rearrange("(p t) i -> p t i", t=PACK)[:, h * half : (h + 1) * half])
+            y_sb.extend(raw[:, u, :] for u in range(half))
+
+        xm_raw = []
+
+        def load_xm(blocks, tag):
+            d0 = len(xm_raw) * P
+            raw = keep.tile([P, PACK, blocks * P], F32, name=f"xm_raw{d0}", tag=tag, align_bytes=64)
+            nc.sync.dma_start(raw[:], xm[0, :, d0 : d0 + blocks * P].rearrange("(p t) d -> p t d", t=PACK))
+            xm_raw.extend(raw[:, :, u * P : (u + 1) * P] for u in range(blocks))
+
+        load_y(0, "y")
         quantize_x(grouped0[:, : half * K_PASS], 0, 0, half)
 
-        pairs = keep.tile([P, N], U32, name="pairs", align_bytes=64)
+        pairs = keep.tile([P, N], U32, name="pairs", tag="pairs", align_bytes=64)
         nc.vector.tensor_copy(pairs[:], word_pool[:].bitcast(U32).indirect(offsets[:]))
+        load_xm(2, "xm0")
         w_codes = keep.tile([P, PASSES * 2 * N], U8, name="w_codes", tag="w_codes", align_bytes=64)
         nc.vector.tensor_copy(
             w_codes[:].bitcast(U16).rearrange("p (o n) -> p o n", o=PASSES),
             pairs[:].bitcast(U16).rearrange("p (n o) -> p o n", o=PASSES),
         )
 
-        grouped1 = [
-            keep.tile([P, half * P * PACK], BF16, name=f"x_grouped1{t0}", tag=f"x_grouped1{t0}", align_bytes=64)
-            for t0 in (0, half)
-        ]
-        for h in range(2):
-            group_x(grouped1[h][:], 1, 0, h * half, half, nc.scalar.copy)
-        group_x(grouped1[0][:], 1, 1, 0, half, nc.vector.tensor_copy)
-        group_x(grouped1[1][:], 1, 1, half, half, nc.scalar.copy)
-        xm_w = D // XM_LOADS
-        xm_raw = []
-        for h, tag in enumerate(("xm0", "x10")):
-            raw = keep.tile([P, PACK, xm_w], F32, name=f"xm_raw{h}", tag=tag, align_bytes=64)
-            nc.sync.dma_start(raw[:], xm[0, :, h * xm_w : (h + 1) * xm_w].rearrange("(p t) d -> p t d", t=PACK))
-            xm_raw.append(raw)
+        load_y(1, "pairs")
+        grouped1 = keep.tile([P, PACK * K_PASS], BF16, name="x_grouped1", align_bytes=64)
+        group_x(grouped1, x_raw[1, 0], 0, P // 2, 0, nc.scalar.copy)
+        load_xm(4, "x10")
+        group_x(grouped1, x_raw[1, 1], 0, P // 2, P // 2, nc.vector.tensor_copy)
         for t in range(half):
-            quantize_x(grouped1[0][:, t * K_PASS : (t + 1) * K_PASS], 1, t, 1)
-        quantize_x(grouped1[1][:], 1, half, half)
-        quantize_x(grouped0[:, half * K_PASS :], 0, half, half, tag="x_grouped10")
+            quantize_x(grouped1[:, t * K_PASS : (t + 1) * K_PASS], 1, t, 1)
+        quantize_x(grouped1[:, half * K_PASS :], 1, half, half)
+        quantize_x(grouped0[:, half * K_PASS :], 0, half, half, tag="x11")
 
         scores = [psum.tile([P, N], F32, name=f"scores{t}") for t in range(PACK)]
         for t in range(PACK):
@@ -158,10 +159,14 @@ def tile_attend_gkl_w_kb_kernel(tc, xT, w_words, w_scales, y, wt, kb, xm, offs, 
                     stop=(o == PASSES - 1),
                 )
 
+        load_xm(2, "w_codes")
+        windows = [keep.tile([P, T], F32, name="window0", tag="x_grouped0", align_bytes=64)]
+        nc.gpsimd.memset(windows[0][:], 0.0)
+
         neg_z = [keep.tile([P, N], F32, name=f"neg_z{t}", tag=f"neg_z{t}", align_bytes=64) for t in range(PACK)]
         neg_m = [keep.tile([P, 1], F32, name=f"neg_m{t}", tag=f"neg_m{t}", align_bytes=64) for t in range(PACK)]
         e = [keep.tile([P, N], F32, name=f"e{t}", tag=f"e{t}", align_bytes=64) for t in range(PACK)]
-        wy = keep.tile([P, PACK, N], F32, name="wy", tag="x_grouped0", align_bytes=64)
+        wy = keep.tile([P, PACK, N], F32, name="wy", align_bytes=64)
         sums = [keep.tile([P, 1], F32, name=f"sums{t}") for t in range(PACK)]
         inv = [keep.tile([P, 1], F32, name=f"inv{t}") for t in range(PACK)]
         coef = [keep.tile([P, 1], F32, name=f"coef{t}") for t in range(PACK)]
@@ -194,10 +199,9 @@ def tile_attend_gkl_w_kb_kernel(tc, xT, w_words, w_scales, y, wt, kb, xm, offs, 
             count = len(copies)
             grouped = keep.tile([P, count * P * PACK], BF16, name=f"xm_grouped{first}", tag=grouped_tag, align_bytes=64)
             for u, copy in enumerate(copies):
-                h, d0 = divmod((first + u) * P, xm_w)
                 copy(
                     grouped[:, u * P * PACK : (u + 1) * P * PACK].rearrange("p (d t) -> p d t", t=PACK),
-                    xm_raw[h][:, :, d0 : d0 + P].rearrange("p t d -> p d t"),
+                    xm_raw[first + u].rearrange("p t d -> p d t"),
                 )
             codes = keep.tile([P, count * P], U32, name=f"xm_codes{first}", tag=codes_tag, align_bytes=64)
             plane = keep.tile([P, count * P], U8, name=f"xm_plane{first}", tag=f"xm_plane{first}", align_bytes=64)
@@ -211,19 +215,17 @@ def tile_attend_gkl_w_kb_kernel(tc, xT, w_words, w_scales, y, wt, kb, xm, offs, 
             exp_row(t)
         invert(0)
         exp_row(PACK - 1)
-        for t in range(PACK):
-            nc.gpsimd.tensor_scalar(wy[:, t, :], y_sb[:, t, :], wt_sb[:, t : t + 1], 0.0, ALU.mult, ALU.add)
-        low, high = slice(0, G_SPLIT), slice(G_SPLIT, N)
-        weigh(0)
-        invert(1)
-        gradient(0)
-        for t in range(1, PACK):
+        for t in range(half):
+            nc.scalar.activation(wy[:, t, :], y_sb[t], ACT.Copy, scale=wt_sb[:, t : t + 1])
+        for t in range(half, PACK):
+            nc.gpsimd.tensor_scalar(wy[:, t, :], y_sb[t], wt_sb[:, t : t + 1], 0.0, ALU.mult, ALU.add)
+        for t in range(PACK - 1):
             weigh(t)
-            if t + 1 < PACK:
-                invert(t + 1)
-            gradient(t, low)
-        for t in range(1, PACK):
-            gradient(t, high)
+            invert(t + 1)
+            gradient(t)
+        weigh(PACK - 1)
+        gradient(PACK - 1, slice(0, G_SPLIT))
+        gradient(PACK - 1, slice(G_SPLIT, N))
 
         g_grouped = keep.tile([P, N * PACK], BF16, name="g_grouped", tag="g_grouped", align_bytes=64)
         g_dst = g_grouped[:].rearrange("p (c i t) -> p c t i", i=RUN, t=PACK)
@@ -232,7 +234,7 @@ def tile_attend_gkl_w_kb_kernel(tc, xT, w_words, w_scales, y, wt, kb, xm, offs, 
         nc.vector.tensor_copy(g_dst[:, G_SPLIT // RUN :], g_src[:, G_SPLIT // RUN :])
 
         on_scalar, on_vector = nc.scalar.copy, nc.vector.tensor_copy
-        quantize_xm(0, [on_scalar] * 2, "neg_z1", "e3")
+        quantize_xm(0, [on_scalar] * 2, "xm_grouped0", "e3")
         g_codes = keep.tile([P, N], U32, name="g_codes", align_bytes=64)
         g_plane = keep.tile([P, N], U8, name="g_plane", align_bytes=64)
         nc.vector.quantize_mx(out=g_codes[:].bitcast(E5M2), scales=g_plane[:], in_=g_grouped[:])

@@ -26,8 +26,9 @@ SCALE_ROWS = 4
 SHIFT_ROWS = 112
 WINDOWS = 4
 X_LOADS = (1, 2)
+X_ON_SCALAR = (40, 20)
 RUN = 4
-G_SPLIT = 288
+G_SPLIT = 240
 
 FLOPS = 2 * 2 * R * D * N
 
@@ -59,7 +60,7 @@ def tile_attend_gkl_w_kb_kernel(tc, xT, w_words, w_scales, y, wt, kb, xm, offs, 
             x_raw[o, u] = raw
 
         load_x(0, 0)
-        for q in range(P // QUADRANT):
+        for q in (0, 2, 1, 3):
             nc.sync.dma_start(
                 scale_pool[QUADRANT * q : QUADRANT * q + PASSES * SCALE_ROWS, :],
                 w_scales.bitcast(I32)[:, SCALE_ROWS * q : SCALE_ROWS * (q + 1), :],
@@ -130,16 +131,16 @@ def tile_attend_gkl_w_kb_kernel(tc, xT, w_words, w_scales, y, wt, kb, xm, offs, 
         nc.vector.tensor_copy(pairs[:], word_pool[:].bitcast(U32).indirect(offsets[:]))
         load_xm(2, "xm0")
         w_codes = keep.tile([P, PASSES * 2 * N], U8, name="w_codes", tag="w_codes", align_bytes=64)
-        nc.vector.tensor_copy(
-            w_codes[:].bitcast(U16).rearrange("p (o n) -> p o n", o=PASSES),
-            pairs[:].bitcast(U16).rearrange("p (n o) -> p o n", o=PASSES),
-        )
+        for o in range(PASSES):
+            nc.vector.tensor_copy(w_codes[:].bitcast(U16)[:, o * N : (o + 1) * N], pairs[:].bitcast(U16)[:, o::PASSES])
 
         load_y(1, "pairs")
         grouped1 = keep.tile([P, PACK * K_PASS], BF16, name="x_grouped1", align_bytes=64)
-        group_x(grouped1, x_raw[1, 0], 0, P // 2, 0, nc.scalar.copy)
+        for u, on_scalar in enumerate(X_ON_SCALAR):
+            first = u * P // 2
+            group_x(grouped1, x_raw[1, u], 0, on_scalar, first, nc.scalar.copy)
+            group_x(grouped1, x_raw[1, u], on_scalar, P // 2 - on_scalar, first + on_scalar, nc.vector.tensor_copy)
         load_xm(4, "x10")
-        group_x(grouped1, x_raw[1, 1], 0, P // 2, P // 2, nc.vector.tensor_copy)
         for t in range(half):
             quantize_x(grouped1[:, t * K_PASS : (t + 1) * K_PASS], 1, t, 1)
         quantize_x(grouped1[:, half * K_PASS :], 1, half, half)
@@ -238,7 +239,9 @@ def tile_attend_gkl_w_kb_kernel(tc, xT, w_words, w_scales, y, wt, kb, xm, offs, 
         g_codes = keep.tile([P, N], U32, name="g_codes", align_bytes=64)
         g_plane = keep.tile([P, N], U8, name="g_plane", align_bytes=64)
         nc.vector.quantize_mx(out=g_codes[:].bitcast(E5M2), scales=g_plane[:], in_=g_grouped[:])
-        quantize_xm(2, [on_scalar] * 2 + [on_vector] * 2, "g_rows", "e2")
+        quantize_xm(2, [on_scalar] * 2, "neg_z3", "g_grouped")
+        quantize_xm(4, [on_scalar] * 2, "g_rows", "e2")
+        quantize_xm(6, [on_vector] * 2, "neg_z2", "e1")
 
         def zero_window(k, tag):
             win = keep.tile([P, T], F32, name=f"window{k}", tag=tag, align_bytes=64)
@@ -257,8 +260,9 @@ def tile_attend_gkl_w_kb_kernel(tc, xT, w_words, w_scales, y, wt, kb, xm, offs, 
                 stop=True,
             )
 
-        def place(b, dense):
+        def place(b):
             bank = acc[b % len(acc)]
+            dense = ring.tile([P, N], F32, name="dense")
             window = windows[b % WINDOWS]
             pieces = 2 if b == 0 else 1
             for u in range(pieces):
@@ -272,13 +276,11 @@ def tile_attend_gkl_w_kb_kernel(tc, xT, w_words, w_scales, y, wt, kb, xm, offs, 
         for b in range(len(acc)):
             multiply(b)
         for b in range(2):
-            place(b, ring.tile([P, N], F32, name="dense"))
+            place(b)
             multiply(b + len(acc))
         zero_window(2, "e2")
-        zero_window(3, "xm_plane2")
-        place(2, keep.tile([P, N], F32, name="dense2", tag="dense2", align_bytes=64))
-        quantize_xm(6, [on_scalar] * 2, "e3", "dense2")
-        for b in range(3, D // P):
-            if b >= 6:
-                multiply(b)
-            place(b, ring.tile([P, N], F32, name="dense"))
+        zero_window(3, "xm_plane4")
+        for b in range(2, D // P):
+            place(b)
+            if b + len(acc) < D // P:
+                multiply(b + len(acc))

@@ -30,6 +30,8 @@ X_ON_SCALAR = (40, 20)
 RUN = 4
 G_SPLIT = 240
 
+FIRST_LATE = 2
+
 FLOPS = 2 * 2 * R * D * N
 
 
@@ -47,6 +49,9 @@ def tile_attend_gkl_w_kb_kernel(tc, xT, w_words, w_scales, y, wt, kb, xm, offs, 
         nc.gpsimd.memset(scale_pool[:], 0)
         identity = keep.tile([P, P], F32, name="identity")
         make_identity(nc, identity[:])
+        windows = [keep.tile([P, T], F32, name="window0", align_bytes=64)]
+        for u in range(PACK):
+            nc.gpsimd.memset(windows[0][:, u * N : (u + 1) * N], 0.0)
         kb_pool = keep.tile([P, T], F32, name="kb_pool", align_bytes=64)
         nc.scalar.dma_start(kb_pool[P - 1 : P, :], kb[0:1, :])
         nc.vector.memset(kb_pool[0 : P - 1, :], 0.0)
@@ -125,7 +130,7 @@ def tile_attend_gkl_w_kb_kernel(tc, xT, w_words, w_scales, y, wt, kb, xm, offs, 
             xm_raw.extend(raw[:, :, u * P : (u + 1) * P] for u in range(blocks))
 
         load_y(0, "y")
-        quantize_x(grouped0[:, : half * K_PASS], 0, 0, half)
+        quantize_x(grouped0[:], 0, 0, PACK)
 
         pairs = keep.tile([P, N], U32, name="pairs", tag="pairs", align_bytes=64)
         nc.vector.tensor_copy(pairs[:], word_pool[:].bitcast(U32).indirect(offsets[:]))
@@ -134,21 +139,21 @@ def tile_attend_gkl_w_kb_kernel(tc, xT, w_words, w_scales, y, wt, kb, xm, offs, 
         for o in range(PASSES):
             nc.vector.tensor_copy(w_codes[:].bitcast(U16)[:, o * N : (o + 1) * N], pairs[:].bitcast(U16)[:, o::PASSES])
 
-        load_y(1, "pairs")
-        grouped1 = keep.tile([P, PACK * K_PASS], BF16, name="x_grouped1", align_bytes=64)
+        load_xm(2, "pairs")
+        grouped1 = keep.tile([P, PACK * K_PASS], BF16, name="x_grouped1", tag="x_grouped1", align_bytes=64)
         for u, on_scalar in enumerate(X_ON_SCALAR):
             first = u * P // 2
             group_x(grouped1, x_raw[1, u], 0, on_scalar, first, nc.scalar.copy)
             group_x(grouped1, x_raw[1, u], on_scalar, P // 2 - on_scalar, first + on_scalar, nc.vector.tensor_copy)
-        load_xm(4, "x10")
+        load_y(1, "x10")
         for t in range(half):
             quantize_x(grouped1[:, t * K_PASS : (t + 1) * K_PASS], 1, t, 1)
         quantize_x(grouped1[:, half * K_PASS :], 1, half, half)
-        quantize_x(grouped0[:, half * K_PASS :], 0, half, half, tag="x11")
 
         scores = [psum.tile([P, N], F32, name=f"scores{t}") for t in range(PACK)]
         for t in range(PACK):
-            for o in range(PASSES):
+            order = range(PASSES) if t < FIRST_LATE else range(PASSES - 1, -1, -1)
+            for step, o in enumerate(order):
                 codes, plane = x_q[o, t]
                 nc.tensor.matmul_mx(
                     out=scores[t][:],
@@ -156,18 +161,16 @@ def tile_attend_gkl_w_kb_kernel(tc, xT, w_words, w_scales, y, wt, kb, xm, offs, 
                     lhsT_scale=plane,
                     rhs=w_codes[:, o * 2 * N : (o + 1) * 2 * N].bitcast(E2M1),
                     rhs_scale=w_planes[o],
-                    start=(o == 0),
-                    stop=(o == PASSES - 1),
+                    start=(step == 0),
+                    stop=(step == PASSES - 1),
                 )
 
-        load_xm(2, "w_codes")
-        windows = [keep.tile([P, T], F32, name="window0", tag="x_grouped0", align_bytes=64)]
-        nc.gpsimd.memset(windows[0][:], 0.0)
+        load_xm(4, "x11")
 
         neg_z = [keep.tile([P, N], F32, name=f"neg_z{t}", tag=f"neg_z{t}", align_bytes=64) for t in range(PACK)]
         neg_m = [keep.tile([P, 1], F32, name=f"neg_m{t}", tag=f"neg_m{t}", align_bytes=64) for t in range(PACK)]
         e = [keep.tile([P, N], F32, name=f"e{t}", tag=f"e{t}", align_bytes=64) for t in range(PACK)]
-        wy = keep.tile([P, PACK, N], F32, name="wy", align_bytes=64)
+        wy = keep.tile([P, PACK, N], F32, name="wy", tag="x_grouped1", align_bytes=64)
         sums = [keep.tile([P, 1], F32, name=f"sums{t}") for t in range(PACK)]
         inv = [keep.tile([P, 1], F32, name=f"inv{t}") for t in range(PACK)]
         coef = [keep.tile([P, 1], F32, name=f"coef{t}") for t in range(PACK)]
@@ -201,8 +204,8 @@ def tile_attend_gkl_w_kb_kernel(tc, xT, w_words, w_scales, y, wt, kb, xm, offs, 
             grouped = keep.tile([P, count * P * PACK], BF16, name=f"xm_grouped{first}", tag=grouped_tag, align_bytes=64)
             for u, copy in enumerate(copies):
                 copy(
-                    grouped[:, u * P * PACK : (u + 1) * P * PACK].rearrange("p (d t) -> p d t", t=PACK),
-                    xm_raw[first + u].rearrange("p t d -> p d t"),
+                    grouped[:, u * P * PACK : (u + 1) * P * PACK].rearrange("p (c i t) -> p c t i", i=RUN, t=PACK),
+                    xm_raw[first + u].rearrange("p t (c i) -> p c t i", i=RUN),
                 )
             codes = keep.tile([P, count * P], U32, name=f"xm_codes{first}", tag=codes_tag, align_bytes=64)
             plane = keep.tile([P, count * P], U8, name=f"xm_plane{first}", tag=f"xm_plane{first}", align_bytes=64)
@@ -216,9 +219,7 @@ def tile_attend_gkl_w_kb_kernel(tc, xT, w_words, w_scales, y, wt, kb, xm, offs, 
             exp_row(t)
         invert(0)
         exp_row(PACK - 1)
-        for t in range(half):
-            nc.scalar.activation(wy[:, t, :], y_sb[t], ACT.Copy, scale=wt_sb[:, t : t + 1])
-        for t in range(half, PACK):
+        for t in range(PACK):
             nc.gpsimd.tensor_scalar(wy[:, t, :], y_sb[t], wt_sb[:, t : t + 1], 0.0, ALU.mult, ALU.add)
         for t in range(PACK - 1):
             weigh(t)
@@ -234,14 +235,15 @@ def tile_attend_gkl_w_kb_kernel(tc, xT, w_words, w_scales, y, wt, kb, xm, offs, 
         nc.scalar.copy(g_dst[:, : G_SPLIT // RUN], g_src[:, : G_SPLIT // RUN])
         nc.vector.tensor_copy(g_dst[:, G_SPLIT // RUN :], g_src[:, G_SPLIT // RUN :])
 
-        on_scalar, on_vector = nc.scalar.copy, nc.vector.tensor_copy
+        on_scalar = nc.scalar.copy
         quantize_xm(0, [on_scalar] * 2, "xm_grouped0", "e3")
         g_codes = keep.tile([P, N], U32, name="g_codes", align_bytes=64)
         g_plane = keep.tile([P, N], U8, name="g_plane", align_bytes=64)
         nc.vector.quantize_mx(out=g_codes[:].bitcast(E5M2), scales=g_plane[:], in_=g_grouped[:])
-        quantize_xm(2, [on_scalar] * 2, "neg_z3", "g_grouped")
-        quantize_xm(4, [on_scalar] * 2, "g_rows", "e2")
-        quantize_xm(6, [on_vector] * 2, "neg_z2", "e1")
+        quantize_xm(2, [on_scalar] * 2, "neg_z0", "g_grouped")
+        quantize_xm(4, [on_scalar] * 2, "neg_z3", "e1")
+        quantize_xm(6, [on_scalar], "neg_m3", "e0")
+        quantize_xm(7, [on_scalar], "g_rows", "e2")
 
         def zero_window(k, tag):
             win = keep.tile([P, T], F32, name=f"window{k}", tag=tag, align_bytes=64)
@@ -260,27 +262,31 @@ def tile_attend_gkl_w_kb_kernel(tc, xT, w_words, w_scales, y, wt, kb, xm, offs, 
                 stop=True,
             )
 
-        def place(b):
-            bank = acc[b % len(acc)]
-            dense = ring.tile([P, N], F32, name="dense")
-            window = windows[b % WINDOWS]
-            pieces = 2 if b == 0 else 1
-            for u in range(pieces):
-                cols = slice(u * N // pieces, (u + 1) * N // pieces)
-                entries = slice(cols.start // 16, cols.stop // 16)
-                nc.scalar.copy(dense[:, cols], bank[:, cols])
-                nc.vector.tensor_copy(window[:].indirect(offsets[:, entries]), dense[:, cols])
-            nc.sync.dma_start(out[b * P : (b + 1) * P, :], window[:])
+        def place(b, cols, dense):
+            nc.scalar.copy(dense, acc[b % len(acc)][:, cols])
+            entries = slice(cols.start // 16, cols.stop // 16)
+            nc.vector.tensor_copy(windows[b % WINDOWS][:].indirect(offsets[:, entries]), dense)
 
-        zero_window(1, "g_rows")
-        for b in range(len(acc)):
-            multiply(b)
-        for b in range(2):
-            place(b)
-            multiply(b + len(acc))
-        zero_window(2, "e2")
-        zero_window(3, "xm_plane4")
-        for b in range(2, D // P):
-            place(b)
+        def finish(b):
+            nc.sync.dma_start(out[b * P : (b + 1) * P, :], windows[b % WINDOWS][:])
             if b + len(acc) < D // P:
                 multiply(b + len(acc))
+
+        def place_whole(b):
+            dense = ring.tile([P, N], F32, name="dense")
+            place(b, slice(0, N), dense[:])
+            finish(b)
+
+        zero_window(1, "x10")
+        for b in range(len(acc)):
+            multiply(b)
+        low = keep.tile([P, N // 2], F32, name="low", align_bytes=64)
+        place(0, slice(0, N // 2), low[:])
+        place_whole(1)
+        high = keep.tile([P, N // 2], F32, name="high", tag="e3", align_bytes=64)
+        place(0, slice(N // 2, N), high[:])
+        finish(0)
+        zero_window(2, "e1")
+        zero_window(3, "xm_plane4")
+        for b in range(2, D // P):
+            place_whole(b)

@@ -49,12 +49,11 @@ def tile_attend_gkl_w_kb_kernel(tc, xT, w_words, w_scales, y, wt, kb, xm, offs, 
         nc.gpsimd.memset(scale_pool[:], 0)
         identity = keep.tile([P, P], F32, name="identity")
         make_identity(nc, identity[:])
-        windows = [keep.tile([P, T], F32, name="window0", align_bytes=64)]
-        for u in range(PACK):
-            nc.gpsimd.memset(windows[0][:, u * N : (u + 1) * N], 0.0)
         kb_pool = keep.tile([P, T], F32, name="kb_pool", align_bytes=64)
         nc.scalar.dma_start(kb_pool[P - 1 : P, :], kb[0:1, :])
         nc.vector.memset(kb_pool[0 : P - 1, :], 0.0)
+        windows = [keep.tile([P, T], F32, name="window0", align_bytes=64)]
+        nc.vector.memset(windows[0][:], 0.0)
         x_raw = {}
 
         def load_x(o, u):

@@ -23,7 +23,7 @@ N, T, D, R = 512, 2048, 1024, 512
 PASSES = D // K_PASS
 QUADRANT = 32
 SCALE_ROWS = 4
-SHIFT_ROWS = 112
+SHIFTS = ((0, 64), (64, 32), (96, 16))
 WINDOWS = 4
 X_LOADS = (1, 2)
 X_ON_SCALAR = (40, 20)
@@ -87,8 +87,8 @@ def tile_attend_gkl_w_kb_kernel(tc, xT, w_words, w_scales, y, wt, kb, xm, offs, 
         x_q = {}
 
         def group_x(grouped, raw, m0, count, first, copy):
-            dst = grouped[:].rearrange("p (t m j) -> p m t j", t=PACK, j=PACK)[:, first : first + count]
-            src = raw[:].rearrange("p j (m t) -> p m t j", t=PACK)[:, m0 : m0 + count]
+            dst = grouped[:].rearrange("p (t m j) -> p m j t", t=PACK, j=PACK)[:, first : first + count]
+            src = raw[:].rearrange("p j (m t) -> p m j t", t=PACK)[:, m0 : m0 + count]
             copy(dst, src)
 
         def quantize_x(grouped, o, t0, count, tag=None):
@@ -111,7 +111,9 @@ def tile_attend_gkl_w_kb_kernel(tc, xT, w_words, w_scales, y, wt, kb, xm, offs, 
 
         both = keep.tile([P, N], U8, name="both", align_bytes=64)
         nc.vector.tensor_copy(both[:], scale_pool[:].bitcast(U8).indirect(offsets[:]))
-        nc.sync.dma_start(plane1[0:SHIFT_ROWS, :], both[SCALE_ROWS : SCALE_ROWS + SHIFT_ROWS, :].bitcast(I32))
+        for first, count in SHIFTS:
+            rows = both[first + SCALE_ROWS : first + SCALE_ROWS + count, :]
+            nc.sync.dma_start(plane1[first : first + count, :], rows.bitcast(I32))
         w_planes = [both[:], plane1[:].bitcast(U8)]
         y_sb = []
 

@@ -28,7 +28,7 @@ WINDOWS = 4
 X_LOADS = (1, 2)
 X_ON_SCALAR = (40, 20)
 RUN = 4
-G_SPLIT = 240
+HALF = N // 2
 
 FIRST_LATE = 2
 
@@ -39,7 +39,7 @@ def tile_attend_gkl_w_kb_kernel(tc, xT, w_words, w_scales, y, wt, kb, xm, offs, 
     nc = tc.nc
     with ExitStack() as ctx:
         keep = ctx.enter_context(tc.tile_pool(name="keep", bufs=1))
-        ring = ctx.enter_context(tc.tile_pool(name="ring", bufs=3))
+        late = ctx.enter_context(tc.tile_pool(name="late", bufs=1))
         psum = ctx.enter_context(tc.psum_pool(name="psum", bufs=1))
 
         offsets = keep.tile([P, N // 16], U16, name="offsets")
@@ -52,7 +52,7 @@ def tile_attend_gkl_w_kb_kernel(tc, xT, w_words, w_scales, y, wt, kb, xm, offs, 
         kb_pool = keep.tile([P, T], F32, name="kb_pool", align_bytes=64)
         nc.scalar.dma_start(kb_pool[P - 1 : P, :], kb[0:1, :])
         nc.vector.memset(kb_pool[0 : P - 1, :], 0.0)
-        windows = [keep.tile([P, T], F32, name="window0", align_bytes=64)]
+        windows = [keep.tile([P, T], F32, name=f"window{k}", align_bytes=64) for k in range(1)]
         nc.vector.memset(windows[0][:], 0.0)
         x_raw = {}
 
@@ -115,12 +115,13 @@ def tile_attend_gkl_w_kb_kernel(tc, xT, w_words, w_scales, y, wt, kb, xm, offs, 
             rows = both[first + SCALE_ROWS : first + SCALE_ROWS + count, :]
             nc.sync.dma_start(plane1[first : first + count, :], rows.bitcast(I32))
         w_planes = [both[:], plane1[:].bitcast(U8)]
+        halves = (slice(0, HALF), slice(HALF, N))
         y_sb = []
 
         def load_y(h, tag):
-            raw = keep.tile([P, half, N], F32, name=f"y_sb{h}", tag=tag, align_bytes=64)
-            nc.sync.dma_start(raw[:], y[0].rearrange("(p t) i -> p t i", t=PACK)[:, h * half : (h + 1) * half])
-            y_sb.extend(raw[:, u, :] for u in range(half))
+            raw = keep.tile([P, PACK, HALF], F32, name=f"y_sb{h}", tag=tag, align_bytes=64)
+            nc.sync.dma_start(raw[:], y[0].rearrange("(p t) i -> p t i", t=PACK)[:, :, halves[h]])
+            y_sb.append(raw)
 
         xm_raw = []
 
@@ -130,12 +131,12 @@ def tile_attend_gkl_w_kb_kernel(tc, xT, w_words, w_scales, y, wt, kb, xm, offs, 
             nc.sync.dma_start(raw[:], xm[0, :, d0 : d0 + blocks * P].rearrange("(p t) d -> p t d", t=PACK))
             xm_raw.extend(raw[:, :, u * P : (u + 1) * P] for u in range(blocks))
 
-        load_y(0, "y")
+        load_xm(2, "y")
         quantize_x(grouped0[:], 0, 0, PACK)
 
         pairs = keep.tile([P, N], U32, name="pairs", tag="pairs", align_bytes=64)
         nc.vector.tensor_copy(pairs[:], word_pool[:].bitcast(U32).indirect(offsets[:]))
-        load_xm(2, "xm0")
+        load_y(0, "xm0")
         w_codes = keep.tile([P, PASSES * 2 * N], U8, name="w_codes", tag="w_codes", align_bytes=64)
         for o in range(PASSES):
             nc.vector.tensor_copy(w_codes[:].bitcast(U16)[:, o * N : (o + 1) * N], pairs[:].bitcast(U16)[:, o::PASSES])
@@ -151,6 +152,12 @@ def tile_attend_gkl_w_kb_kernel(tc, xT, w_words, w_scales, y, wt, kb, xm, offs, 
             quantize_x(grouped1[:, t * K_PASS : (t + 1) * K_PASS], 1, t, 1)
         quantize_x(grouped1[:, half * K_PASS :], 1, half, half)
 
+        def zero_window(k, tag):
+            win = keep.tile([P, T], F32, name=f"window{k}", tag=tag, align_bytes=64)
+            nc.gpsimd.memset(win[:], 0.0)
+            windows.append(win)
+
+        zero_window(1, "x_grouped1")
         scores = [psum.tile([P, N], F32, name=f"scores{t}") for t in range(PACK)]
         for t in range(PACK):
             order = range(PASSES) if t < FIRST_LATE else range(PASSES - 1, -1, -1)
@@ -171,11 +178,11 @@ def tile_attend_gkl_w_kb_kernel(tc, xT, w_words, w_scales, y, wt, kb, xm, offs, 
         neg_z = [keep.tile([P, N], F32, name=f"neg_z{t}", tag=f"neg_z{t}", align_bytes=64) for t in range(PACK)]
         neg_m = [keep.tile([P, 1], F32, name=f"neg_m{t}", tag=f"neg_m{t}", align_bytes=64) for t in range(PACK)]
         e = [keep.tile([P, N], F32, name=f"e{t}", tag=f"e{t}", align_bytes=64) for t in range(PACK)]
-        wy = keep.tile([P, PACK, N], F32, name="wy", tag="x_grouped1", align_bytes=64)
-        sums = [keep.tile([P, 1], F32, name=f"sums{t}") for t in range(PACK)]
-        inv = [keep.tile([P, 1], F32, name=f"inv{t}") for t in range(PACK)]
+        wy = [keep.tile([P, PACK, HALF], F32, name=f"wy{h}", tag=f"wy{h}", align_bytes=64) for h in range(2)]
+        sums = [keep.tile([P, 1], F32, name=f"sums{t}", tag=f"sums{t}", align_bytes=64) for t in range(PACK)]
+        inv = [keep.tile([P, 1], F32, name=f"inv{t}", tag=f"inv{t}", align_bytes=64) for t in range(PACK)]
         coef = [keep.tile([P, 1], F32, name=f"coef{t}") for t in range(PACK)]
-        g_rows = keep.tile([P, PACK, N], BF16, name="g_rows", tag="g_rows", align_bytes=64)
+        g_rows = [keep.tile([P, PACK, HALF], BF16, name="g_rows0", tag="g_rows0", align_bytes=64)]
 
         def add_bias(t):
             nc.vector.scalar_tensor_tensor(neg_z[t][:], scores[t][:], -1.0, kb_all[:], ALU.mult, ALU.subtract)
@@ -193,26 +200,50 @@ def tile_attend_gkl_w_kb_kernel(tc, xT, w_words, w_scales, y, wt, kb, xm, offs, 
         def weigh(t):
             nc.vector.tensor_scalar(coef[t][:], inv[t][:], wt_sb[:, t : t + 1], None, ALU.mult)
 
-        def gradient(t, cols=slice(0, N)):
+        def gradient(t, h):
             nc.vector.scalar_tensor_tensor(
-                g_rows[:, t, cols], e[t][:, cols], coef[t][:], wy[:, t, cols], ALU.mult, ALU.subtract
+                g_rows[h][:, t, :], e[t][:, halves[h]], coef[t][:], wy[h][:, t, :], ALU.mult, ALU.subtract
             )
 
-        xm_q = []
+        xm_grouped = {}
 
-        def quantize_xm(first, copies, grouped_tag, codes_tag):
-            count = len(copies)
-            grouped = keep.tile([P, count * P * PACK], BF16, name=f"xm_grouped{first}", tag=grouped_tag, align_bytes=64)
-            for u, copy in enumerate(copies):
-                copy(
-                    grouped[:, u * P * PACK : (u + 1) * P * PACK].rearrange("p (c i t) -> p c t i", i=RUN, t=PACK),
-                    xm_raw[first + u].rearrange("p t (c i) -> p c t i", i=RUN),
+        def group_xm(blocks, tag):
+            grouped = keep.tile([P, len(blocks) * K_PASS], BF16, name=f"xm_grouped{blocks[0]}", tag=tag, align_bytes=64)
+            for u, b in enumerate(blocks):
+                nc.scalar.copy(
+                    grouped[:, u * K_PASS : (u + 1) * K_PASS].rearrange("p (c i t) -> p c t i", i=RUN, t=PACK),
+                    xm_raw[b].rearrange("p t (c i) -> p c t i", i=RUN),
                 )
-            codes = keep.tile([P, count * P], U32, name=f"xm_codes{first}", tag=codes_tag, align_bytes=64)
-            plane = keep.tile([P, count * P], U8, name=f"xm_plane{first}", tag=f"xm_plane{first}", align_bytes=64)
-            nc.vector.quantize_mx(out=codes[:].bitcast(E4M3), scales=plane[:], in_=grouped[:])
+                xm_grouped[b] = (grouped, u)
+
+        xm_q = {}
+
+        def quantize_xm(first, count, codes_tag=None):
+            name = f"xm_codes{first}"
+            codes = keep.tile([P, count * P], U32, name=name, tag=codes_tag or name, align_bytes=64)
+            plane = keep.tile([P, count * P], U8, name=f"xm_plane{first}", align_bytes=64)
+            grouped, u = xm_grouped[first]
+            nc.vector.quantize_mx(
+                out=codes[:].bitcast(E4M3), scales=plane[:], in_=grouped[:, u * K_PASS : (u + count) * K_PASS]
+            )
             for u in range(count):
-                xm_q.append((codes[:, u * P : (u + 1) * P], plane[:, u * P : (u + 1) * P]))
+                xm_q[first + u] = (codes[:, u * P : (u + 1) * P], plane[:, u * P : (u + 1) * P])
+
+        g_grouped = [
+            keep.tile([P, HALF * PACK], BF16, name="g_grouped0", align_bytes=64),
+            late.tile([P, HALF * PACK], BF16, name="g_grouped1", align_bytes=64, offset=4 * T - HALF * PACK),
+        ]
+        g_codes = [keep.tile([P, HALF], U32, name=f"g_codes{h}", align_bytes=64) for h in range(2)]
+        g_plane = [keep.tile([P, HALF], U8, name=f"g_plane{h}", tag=f"g_plane{h}", align_bytes=64) for h in range(2)]
+
+        def interleave(h):
+            nc.vector.tensor_copy(
+                g_grouped[h][:].rearrange("p (c i t) -> p c t i", i=RUN, t=PACK),
+                g_rows[h][:].rearrange("p t (c i) -> p c t i", i=RUN),
+            )
+
+        def quantize_g(h):
+            nc.vector.quantize_mx(out=g_codes[h][:].bitcast(E5M2), scales=g_plane[h][:], in_=g_grouped[h][:])
 
         add_bias(0)
         for t in range(PACK - 1):
@@ -220,74 +251,98 @@ def tile_attend_gkl_w_kb_kernel(tc, xT, w_words, w_scales, y, wt, kb, xm, offs, 
             exp_row(t)
         invert(0)
         exp_row(PACK - 1)
+        for h in range(2):
+            for t in range(PACK):
+                nc.gpsimd.tensor_scalar(wy[h][:, t, :], y_sb[h][:, t, :], wt_sb[:, t : t + 1], 0.0, ALU.mult, ALU.add)
+        group_xm([0, 1], "xm_grouped0")
+        group_xm([2, 3], "xm_grouped2")
+        group_xm([4, 5, 6, 7], "neg_z3")
         for t in range(PACK):
-            nc.gpsimd.tensor_scalar(wy[:, t, :], y_sb[t], wt_sb[:, t : t + 1], 0.0, ALU.mult, ALU.add)
-        for t in range(PACK - 1):
             weigh(t)
-            invert(t + 1)
-            gradient(t)
-        weigh(PACK - 1)
-        gradient(PACK - 1, slice(0, G_SPLIT))
-        gradient(PACK - 1, slice(G_SPLIT, N))
+            if t + 1 < PACK:
+                invert(t + 1)
+            gradient(t, 0)
+        interleave(0)
+        quantize_g(0)
+        quantize_xm(0, 2, "sums3")
+        g_rows.append(keep.tile([P, PACK, HALF], BF16, name="g_rows1", tag="inv3", align_bytes=64))
+        for t in range(PACK):
+            gradient(t, 1)
+        interleave(1)
+        quantize_g(1)
+        quantize_xm(2, 2, "wy0")
+        quantize_xm(4, 2, "g_rows0")
 
-        g_grouped = keep.tile([P, N * PACK], BF16, name="g_grouped", tag="g_grouped", align_bytes=64)
-        g_dst = g_grouped[:].rearrange("p (c i t) -> p c t i", i=RUN, t=PACK)
-        g_src = g_rows[:].rearrange("p t (c i) -> p c t i", i=RUN)
-        nc.scalar.copy(g_dst[:, : G_SPLIT // RUN], g_src[:, : G_SPLIT // RUN])
-        nc.vector.tensor_copy(g_dst[:, G_SPLIT // RUN :], g_src[:, G_SPLIT // RUN :])
-
-        on_scalar = nc.scalar.copy
-        quantize_xm(0, [on_scalar] * 2, "xm_grouped0", "e3")
-        g_codes = keep.tile([P, N], U32, name="g_codes", align_bytes=64)
-        g_plane = keep.tile([P, N], U8, name="g_plane", align_bytes=64)
-        nc.vector.quantize_mx(out=g_codes[:].bitcast(E5M2), scales=g_plane[:], in_=g_grouped[:])
-        quantize_xm(2, [on_scalar] * 2, "neg_z0", "g_grouped")
-        quantize_xm(4, [on_scalar] * 2, "neg_z3", "e1")
-        quantize_xm(6, [on_scalar], "neg_m3", "e0")
-        quantize_xm(7, [on_scalar], "g_rows", "e2")
-
-        def zero_window(k, tag):
-            win = keep.tile([P, T], F32, name=f"window{k}", tag=tag, align_bytes=64)
-            nc.gpsimd.memset(win[:], 0.0)
-            windows.append(win)
-
-        def multiply(b):
+        def multiply(b, h, bank):
             codes, plane = xm_q[b]
             nc.tensor.matmul_mx(
-                out=acc[b % len(acc)][:],
+                out=bank,
                 lhsT=codes.bitcast(E4M3),
                 lhsT_scale=plane,
-                rhs=g_codes[:].bitcast(E5M2),
-                rhs_scale=g_plane[:],
+                rhs=g_codes[h][:].bitcast(E5M2),
+                rhs_scale=g_plane[h][:],
                 start=True,
                 stop=True,
             )
 
-        def place(b, cols, dense):
-            nc.scalar.copy(dense, acc[b % len(acc)][:, cols])
-            entries = slice(cols.start // 16, cols.stop // 16)
-            nc.vector.tensor_copy(windows[b % WINDOWS][:].indirect(offsets[:, entries]), dense)
+        dense = {}
 
-        def finish(b):
+        def empty_half(b, h, bank, tag, copy):
+            dense[b, h] = keep.tile([P, HALF], F32, name=f"dense{b}{h}", tag=tag, align_bytes=64)
+            multiply(b, h, bank[:, :HALF])
+            copy(dense[b, h][:], bank[:, :HALF])
+
+        def scatter_half(b, h):
+            entries = offsets[:, h * HALF // 16 : (h + 1) * HALF // 16]
+            nc.scalar.activation(windows[b % WINDOWS][:].indirect(entries), dense[b, h][:], ACT.Copy)
+
+        def store(b):
             nc.sync.dma_start(out[b * P : (b + 1) * P, :], windows[b % WINDOWS][:])
-            if b + len(acc) < D // P:
-                multiply(b + len(acc))
 
-        def place_whole(b):
-            dense = ring.tile([P, N], F32, name="dense")
-            place(b, slice(0, N), dense[:])
-            finish(b)
+        def multiply_whole(b):
+            for h in range(2):
+                multiply(b, h, acc[2][:, halves[h]])
 
-        zero_window(1, "x10")
-        for b in range(len(acc)):
-            multiply(b)
-        low = keep.tile([P, N // 2], F32, name="low", align_bytes=64)
-        place(0, slice(0, N // 2), low[:])
-        place_whole(1)
-        high = keep.tile([P, N // 2], F32, name="high", tag="e3", align_bytes=64)
-        place(0, slice(N // 2, N), high[:])
-        finish(0)
-        zero_window(2, "e1")
-        zero_window(3, "xm_plane4")
-        for b in range(2, D // P):
-            place_whole(b)
+        def place_on_vector(b, tag):
+            whole = keep.tile([P, N], F32, name=f"dense{b}", tag=tag, align_bytes=64)
+            nc.vector.tensor_copy(whole[:], acc[2][:])
+            nc.vector.tensor_copy(windows[b % WINDOWS][:].indirect(offsets[:]), whole[:])
+            store(b)
+
+        on_scalar = nc.scalar.copy
+        empty_half(0, 0, acc[0], "half0", on_scalar)
+        scatter_half(0, 0)
+        empty_half(1, 0, acc[3], "half1", on_scalar)
+        empty_half(0, 1, acc[1], "half3", nc.vector.tensor_copy)
+        nc.vector.tensor_copy(windows[0][:].indirect(offsets[:, HALF // 16 :]), dense[0, 1][:])
+        store(0)
+        scatter_half(1, 0)
+        empty_half(1, 1, acc[1], "half0", on_scalar)
+        empty_half(3, 0, acc[0], "half2", on_scalar)
+        scatter_half(1, 1)
+        store(1)
+        for k in range(2):
+            win = late.tile([P, T], F32, name=f"window{2 + k}", align_bytes=64, offset=k * 4 * T)
+            nc.gpsimd.memset(win[:], 0.0)
+            windows.append(win)
+        multiply_whole(2)
+        place_on_vector(2, "dense2")
+        empty_half(3, 1, acc[1], "half1", on_scalar)
+        scatter_half(3, 0)
+        empty_half(5, 0, acc[3], "half0", on_scalar)
+        scatter_half(3, 1)
+        store(3)
+        multiply_whole(4)
+        place_on_vector(4, "dense4")
+        quantize_xm(6, 2, "dense2")
+        empty_half(5, 1, acc[1], "half2", on_scalar)
+        scatter_half(5, 0)
+        empty_half(7, 0, acc[0], "half1", on_scalar)
+        scatter_half(5, 1)
+        store(5)
+        multiply_whole(6)
+        place_on_vector(6, "dense6")
+        empty_half(7, 1, acc[1], "half0", on_scalar)
+        scatter_half(7, 0)
+        scatter_half(7, 1)
+        store(7)

@@ -24,12 +24,14 @@ PASSES = D // K_PASS
 QUADRANT = 32
 SCALE_ROWS = 4
 SHIFTS = ((0, 64), (64, 32), (96, 16))
-WINDOWS = 4
+BLOCKS = D // P
 X_LOADS = (1, 2)
 X_ON_SCALAR = (40, 20)
 RUN = 4
 HALF = N // 2
 
+ROW = 4 * T
+SHARED = 5 * ROW
 FIRST_LATE = 2
 
 FLOPS = 2 * 2 * R * D * N
@@ -52,8 +54,9 @@ def tile_attend_gkl_w_kb_kernel(tc, xT, w_words, w_scales, y, wt, kb, xm, offs, 
         kb_pool = keep.tile([P, T], F32, name="kb_pool", align_bytes=64)
         nc.scalar.dma_start(kb_pool[P - 1 : P, :], kb[0:1, :])
         nc.vector.memset(kb_pool[0 : P - 1, :], 0.0)
-        windows = [keep.tile([P, T], F32, name=f"window{k}", align_bytes=64) for k in range(1)]
-        nc.vector.memset(windows[0][:], 0.0)
+        windows = [keep.tile([P, T], F32, name=f"window{k}", align_bytes=64) for k in range(2)]
+        for win in windows:
+            nc.vector.memset(win[:], 0.0)
         x_raw = {}
 
         def load_x(o, u):
@@ -119,9 +122,9 @@ def tile_attend_gkl_w_kb_kernel(tc, xT, w_words, w_scales, y, wt, kb, xm, offs, 
         y_sb = []
 
         def load_y(h, tag):
-            raw = keep.tile([P, PACK, HALF], F32, name=f"y_sb{h}", tag=tag, align_bytes=64)
-            nc.sync.dma_start(raw[:], y[0].rearrange("(p t) i -> p t i", t=PACK)[:, :, halves[h]])
-            y_sb.append(raw)
+            raw = keep.tile([P, half, N], F32, name=f"y_sb{h}", tag=tag, align_bytes=64)
+            nc.sync.dma_start(raw[:], y[0].rearrange("(p t) i -> p t i", t=PACK)[:, h * half : (h + 1) * half])
+            y_sb.extend(raw[:, u, :] for u in range(half))
 
         xm_raw = []
 
@@ -141,13 +144,13 @@ def tile_attend_gkl_w_kb_kernel(tc, xT, w_words, w_scales, y, wt, kb, xm, offs, 
         for o in range(PASSES):
             nc.vector.tensor_copy(w_codes[:].bitcast(U16)[:, o * N : (o + 1) * N], pairs[:].bitcast(U16)[:, o::PASSES])
 
-        load_xm(2, "pairs")
+        load_y(1, "pairs")
         grouped1 = keep.tile([P, PACK * K_PASS], BF16, name="x_grouped1", tag="x_grouped1", align_bytes=64)
         for u, on_scalar in enumerate(X_ON_SCALAR):
             first = u * P // 2
             group_x(grouped1, x_raw[1, u], 0, on_scalar, first, nc.scalar.copy)
             group_x(grouped1, x_raw[1, u], on_scalar, P // 2 - on_scalar, first + on_scalar, nc.vector.tensor_copy)
-        load_y(1, "x10")
+        load_xm(2, "x10")
         for t in range(half):
             quantize_x(grouped1[:, t * K_PASS : (t + 1) * K_PASS], 1, t, 1)
         quantize_x(grouped1[:, half * K_PASS :], 1, half, half)
@@ -157,8 +160,7 @@ def tile_attend_gkl_w_kb_kernel(tc, xT, w_words, w_scales, y, wt, kb, xm, offs, 
             nc.gpsimd.memset(win[:], 0.0)
             windows.append(win)
 
-        zero_window(1, "x_grouped1")
-        scores = [psum.tile([P, N], F32, name=f"scores{t}") for t in range(PACK)]
+        scores = [psum.tile([P, N], F32, name=f"scores{t}", tag=f"scores{t}") for t in range(PACK)]
         for t in range(PACK):
             order = range(PASSES) if t < FIRST_LATE else range(PASSES - 1, -1, -1)
             for step, o in enumerate(order):
@@ -173,14 +175,17 @@ def tile_attend_gkl_w_kb_kernel(tc, xT, w_words, w_scales, y, wt, kb, xm, offs, 
                     stop=(step == PASSES - 1),
                 )
 
-        load_xm(4, "x11")
+        load_xm(2, "x11")
+        load_xm(2, "x_codes10")
 
         neg_z = [keep.tile([P, N], F32, name=f"neg_z{t}", tag=f"neg_z{t}", align_bytes=64) for t in range(PACK)]
-        neg_m = [keep.tile([P, 1], F32, name=f"neg_m{t}", tag=f"neg_m{t}", align_bytes=64) for t in range(PACK)]
+        neg_m = [keep.tile([P, 1], F32, name=f"neg_m{t}", align_bytes=64) for t in range(PACK - 1)]
+        neg_m.append(late.tile([P, 1], F32, name="neg_m3", align_bytes=64, offset=ROW))
         e = [keep.tile([P, N], F32, name=f"e{t}", tag=f"e{t}", align_bytes=64) for t in range(PACK)]
-        wy = [keep.tile([P, PACK, HALF], F32, name=f"wy{h}", tag=f"wy{h}", align_bytes=64) for h in range(2)]
+        wy = keep.tile([P, PACK, N], F32, name="wy", tag="x_grouped1", align_bytes=64)
         sums = [keep.tile([P, 1], F32, name=f"sums{t}", tag=f"sums{t}", align_bytes=64) for t in range(PACK)]
-        inv = [keep.tile([P, 1], F32, name=f"inv{t}", tag=f"inv{t}", align_bytes=64) for t in range(PACK)]
+        inv = [keep.tile([P, 1], F32, name=f"inv{t}") for t in range(PACK - 1)]
+        inv.append(late.tile([P, 1], F32, name="inv3", align_bytes=64, offset=SHARED))
         coef = [keep.tile([P, 1], F32, name=f"coef{t}") for t in range(PACK)]
         g_rows = [keep.tile([P, PACK, HALF], BF16, name="g_rows0", tag="g_rows0", align_bytes=64)]
 
@@ -202,15 +207,15 @@ def tile_attend_gkl_w_kb_kernel(tc, xT, w_words, w_scales, y, wt, kb, xm, offs, 
 
         def gradient(t, h):
             nc.vector.scalar_tensor_tensor(
-                g_rows[h][:, t, :], e[t][:, halves[h]], coef[t][:], wy[h][:, t, :], ALU.mult, ALU.subtract
+                g_rows[h][:, t, :], e[t][:, halves[h]], coef[t][:], wy[:, t, halves[h]], ALU.mult, ALU.subtract
             )
 
         xm_grouped = {}
 
-        def group_xm(blocks, tag):
-            grouped = keep.tile([P, len(blocks) * K_PASS], BF16, name=f"xm_grouped{blocks[0]}", tag=tag, align_bytes=64)
-            for u, b in enumerate(blocks):
-                nc.scalar.copy(
+        def group_xm(first, grouped, copies):
+            for u, copy in enumerate(copies):
+                b = first + u
+                copy(
                     grouped[:, u * K_PASS : (u + 1) * K_PASS].rearrange("p (c i t) -> p c t i", i=RUN, t=PACK),
                     xm_raw[b].rearrange("p t (c i) -> p c t i", i=RUN),
                 )
@@ -218,10 +223,8 @@ def tile_attend_gkl_w_kb_kernel(tc, xT, w_words, w_scales, y, wt, kb, xm, offs, 
 
         xm_q = {}
 
-        def quantize_xm(first, count, codes_tag=None):
-            name = f"xm_codes{first}"
-            codes = keep.tile([P, count * P], U32, name=name, tag=codes_tag or name, align_bytes=64)
-            plane = keep.tile([P, count * P], U8, name=f"xm_plane{first}", align_bytes=64)
+        def quantize_xm(first, codes, plane):
+            count = 2
             grouped, u = xm_grouped[first]
             nc.vector.quantize_mx(
                 out=codes[:].bitcast(E4M3), scales=plane[:], in_=grouped[:, u * K_PASS : (u + count) * K_PASS]
@@ -229,15 +232,12 @@ def tile_attend_gkl_w_kb_kernel(tc, xT, w_words, w_scales, y, wt, kb, xm, offs, 
             for u in range(count):
                 xm_q[first + u] = (codes[:, u * P : (u + 1) * P], plane[:, u * P : (u + 1) * P])
 
-        g_grouped = [
-            keep.tile([P, HALF * PACK], BF16, name="g_grouped0", align_bytes=64),
-            late.tile([P, HALF * PACK], BF16, name="g_grouped1", align_bytes=64, offset=4 * T - HALF * PACK),
-        ]
+        g_grouped = [keep.tile([P, HALF * PACK], BF16, name=f"g_grouped{h}", align_bytes=64) for h in range(2)]
         g_codes = [keep.tile([P, HALF], U32, name=f"g_codes{h}", align_bytes=64) for h in range(2)]
         g_plane = [keep.tile([P, HALF], U8, name=f"g_plane{h}", tag=f"g_plane{h}", align_bytes=64) for h in range(2)]
 
-        def interleave(h):
-            nc.vector.tensor_copy(
+        def interleave(h, copy):
+            copy(
                 g_grouped[h][:].rearrange("p (c i t) -> p c t i", i=RUN, t=PACK),
                 g_rows[h][:].rearrange("p t (c i) -> p c t i", i=RUN),
             )
@@ -251,27 +251,46 @@ def tile_attend_gkl_w_kb_kernel(tc, xT, w_words, w_scales, y, wt, kb, xm, offs, 
             exp_row(t)
         invert(0)
         exp_row(PACK - 1)
-        for h in range(2):
-            for t in range(PACK):
-                nc.gpsimd.tensor_scalar(wy[h][:, t, :], y_sb[h][:, t, :], wt_sb[:, t : t + 1], 0.0, ALU.mult, ALU.add)
-        group_xm([0, 1], "xm_grouped0")
-        group_xm([2, 3], "xm_grouped2")
-        group_xm([4, 5, 6, 7], "neg_z3")
+        for t in range(PACK):
+            nc.gpsimd.tensor_scalar(wy[:, t, :], y_sb[t], wt_sb[:, t : t + 1], 0.0, ALU.mult, ALU.add)
+        zero_window(2, "pairs")
+        on_scalar, on_vector = nc.scalar.copy, nc.vector.tensor_copy
+        pair = [P, 2 * K_PASS]
+        group_xm(0, keep.tile(pair, BF16, name="xm_grouped0", align_bytes=64), [on_scalar] * 2)
+        group_xm(2, keep.tile(pair, BF16, name="xm_grouped2", align_bytes=64), [on_scalar] * 2)
         for t in range(PACK):
             weigh(t)
             if t + 1 < PACK:
                 invert(t + 1)
             gradient(t, 0)
-        interleave(0)
+        interleave(0, on_vector)
+        group_xm(4, keep.tile(pair, BF16, name="xm_grouped4", tag="neg_z3", align_bytes=64), [on_scalar] * 2)
         quantize_g(0)
-        quantize_xm(0, 2, "sums3")
-        g_rows.append(keep.tile([P, PACK, HALF], BF16, name="g_rows1", tag="inv3", align_bytes=64))
+        quantize_xm(
+            0,
+            keep.tile([P, 2 * P], U32, name="xm_codes0", tag="sums3", align_bytes=64),
+            keep.tile([P, 2 * P], U8, name="xm_plane0", align_bytes=64),
+        )
+        g_rows.append(late.tile([P, PACK, HALF], BF16, name="g_rows1", align_bytes=64, offset=SHARED))
         for t in range(PACK):
             gradient(t, 1)
-        interleave(1)
+        interleave(1, on_vector)
         quantize_g(1)
-        quantize_xm(2, 2, "wy0")
-        quantize_xm(4, 2, "g_rows0")
+        group_xm(6, late.tile(pair, BF16, name="xm_grouped6", align_bytes=64, offset=ROW - K_PASS * 2), [on_scalar] * 2)
+        quantize_xm(
+            2,
+            keep.tile([P, 2 * P], U32, name="xm_codes2", tag="g_rows0", align_bytes=64),
+            keep.tile([P, 2 * P], U8, name="xm_plane2", align_bytes=64),
+        )
+
+        def quantize_later_xm():
+            for u in range(2):
+                first = 4 + 2 * u
+                quantize_xm(
+                    first,
+                    late.tile([P, 2 * P], U32, name=f"xm_codes{first}", align_bytes=64, offset=SHARED + u * 8 * P),
+                    late.tile([P, 2 * P], U8, name=f"xm_plane{first}", align_bytes=64, offset=(4 * ROW, 3 * ROW - P)[u]),
+                )
 
         def multiply(b, h, bank):
             codes, plane = xm_q[b]
@@ -285,64 +304,75 @@ def tile_attend_gkl_w_kb_kernel(tc, xT, w_words, w_scales, y, wt, kb, xm, offs, 
                 stop=True,
             )
 
+        banks = {0: acc[0], 1: acc[2], 2: acc[3], 7: acc[0]}
+        for t in range(PACK):
+            banks[3 + t] = psum.tile([P, N], F32, name=f"bank{3 + t}", tag=f"scores{t}")
         dense = {}
 
-        def empty_half(b, h, bank, tag, copy):
+        def empty_half(b, h, tag, bank=None):
             dense[b, h] = keep.tile([P, HALF], F32, name=f"dense{b}{h}", tag=tag, align_bytes=64)
-            multiply(b, h, bank[:, :HALF])
-            copy(dense[b, h][:], bank[:, :HALF])
+            nc.scalar.copy(dense[b, h][:], (bank or banks[b])[:, halves[h]])
 
         def scatter_half(b, h):
             entries = offsets[:, h * HALF // 16 : (h + 1) * HALF // 16]
-            nc.scalar.activation(windows[b % WINDOWS][:].indirect(entries), dense[b, h][:], ACT.Copy)
+            nc.scalar.activation(windows[b][:].indirect(entries), dense[b, h][:], ACT.Copy)
 
         def store(b):
-            nc.sync.dma_start(out[b * P : (b + 1) * P, :], windows[b % WINDOWS][:])
+            nc.sync.dma_start(out[b * P : (b + 1) * P, :], windows[b][:])
 
         def multiply_whole(b):
             for h in range(2):
-                multiply(b, h, acc[2][:, halves[h]])
+                multiply(b, h, banks[b][:, halves[h]])
 
-        def place_on_vector(b, tag):
-            whole = keep.tile([P, N], F32, name=f"dense{b}", tag=tag, align_bytes=64)
-            nc.vector.tensor_copy(whole[:], acc[2][:])
-            nc.vector.tensor_copy(windows[b % WINDOWS][:].indirect(offsets[:]), whole[:])
+        def empty_whole(b, tag):
+            dense[b] = keep.tile([P, N], F32, name=f"dense{b}", tag=tag, align_bytes=64)
+            nc.vector.tensor_copy(dense[b][:], banks[b][:])
+
+        def place_on_vector(b):
+            nc.vector.tensor_copy(windows[b][:].indirect(offsets[:]), dense[b][:])
             store(b)
 
-        on_scalar = nc.scalar.copy
-        empty_half(0, 0, acc[0], "half0", on_scalar)
+        multiply(0, 0, banks[0][:, :HALF])
+        empty_half(0, 0, "half0")
         scatter_half(0, 0)
-        empty_half(1, 0, acc[3], "half1", on_scalar)
-        empty_half(0, 1, acc[1], "half3", nc.vector.tensor_copy)
+        multiply(1, 0, banks[1][:, :HALF])
+        empty_half(1, 0, "half1")
+        dense[0, 1] = keep.tile([P, HALF], F32, name="dense01", tag="dense01", align_bytes=64)
+        multiply(0, 1, acc[1][:, :HALF])
+        nc.vector.tensor_copy(dense[0, 1][:], acc[1][:, :HALF])
+        quantize_later_xm()
+        multiply_whole(2)
+        for b in range(3, BLOCKS):
+            multiply_whole(b)
+        empty_whole(2, "dense2")
+        multiply(1, 1, banks[2][:, HALF:])
         nc.vector.tensor_copy(windows[0][:].indirect(offsets[:, HALF // 16 :]), dense[0, 1][:])
         store(0)
         scatter_half(1, 0)
-        empty_half(1, 1, acc[1], "half0", on_scalar)
-        empty_half(3, 0, acc[0], "half2", on_scalar)
+        empty_half(1, 1, "half0", banks[2])
+        empty_half(3, 0, "half2")
         scatter_half(1, 1)
         store(1)
-        for k in range(2):
-            win = late.tile([P, T], F32, name=f"window{2 + k}", align_bytes=64, offset=k * 4 * T)
+        place_on_vector(2)
+        for k in range(5):
+            win = late.tile([P, T], F32, name=f"window{3 + k}", align_bytes=64, offset=k * ROW)
             nc.gpsimd.memset(win[:], 0.0)
             windows.append(win)
-        multiply_whole(2)
-        place_on_vector(2, "dense2")
-        empty_half(3, 1, acc[1], "half1", on_scalar)
+        empty_half(3, 1, "half1")
         scatter_half(3, 0)
-        empty_half(5, 0, acc[3], "half0", on_scalar)
+        empty_half(5, 0, "half0")
         scatter_half(3, 1)
         store(3)
-        multiply_whole(4)
-        place_on_vector(4, "dense4")
-        quantize_xm(6, 2, "dense2")
-        empty_half(5, 1, acc[1], "half2", on_scalar)
+        empty_whole(4, "dense01")
+        place_on_vector(4)
+        empty_half(5, 1, "half2")
         scatter_half(5, 0)
-        empty_half(7, 0, acc[0], "half1", on_scalar)
+        empty_half(7, 0, "half1")
         scatter_half(5, 1)
         store(5)
-        multiply_whole(6)
-        place_on_vector(6, "dense6")
-        empty_half(7, 1, acc[1], "half0", on_scalar)
+        empty_whole(6, "dense2")
+        place_on_vector(6)
+        empty_half(7, 1, "half0")
         scatter_half(7, 0)
         scatter_half(7, 1)
         store(7)

@@ -31,7 +31,8 @@ RUN = 4
 HALF = N // 2
 
 ROW = 4 * T
-SHARED = 5 * ROW
+WINDOWS = 5
+SHARED = 2 * ROW + 4096
 FIRST_LATE = 2
 
 FLOPS = 2 * 2 * R * D * N
@@ -82,7 +83,7 @@ def tile_attend_gkl_w_kb_kernel(tc, xT, w_words, w_scales, y, wt, kb, xm, offs, 
         nc.vector.memset(plane1[P - QUADRANT : P], 0)
 
         kb_g = keep.tile([P, N], F32, name="kb_g", align_bytes=64)
-        nc.vector.tensor_copy(kb_g[:], kb_pool[:].indirect(offsets[:]))
+        nc.scalar.activation(kb_g[:], kb_pool[:].indirect(offsets[:]), ACT.Copy)
         acc = [psum.tile([P, N], F32, name=f"acc{k}") for k in range(4)]
         for c in range(N // P):
             nc.tensor.transpose(acc[0][:, c * P : (c + 1) * P], kb_g[:, c * P : (c + 1) * P], identity[:])
@@ -144,21 +145,16 @@ def tile_attend_gkl_w_kb_kernel(tc, xT, w_words, w_scales, y, wt, kb, xm, offs, 
         for o in range(PASSES):
             nc.vector.tensor_copy(w_codes[:].bitcast(U16)[:, o * N : (o + 1) * N], pairs[:].bitcast(U16)[:, o::PASSES])
 
-        load_y(1, "pairs")
-        grouped1 = keep.tile([P, PACK * K_PASS], BF16, name="x_grouped1", tag="x_grouped1", align_bytes=64)
+        load_xm(2, "pairs")
+        grouped1 = late.tile([P, PACK * K_PASS], BF16, name="x_grouped1", align_bytes=64, offset=0)
         for u, on_scalar in enumerate(X_ON_SCALAR):
             first = u * P // 2
             group_x(grouped1, x_raw[1, u], 0, on_scalar, first, nc.scalar.copy)
             group_x(grouped1, x_raw[1, u], on_scalar, P // 2 - on_scalar, first + on_scalar, nc.vector.tensor_copy)
-        load_xm(2, "x10")
+        load_y(1, "x10")
         for t in range(half):
             quantize_x(grouped1[:, t * K_PASS : (t + 1) * K_PASS], 1, t, 1)
         quantize_x(grouped1[:, half * K_PASS :], 1, half, half)
-
-        def zero_window(k, tag):
-            win = keep.tile([P, T], F32, name=f"window{k}", tag=tag, align_bytes=64)
-            nc.gpsimd.memset(win[:], 0.0)
-            windows.append(win)
 
         scores = [psum.tile([P, N], F32, name=f"scores{t}", tag=f"scores{t}") for t in range(PACK)]
         for t in range(PACK):
@@ -178,14 +174,13 @@ def tile_attend_gkl_w_kb_kernel(tc, xT, w_words, w_scales, y, wt, kb, xm, offs, 
         load_xm(2, "x11")
         load_xm(2, "x_codes10")
 
-        neg_z = [keep.tile([P, N], F32, name=f"neg_z{t}", tag=f"neg_z{t}", align_bytes=64) for t in range(PACK)]
-        neg_m = [keep.tile([P, 1], F32, name=f"neg_m{t}", align_bytes=64) for t in range(PACK - 1)]
-        neg_m.append(late.tile([P, 1], F32, name="neg_m3", align_bytes=64, offset=ROW))
+        neg_z = [keep.tile([P, N], F32, name=f"neg_z{t}", align_bytes=64) for t in range(PACK - 1)]
+        neg_z.append(late.tile([P, N], F32, name="neg_z3", align_bytes=64, offset=SHARED + 3072))
+        neg_m = [keep.tile([P, 1], F32, name=f"neg_m{t}", align_bytes=64) for t in range(PACK)]
         e = [keep.tile([P, N], F32, name=f"e{t}", tag=f"e{t}", align_bytes=64) for t in range(PACK)]
-        wy = keep.tile([P, PACK, N], F32, name="wy", tag="x_grouped1", align_bytes=64)
+        wy = keep.tile([P, PACK, N], F32, name="wy", align_bytes=64)
         sums = [keep.tile([P, 1], F32, name=f"sums{t}", tag=f"sums{t}", align_bytes=64) for t in range(PACK)]
-        inv = [keep.tile([P, 1], F32, name=f"inv{t}") for t in range(PACK - 1)]
-        inv.append(late.tile([P, 1], F32, name="inv3", align_bytes=64, offset=SHARED))
+        inv = [keep.tile([P, 1], F32, name=f"inv{t}") for t in range(PACK)]
         coef = [keep.tile([P, 1], F32, name=f"coef{t}") for t in range(PACK)]
         g_rows = [keep.tile([P, PACK, HALF], BF16, name="g_rows0", tag="g_rows0", align_bytes=64)]
 
@@ -205,9 +200,9 @@ def tile_attend_gkl_w_kb_kernel(tc, xT, w_words, w_scales, y, wt, kb, xm, offs, 
         def weigh(t):
             nc.vector.tensor_scalar(coef[t][:], inv[t][:], wt_sb[:, t : t + 1], None, ALU.mult)
 
-        def gradient(t, h):
+        def gradient(t, cols, numerator, factor):
             nc.vector.scalar_tensor_tensor(
-                g_rows[h][:, t, :], e[t][:, halves[h]], coef[t][:], wy[:, t, halves[h]], ALU.mult, ALU.subtract
+                g_rows[0][:, t, cols], numerator[:, cols], factor[:], wy[:, t, cols], ALU.mult, ALU.subtract
             )
 
         xm_grouped = {}
@@ -223,8 +218,7 @@ def tile_attend_gkl_w_kb_kernel(tc, xT, w_words, w_scales, y, wt, kb, xm, offs, 
 
         xm_q = {}
 
-        def quantize_xm(first, codes, plane):
-            count = 2
+        def quantize_xm(first, codes, plane, count=2):
             grouped, u = xm_grouped[first]
             nc.vector.quantize_mx(
                 out=codes[:].bitcast(E4M3), scales=plane[:], in_=grouped[:, u * K_PASS : (u + count) * K_PASS]
@@ -232,18 +226,23 @@ def tile_attend_gkl_w_kb_kernel(tc, xT, w_words, w_scales, y, wt, kb, xm, offs, 
             for u in range(count):
                 xm_q[first + u] = (codes[:, u * P : (u + 1) * P], plane[:, u * P : (u + 1) * P])
 
-        g_grouped = [keep.tile([P, HALF * PACK], BF16, name=f"g_grouped{h}", align_bytes=64) for h in range(2)]
+        quarters = (slice(0, P), slice(P, HALF))
+        low_grouped = [
+            late.tile([P, K_PASS], BF16, name="low_grouped0", align_bytes=64, offset=2 * ROW - K_PASS),
+            keep.tile([P, K_PASS], BF16, name="low_grouped1", align_bytes=64),
+        ]
+        high_grouped = late.tile([P, HALF * PACK], BF16, name="high_grouped", align_bytes=64, offset=2 * ROW - K_PASS)
         g_codes = [keep.tile([P, HALF], U32, name=f"g_codes{h}", align_bytes=64) for h in range(2)]
         g_plane = [keep.tile([P, HALF], U8, name=f"g_plane{h}", tag=f"g_plane{h}", align_bytes=64) for h in range(2)]
 
-        def interleave(h, copy):
-            copy(
-                g_grouped[h][:].rearrange("p (c i t) -> p c t i", i=RUN, t=PACK),
-                g_rows[h][:].rearrange("p t (c i) -> p c t i", i=RUN),
+        def interleave(q):
+            nc.vector.tensor_copy(
+                low_grouped[q][:].rearrange("p (c i t) -> p c t i", i=RUN, t=PACK),
+                g_rows[0][:, :, quarters[q]].rearrange("p t (c i) -> p c t i", i=RUN),
             )
 
-        def quantize_g(h):
-            nc.vector.quantize_mx(out=g_codes[h][:].bitcast(E5M2), scales=g_plane[h][:], in_=g_grouped[h][:])
+        def quantize_g(h, cols, grouped):
+            nc.vector.quantize_mx(out=g_codes[h][:, cols].bitcast(E5M2), scales=g_plane[h][:, cols], in_=grouped[:])
 
         add_bias(0)
         for t in range(PACK - 1):
@@ -253,53 +252,65 @@ def tile_attend_gkl_w_kb_kernel(tc, xT, w_words, w_scales, y, wt, kb, xm, offs, 
         exp_row(PACK - 1)
         for t in range(PACK):
             nc.gpsimd.tensor_scalar(wy[:, t, :], y_sb[t], wt_sb[:, t : t + 1], 0.0, ALU.mult, ALU.add)
-        zero_window(2, "pairs")
+
+        def zero_late(k):
+            win = late.tile([P, T], F32, name=f"window{k}", align_bytes=64, offset=(k - 2) * ROW)
+            nc.gpsimd.memset(win[:], 0.0)
+            windows.append(win)
+
+        zero_late(2)
         on_scalar, on_vector = nc.scalar.copy, nc.vector.tensor_copy
         pair = [P, 2 * K_PASS]
-        group_xm(0, keep.tile(pair, BF16, name="xm_grouped0", align_bytes=64), [on_scalar] * 2)
-        group_xm(2, keep.tile(pair, BF16, name="xm_grouped2", align_bytes=64), [on_scalar] * 2)
-        for t in range(PACK):
+        last = PACK - 1
+        weighed = keep.tile([P, HALF], F32, name="weighed", align_bytes=64)
+        nc.scalar.activation(weighed[:], e[last][:, halves[0]], ACT.Copy, scale=wt_sb[:, last : last + 1])
+        triple = [P, 3 * K_PASS]
+        group_xm(0, keep.tile(triple, BF16, name="xm_grouped0", align_bytes=64), [on_scalar] * 3)
+        xm_grouped3 = keep.tile(pair, BF16, name="xm_grouped3", align_bytes=64)
+        group_xm(3, xm_grouped3[:, :K_PASS], [on_scalar])
+        for t in range(last):
             weigh(t)
-            if t + 1 < PACK:
-                invert(t + 1)
-            gradient(t, 0)
-        interleave(0, on_vector)
-        group_xm(4, keep.tile(pair, BF16, name="xm_grouped4", tag="neg_z3", align_bytes=64), [on_scalar] * 2)
-        quantize_g(0)
+            invert(t + 1)
+            gradient(t, halves[0], e[t], coef[t])
+        for q in range(2):
+            gradient(last, quarters[q], weighed, inv[last])
+        weigh(last)
+        for q in range(2):
+            interleave(q)
+        scaled = late.tile([P, PACK, HALF], F32, name="scaled", align_bytes=64, offset=SHARED)
+        for t in range(PACK):
+            nc.scalar.activation(scaled[:, t, :], e[t][:, halves[1]], ACT.Copy, scale=coef[t][:])
+        group_xm(4, xm_grouped3[:, K_PASS:], [on_scalar])
+        xm_grouped[3] = (xm_grouped3, 0)
+        for q in range(2):
+            quantize_g(0, quarters[q], low_grouped[q])
         quantize_xm(
             0,
-            keep.tile([P, 2 * P], U32, name="xm_codes0", tag="sums3", align_bytes=64),
-            keep.tile([P, 2 * P], U8, name="xm_plane0", align_bytes=64),
+            keep.tile([P, 3 * P], U32, name="xm_codes0", tag="sums3", align_bytes=64),
+            keep.tile([P, 3 * P], U8, name="xm_plane0", align_bytes=64),
+            3,
         )
-        g_rows.append(late.tile([P, PACK, HALF], BF16, name="g_rows1", align_bytes=64, offset=SHARED))
-        for t in range(PACK):
-            gradient(t, 1)
-        interleave(1, on_vector)
-        quantize_g(1)
-        group_xm(6, late.tile(pair, BF16, name="xm_grouped6", align_bytes=64, offset=ROW - K_PASS * 2), [on_scalar] * 2)
+        nc.vector.tensor_tensor(
+            high_grouped[:].rearrange("p (c i t) -> p c t i", i=2, t=PACK),
+            scaled[:].rearrange("p t (c i) -> p c t i", i=2),
+            wy[:, :, halves[1]].rearrange("p t (c i) -> p c t i", i=2),
+            ALU.subtract,
+        )
+        quantize_g(1, slice(0, HALF), high_grouped)
         quantize_xm(
-            2,
-            keep.tile([P, 2 * P], U32, name="xm_codes2", tag="g_rows0", align_bytes=64),
-            keep.tile([P, 2 * P], U8, name="xm_plane2", align_bytes=64),
+            3,
+            late.tile([P, 2 * P], U32, name="xm_codes3", align_bytes=64, offset=2 * ROW),
+            keep.tile([P, 2 * P], U8, name="xm_plane3", align_bytes=64),
         )
 
-        def quantize_later_xm():
-            for u in range(2):
-                first = 4 + 2 * u
-                quantize_xm(
-                    first,
-                    late.tile([P, 2 * P], U32, name=f"xm_codes{first}", align_bytes=64, offset=SHARED + u * 8 * P),
-                    late.tile([P, 2 * P], U8, name=f"xm_plane{first}", align_bytes=64, offset=(4 * ROW, 3 * ROW - P)[u]),
-                )
-
-        def multiply(b, h, bank):
+        def multiply(b, h, bank, cols=slice(0, HALF)):
             codes, plane = xm_q[b]
             nc.tensor.matmul_mx(
                 out=bank,
                 lhsT=codes.bitcast(E4M3),
                 lhsT_scale=plane,
-                rhs=g_codes[h][:].bitcast(E5M2),
-                rhs_scale=g_plane[h][:],
+                rhs=g_codes[h][:, cols].bitcast(E5M2),
+                rhs_scale=g_plane[h][:, cols],
                 start=True,
                 stop=True,
             )
@@ -307,72 +318,99 @@ def tile_attend_gkl_w_kb_kernel(tc, xT, w_words, w_scales, y, wt, kb, xm, offs, 
         banks = {0: acc[0], 1: acc[2], 2: acc[3], 7: acc[0]}
         for t in range(PACK):
             banks[3 + t] = psum.tile([P, N], F32, name=f"bank{3 + t}", tag=f"scores{t}")
+        quarter_banks = (acc[0], banks[6])
         dense = {}
 
-        def empty_half(b, h, tag, bank=None):
-            dense[b, h] = keep.tile([P, HALF], F32, name=f"dense{b}{h}", tag=tag, align_bytes=64)
-            nc.scalar.copy(dense[b, h][:], (bank or banks[b])[:, halves[h]])
+        def half_tile(b, h, place):
+            offset = SHARED + ROW + 8 * N + int(place * 4 * HALF)
+            dense[b, h] = late.tile([P, HALF], F32, name=f"dense{b}{h}", align_bytes=64, offset=offset)
+
+        def empty_half(b, h, place):
+            half_tile(b, h, place)
+            nc.scalar.copy(dense[b, h][:], banks[b][:, halves[h]])
 
         def scatter_half(b, h):
             entries = offsets[:, h * HALF // 16 : (h + 1) * HALF // 16]
-            nc.scalar.activation(windows[b][:].indirect(entries), dense[b, h][:], ACT.Copy)
+            nc.scalar.activation(windows[b % WINDOWS][:].indirect(entries), dense[b, h][:], ACT.Copy)
 
         def store(b):
-            nc.sync.dma_start(out[b * P : (b + 1) * P, :], windows[b][:])
+            nc.sync.dma_start(out[b * P : (b + 1) * P, :], windows[b % WINDOWS][:])
 
         def multiply_whole(b):
             for h in range(2):
                 multiply(b, h, banks[b][:, halves[h]])
 
-        def empty_whole(b, tag):
-            dense[b] = keep.tile([P, N], F32, name=f"dense{b}", tag=tag, align_bytes=64)
-            nc.vector.tensor_copy(dense[b][:], banks[b][:])
+        def empty_whole(b, offset, copy):
+            dense[b] = late.tile([P, N], F32, name=f"dense{b}", align_bytes=64, offset=SHARED + ROW + offset)
+            copy(dense[b][:], banks[b][:])
 
         def place_on_vector(b):
-            nc.vector.tensor_copy(windows[b][:].indirect(offsets[:]), dense[b][:])
+            nc.vector.tensor_copy(windows[b % WINDOWS][:].indirect(offsets[:]), dense[b][:])
             store(b)
 
-        multiply(0, 0, banks[0][:, :HALF])
-        empty_half(0, 0, "half0")
+        half_tile(0, 0, 0)
+        for q in range(2):
+            multiply(0, 0, quarter_banks[q][:, :P], quarters[q])
+            nc.scalar.copy(dense[0, 0][:, quarters[q]], quarter_banks[q][:, :P])
         scatter_half(0, 0)
         multiply(1, 0, banks[1][:, :HALF])
-        empty_half(1, 0, "half1")
-        dense[0, 1] = keep.tile([P, HALF], F32, name="dense01", tag="dense01", align_bytes=64)
+        empty_half(1, 0, 1)
+        dense[0, 1] = late.tile([P, HALF], F32, name="dense01", align_bytes=64, offset=SHARED + ROW + 4 * N)
+        dense[2, 0] = late.tile([P, HALF], F32, name="dense20", align_bytes=64, offset=SHARED + ROW)
+        multiply(2, 0, banks[2][:, :HALF])
+        nc.vector.tensor_copy(dense[2, 0][:], banks[2][:, :HALF])
         multiply(0, 1, acc[1][:, :HALF])
+        multiply(2, 1, banks[5][:, HALF:])
+        multiply(1, 1, banks[1][:, HALF:])
         nc.vector.tensor_copy(dense[0, 1][:], acc[1][:, :HALF])
-        quantize_later_xm()
-        multiply_whole(2)
-        for b in range(3, BLOCKS):
+        dense[2, 1] = late.tile([P, HALF], F32, name="dense21", align_bytes=64, offset=SHARED + ROW + 2 * N)
+        nc.vector.tensor_copy(dense[2, 1][:], banks[5][:, HALF:])
+        for b in range(3, 5):
             multiply_whole(b)
-        empty_whole(2, "dense2")
-        multiply(1, 1, banks[2][:, HALF:])
         nc.vector.tensor_copy(windows[0][:].indirect(offsets[:, HALF // 16 :]), dense[0, 1][:])
         store(0)
+        xm_grouped5 = late.tile(triple, BF16, name="xm_grouped5", align_bytes=64, offset=2 * ROW + 2 * K_PASS)
+        for u in range(3):
+            nc.gpsimd.tensor_scalar(
+                xm_grouped5[:, u * K_PASS : (u + 1) * K_PASS].rearrange("p (d t) -> p d t", t=PACK),
+                xm_raw[5 + u].rearrange("p t d -> p d t"),
+                1.0, 0.0, ALU.mult, ALU.add,
+            )
+        xm_grouped[5] = (xm_grouped5, 0)
+        zero_late(3)
+        windows.append(keep.tile([P, T], F32, name="window4", tag="x_codes10", align_bytes=64))
+        nc.gpsimd.memset(windows[4][:], 0.0)
         scatter_half(1, 0)
-        empty_half(1, 1, "half0", banks[2])
-        empty_half(3, 0, "half2")
+        empty_half(1, 1, 0)
+        empty_half(3, 0, 2)
         scatter_half(1, 1)
         store(1)
-        place_on_vector(2)
-        for k in range(5):
-            win = late.tile([P, T], F32, name=f"window{3 + k}", align_bytes=64, offset=k * ROW)
-            nc.gpsimd.memset(win[:], 0.0)
-            windows.append(win)
-        empty_half(3, 1, "half1")
+        nc.vector.tensor_copy(windows[2][:].indirect(offsets[:, HALF // 16 :]), dense[2, 1][:])
+        empty_whole(4, 4 * N, on_vector)
+        nc.vector.tensor_copy(windows[2][:].indirect(offsets[:, : HALF // 16]), dense[2, 0][:])
+        store(2)
+        quantize_xm(
+            5,
+            keep.tile([P, 3 * P], U32, name="xm_codes5", align_bytes=64),
+            keep.tile([P, 3 * P], U8, name="xm_plane5", align_bytes=64),
+            3,
+        )
+        for b in range(5, BLOCKS):
+            multiply_whole(b)
+        empty_half(3, 1, 0.5)
         scatter_half(3, 0)
-        empty_half(5, 0, "half0")
         scatter_half(3, 1)
         store(3)
-        empty_whole(4, "dense01")
         place_on_vector(4)
-        empty_half(5, 1, "half2")
+        empty_half(5, 0, 0)
+        empty_half(5, 1, 1)
         scatter_half(5, 0)
-        empty_half(7, 0, "half1")
+        empty_half(7, 0, 2)
         scatter_half(5, 1)
         store(5)
-        empty_whole(6, "dense2")
+        empty_whole(6, 4 * N, on_vector)
         place_on_vector(6)
-        empty_half(7, 1, "half0")
+        empty_half(7, 1, 0)
         scatter_half(7, 0)
         scatter_half(7, 1)
         store(7)

@@ -23,7 +23,7 @@ N, T, D, R = 512, 2048, 1024, 512
 PASSES = D // K_PASS
 QUADRANT = 32
 SCALE_ROWS = 4
-SHIFTS = ((0, 64), (64, 32), (96, 16))
+SPREAD = 8
 BLOCKS = D // P
 X_LOADS = (1, 2)
 X_ON_SCALAR = (40, 20)
@@ -70,9 +70,10 @@ def tile_attend_gkl_w_kb_kernel(tc, xT, w_words, w_scales, y, wt, kb, xm, offs, 
         load_x(0, 0)
         for q in (0, 2, 1, 3):
             nc.sync.dma_start(
-                scale_pool[QUADRANT * q : QUADRANT * q + PASSES * SCALE_ROWS, :],
-                w_scales.bitcast(I32)[:, SCALE_ROWS * q : SCALE_ROWS * (q + 1), :],
+                scale_pool[QUADRANT * q : QUADRANT * q + SCALE_ROWS, :],
+                w_scales.bitcast(I32)[0, SCALE_ROWS * q : SCALE_ROWS * (q + 1), :],
             )
+        nc.sync.dma_start(scale_pool[SCALE_ROWS:P:SPREAD, :], w_scales.bitcast(I32)[1])
         word_pool = keep.tile([P, T], I32, name="word_pool", tag="xm0", align_bytes=64)
         nc.sync.dma_start(word_pool[:], w_words[0].rearrange("p n t -> p (n t)").bitcast(I32))
         load_x(1, 0)
@@ -80,7 +81,7 @@ def tile_attend_gkl_w_kb_kernel(tc, xT, w_words, w_scales, y, wt, kb, xm, offs, 
         wt_sb = keep.tile([P, PACK], F32, name="wt_sb", align_bytes=64)
         nc.sync.dma_start(wt_sb[:], wt[0].rearrange("(p t) one -> p (t one)", t=PACK))
         plane1 = keep.tile([P, N // 4], I32, name="plane1", align_bytes=64)
-        nc.vector.memset(plane1[P - QUADRANT : P], 0)
+        nc.vector.memset(plane1[:], 0)
 
         kb_g = keep.tile([P, N], F32, name="kb_g", align_bytes=64)
         nc.scalar.activation(kb_g[:], kb_pool[:].indirect(offsets[:]), ACT.Copy)
@@ -115,9 +116,9 @@ def tile_attend_gkl_w_kb_kernel(tc, xT, w_words, w_scales, y, wt, kb, xm, offs, 
 
         both = keep.tile([P, N], U8, name="both", align_bytes=64)
         nc.vector.tensor_copy(both[:], scale_pool[:].bitcast(U8).indirect(offsets[:]))
-        for first, count in SHIFTS:
-            rows = both[first + SCALE_ROWS : first + SCALE_ROWS + count, :]
-            nc.sync.dma_start(plane1[first : first + count, :], rows.bitcast(I32))
+        for first in range(0, P, QUADRANT):
+            rows = both[first + SCALE_ROWS : first + QUADRANT : SPREAD, :]
+            nc.sync.dma_start(plane1[first : first + SCALE_ROWS, :], rows.bitcast(I32))
         w_planes = [both[:], plane1[:].bitcast(U8)]
         halves = (slice(0, HALF), slice(HALF, N))
         y_sb = []

@@ -26,6 +26,7 @@ SCALE_ROWS = 4
 SPREAD = 8
 BLOCKS = D // P
 X_LOADS = (1, 2)
+X0_ON_SCALAR = 32
 X_ON_SCALAR = (40, 20)
 RUN = 4
 HALF = N // 2
@@ -33,6 +34,7 @@ HALF = N // 2
 ROW = 4 * T
 WINDOWS = 5
 SHARED = 2 * ROW + 4096
+BEHIND = SHARED + ROW + 7168
 FIRST_LATE = 2
 
 FLOPS = 2 * 2 * R * D * N
@@ -55,6 +57,8 @@ def tile_attend_gkl_w_kb_kernel(tc, xT, w_words, w_scales, y, wt, kb, xm, offs, 
         kb_pool = keep.tile([P, T], F32, name="kb_pool", align_bytes=64)
         nc.scalar.dma_start(kb_pool[P - 1 : P, :], kb[0:1, :])
         nc.vector.memset(kb_pool[0 : P - 1, :], 0.0)
+        wt_sb = keep.tile([P, PACK], F32, name="wt_sb", align_bytes=64)
+        nc.scalar.dma_start(wt_sb[:], wt[0].rearrange("(p t) one -> p (t one)", t=PACK))
         windows = [keep.tile([P, T], F32, name=f"window{k}", align_bytes=64) for k in range(2)]
         for win in windows:
             nc.vector.memset(win[:], 0.0)
@@ -78,8 +82,6 @@ def tile_attend_gkl_w_kb_kernel(tc, xT, w_words, w_scales, y, wt, kb, xm, offs, 
         nc.sync.dma_start(word_pool[:], w_words[0].rearrange("p n t -> p (n t)").bitcast(I32))
         load_x(1, 0)
         load_x(1, 1)
-        wt_sb = keep.tile([P, PACK], F32, name="wt_sb", align_bytes=64)
-        nc.sync.dma_start(wt_sb[:], wt[0].rearrange("(p t) one -> p (t one)", t=PACK))
         plane1 = keep.tile([P, N // 4], I32, name="plane1", align_bytes=64)
         nc.vector.memset(plane1[:], 0)
 
@@ -105,8 +107,8 @@ def tile_attend_gkl_w_kb_kernel(tc, xT, w_words, w_scales, y, wt, kb, xm, offs, 
 
         half = PACK // 2
         grouped0 = keep.tile([P, PACK * K_PASS], BF16, name="x_grouped0", tag="x_grouped0", align_bytes=64)
-        group_x(grouped0, x_raw[0, 0], 0, P // 2, 0, nc.scalar.copy)
-        group_x(grouped0, x_raw[0, 0], P // 2, P // 2, P // 2, nc.vector.tensor_copy)
+        group_x(grouped0, x_raw[0, 0], 0, X0_ON_SCALAR, 0, nc.scalar.copy)
+        group_x(grouped0, x_raw[0, 0], X0_ON_SCALAR, P - X0_ON_SCALAR, X0_ON_SCALAR, nc.vector.tensor_copy)
         kb_col = keep.tile([P, N // P], F32, name="kb_col", align_bytes=64)
         nc.scalar.copy(kb_col[:], acc[0][:, P - 1 : N : P])
         for c in range(N // P):
@@ -136,7 +138,7 @@ def tile_attend_gkl_w_kb_kernel(tc, xT, w_words, w_scales, y, wt, kb, xm, offs, 
             nc.sync.dma_start(raw[:], xm[0, :, d0 : d0 + blocks * P].rearrange("(p t) d -> p t d", t=PACK))
             xm_raw.extend(raw[:, :, u * P : (u + 1) * P] for u in range(blocks))
 
-        load_xm(2, "y")
+        load_xm(3, "y")
         quantize_x(grouped0[:], 0, 0, PACK)
 
         pairs = keep.tile([P, N], U32, name="pairs", tag="pairs", align_bytes=64)
@@ -146,13 +148,13 @@ def tile_attend_gkl_w_kb_kernel(tc, xT, w_words, w_scales, y, wt, kb, xm, offs, 
         for o in range(PASSES):
             nc.vector.tensor_copy(w_codes[:].bitcast(U16)[:, o * N : (o + 1) * N], pairs[:].bitcast(U16)[:, o::PASSES])
 
-        load_xm(2, "pairs")
+        load_y(1, "pairs")
         grouped1 = late.tile([P, PACK * K_PASS], BF16, name="x_grouped1", align_bytes=64, offset=0)
         for u, on_scalar in enumerate(X_ON_SCALAR):
             first = u * P // 2
             group_x(grouped1, x_raw[1, u], 0, on_scalar, first, nc.scalar.copy)
             group_x(grouped1, x_raw[1, u], on_scalar, P // 2 - on_scalar, first + on_scalar, nc.vector.tensor_copy)
-        load_y(1, "x10")
+        load_xm(1, "x10")
         for t in range(half):
             quantize_x(grouped1[:, t * K_PASS : (t + 1) * K_PASS], 1, t, 1)
         quantize_x(grouped1[:, half * K_PASS :], 1, half, half)
@@ -172,10 +174,9 @@ def tile_attend_gkl_w_kb_kernel(tc, xT, w_words, w_scales, y, wt, kb, xm, offs, 
                     stop=(step == PASSES - 1),
                 )
 
-        load_xm(2, "x11")
-        load_xm(2, "x_codes10")
+        load_xm(4, "x11")
 
-        neg_z = [keep.tile([P, N], F32, name=f"neg_z{t}", align_bytes=64) for t in range(PACK - 1)]
+        neg_z = [keep.tile([P, N], F32, name=f"neg_z{t}", tag=f"neg_z{t}", align_bytes=64) for t in range(PACK - 1)]
         neg_z.append(late.tile([P, N], F32, name="neg_z3", align_bytes=64, offset=SHARED + 3072))
         neg_m = [keep.tile([P, 1], F32, name=f"neg_m{t}", align_bytes=64) for t in range(PACK)]
         e = [keep.tile([P, N], F32, name=f"e{t}", tag=f"e{t}", align_bytes=64) for t in range(PACK)]
@@ -254,21 +255,19 @@ def tile_attend_gkl_w_kb_kernel(tc, xT, w_words, w_scales, y, wt, kb, xm, offs, 
         for t in range(PACK):
             nc.gpsimd.tensor_scalar(wy[:, t, :], y_sb[t], wt_sb[:, t : t + 1], 0.0, ALU.mult, ALU.add)
 
-        def zero_late(k):
-            win = late.tile([P, T], F32, name=f"window{k}", align_bytes=64, offset=(k - 2) * ROW)
+        def zero_late(k, offset):
+            win = late.tile([P, T], F32, name=f"window{k}", align_bytes=64, offset=offset)
             nc.gpsimd.memset(win[:], 0.0)
             windows.append(win)
 
-        zero_late(2)
+        zero_late(2, 0)
         on_scalar, on_vector = nc.scalar.copy, nc.vector.tensor_copy
-        pair = [P, 2 * K_PASS]
         last = PACK - 1
-        weighed = keep.tile([P, HALF], F32, name="weighed", align_bytes=64)
+        weighed = late.tile([P, HALF], F32, name="weighed", align_bytes=64, offset=BEHIND + 2560)
         nc.scalar.activation(weighed[:], e[last][:, halves[0]], ACT.Copy, scale=wt_sb[:, last : last + 1])
         triple = [P, 3 * K_PASS]
         group_xm(0, keep.tile(triple, BF16, name="xm_grouped0", align_bytes=64), [on_scalar] * 3)
-        xm_grouped3 = keep.tile(pair, BF16, name="xm_grouped3", align_bytes=64)
-        group_xm(3, xm_grouped3[:, :K_PASS], [on_scalar])
+        group_xm(3, keep.tile([P, K_PASS], BF16, name="xm_grouped3", tag="neg_z1", align_bytes=64), [on_scalar])
         for t in range(last):
             weigh(t)
             invert(t + 1)
@@ -281,8 +280,7 @@ def tile_attend_gkl_w_kb_kernel(tc, xT, w_words, w_scales, y, wt, kb, xm, offs, 
         scaled = late.tile([P, PACK, HALF], F32, name="scaled", align_bytes=64, offset=SHARED)
         for t in range(PACK):
             nc.scalar.activation(scaled[:, t, :], e[t][:, halves[1]], ACT.Copy, scale=coef[t][:])
-        group_xm(4, xm_grouped3[:, K_PASS:], [on_scalar])
-        xm_grouped[3] = (xm_grouped3, 0)
+        group_xm(4, late.tile([P, K_PASS], BF16, name="xm_grouped4", align_bytes=64, offset=BEHIND + 2560), [on_scalar])
         for q in range(2):
             quantize_g(0, quarters[q], low_grouped[q])
         quantize_xm(
@@ -298,11 +296,13 @@ def tile_attend_gkl_w_kb_kernel(tc, xT, w_words, w_scales, y, wt, kb, xm, offs, 
             ALU.subtract,
         )
         quantize_g(1, slice(0, HALF), high_grouped)
-        quantize_xm(
-            3,
-            late.tile([P, 2 * P], U32, name="xm_codes3", align_bytes=64, offset=2 * ROW),
-            keep.tile([P, 2 * P], U8, name="xm_plane3", align_bytes=64),
-        )
+        for b in (3, 4):
+            quantize_xm(
+                b,
+                late.tile([P, P], U32, name=f"xm_codes{b}", align_bytes=64, offset=2 * ROW + (b - 3) * 4 * P),
+                keep.tile([P, P], U8, name=f"xm_plane{b}", align_bytes=64),
+                1,
+            )
 
         def multiply(b, h, bank, cols=slice(0, HALF)):
             codes, plane = xm_q[b]
@@ -370,7 +370,8 @@ def tile_attend_gkl_w_kb_kernel(tc, xT, w_words, w_scales, y, wt, kb, xm, offs, 
             multiply_whole(b)
         nc.vector.tensor_copy(windows[0][:].indirect(offsets[:, HALF // 16 :]), dense[0, 1][:])
         store(0)
-        xm_grouped5 = late.tile(triple, BF16, name="xm_grouped5", align_bytes=64, offset=2 * ROW + 2 * K_PASS)
+        zero_late(3, BEHIND + 3072)
+        xm_grouped5 = late.tile(triple, BF16, name="xm_grouped5", align_bytes=64, offset=BEHIND)
         for u in range(3):
             nc.gpsimd.tensor_scalar(
                 xm_grouped5[:, u * K_PASS : (u + 1) * K_PASS].rearrange("p (d t) -> p d t", t=PACK),
@@ -378,8 +379,7 @@ def tile_attend_gkl_w_kb_kernel(tc, xT, w_words, w_scales, y, wt, kb, xm, offs, 
                 1.0, 0.0, ALU.mult, ALU.add,
             )
         xm_grouped[5] = (xm_grouped5, 0)
-        zero_late(3)
-        windows.append(keep.tile([P, T], F32, name="window4", tag="x_codes10", align_bytes=64))
+        windows.append(keep.tile([P, T], F32, name="window4", tag="x11", align_bytes=64))
         nc.gpsimd.memset(windows[4][:], 0.0)
         scatter_half(1, 0)
         empty_half(1, 1, 0)

@@ -231,7 +231,7 @@ def tile_attend_gkl_w_kb_kernel(tc, xT, w_words, w_scales, y, wt, kb, xm, offs, 
         quarters = (slice(0, P), slice(P, HALF))
         low_grouped = [
             late.tile([P, K_PASS], BF16, name="low_grouped0", align_bytes=64, offset=2 * ROW - K_PASS),
-            keep.tile([P, K_PASS], BF16, name="low_grouped1", align_bytes=64),
+            late.tile([P, K_PASS], BF16, name="low_grouped1", align_bytes=64, offset=ROW),
         ]
         high_grouped = late.tile([P, HALF * PACK], BF16, name="high_grouped", align_bytes=64, offset=2 * ROW - K_PASS)
         g_codes = [keep.tile([P, HALF], U32, name=f"g_codes{h}", align_bytes=64) for h in range(2)]
@@ -299,7 +299,7 @@ def tile_attend_gkl_w_kb_kernel(tc, xT, w_words, w_scales, y, wt, kb, xm, offs, 
         for b in (3, 4):
             quantize_xm(
                 b,
-                late.tile([P, P], U32, name=f"xm_codes{b}", align_bytes=64, offset=2 * ROW + (b - 3) * 4 * P),
+                late.tile([P, P], U32, name=f"xm_codes{b}", align_bytes=64, offset=ROW + (b - 3) * 4 * P),
                 keep.tile([P, P], U8, name=f"xm_plane{b}", align_bytes=64),
                 1,
             )
@@ -323,12 +323,12 @@ def tile_attend_gkl_w_kb_kernel(tc, xT, w_words, w_scales, y, wt, kb, xm, offs, 
         dense = {}
 
         def half_tile(b, h, place):
-            offset = SHARED + ROW + 8 * N + int(place * 4 * HALF)
+            offset = SHARED + ROW + 8 * N + place * 4 * HALF
             dense[b, h] = late.tile([P, HALF], F32, name=f"dense{b}{h}", align_bytes=64, offset=offset)
 
-        def empty_half(b, h, place):
+        def empty_half(b, h, place, columns=None):
             half_tile(b, h, place)
-            nc.scalar.copy(dense[b, h][:], banks[b][:, halves[h]])
+            nc.scalar.copy(dense[b, h][:], banks[b][:, halves[h]] if columns is None else columns)
 
         def scatter_half(b, h):
             entries = offsets[:, h * HALF // 16 : (h + 1) * HALF // 16]
@@ -357,17 +357,17 @@ def tile_attend_gkl_w_kb_kernel(tc, xT, w_words, w_scales, y, wt, kb, xm, offs, 
         multiply(1, 0, banks[1][:, :HALF])
         empty_half(1, 0, 1)
         dense[0, 1] = late.tile([P, HALF], F32, name="dense01", align_bytes=64, offset=SHARED + ROW + 4 * N)
-        dense[2, 0] = late.tile([P, HALF], F32, name="dense20", align_bytes=64, offset=SHARED + ROW)
+        dense[2] = late.tile([P, N], F32, name="dense2", align_bytes=64, offset=SHARED + ROW)
         multiply(2, 0, banks[2][:, :HALF])
-        nc.vector.tensor_copy(dense[2, 0][:], banks[2][:, :HALF])
+        nc.vector.tensor_copy(dense[2][:, :HALF], banks[2][:, :HALF])
         multiply(0, 1, acc[1][:, :HALF])
         multiply(2, 1, banks[5][:, HALF:])
         multiply(1, 1, banks[1][:, HALF:])
         nc.vector.tensor_copy(dense[0, 1][:], acc[1][:, :HALF])
-        dense[2, 1] = late.tile([P, HALF], F32, name="dense21", align_bytes=64, offset=SHARED + ROW + 2 * N)
-        nc.vector.tensor_copy(dense[2, 1][:], banks[5][:, HALF:])
-        for b in range(3, 5):
-            multiply_whole(b)
+        nc.vector.tensor_copy(dense[2][:, HALF:], banks[5][:, HALF:])
+        multiply(3, 0, acc[1][:, HALF:])
+        multiply(3, 1, banks[3][:, HALF:])
+        multiply_whole(4)
         nc.vector.tensor_copy(windows[0][:].indirect(offsets[:, HALF // 16 :]), dense[0, 1][:])
         store(0)
         zero_late(3, BEHIND + 3072)
@@ -383,13 +383,11 @@ def tile_attend_gkl_w_kb_kernel(tc, xT, w_words, w_scales, y, wt, kb, xm, offs, 
         nc.gpsimd.memset(windows[4][:], 0.0)
         scatter_half(1, 0)
         empty_half(1, 1, 0)
-        empty_half(3, 0, 2)
+        empty_half(3, 0, 2, acc[1][:, HALF:])
         scatter_half(1, 1)
         store(1)
-        nc.vector.tensor_copy(windows[2][:].indirect(offsets[:, HALF // 16 :]), dense[2, 1][:])
+        place_on_vector(2)
         empty_whole(4, 4 * N, on_vector)
-        nc.vector.tensor_copy(windows[2][:].indirect(offsets[:, : HALF // 16]), dense[2, 0][:])
-        store(2)
         quantize_xm(
             5,
             keep.tile([P, 3 * P], U32, name="xm_codes5", align_bytes=64),
@@ -398,20 +396,21 @@ def tile_attend_gkl_w_kb_kernel(tc, xT, w_words, w_scales, y, wt, kb, xm, offs, 
         )
         for b in range(5, BLOCKS):
             multiply_whole(b)
-        empty_half(3, 1, 0.5)
+        empty_half(3, 1, 1)
         scatter_half(3, 0)
         scatter_half(3, 1)
         store(3)
         place_on_vector(4)
         empty_half(5, 0, 0)
-        empty_half(5, 1, 1)
+        empty_half(5, 1, 2)
         scatter_half(5, 0)
-        empty_half(7, 0, 2)
+        empty_half(7, 0, 1)
         scatter_half(5, 1)
         store(5)
-        empty_whole(6, 4 * N, on_vector)
+        empty_whole(6, 2 * N, on_vector)
+        dense[7, 1] = late.tile([P, HALF], F32, name="dense71", align_bytes=64, offset=SHARED + ROW + 6 * N)
+        nc.vector.tensor_copy(dense[7, 1][:], banks[7][:, HALF:])
         place_on_vector(6)
-        empty_half(7, 1, 0)
         scatter_half(7, 0)
         scatter_half(7, 1)
         store(7)

@@ -247,11 +247,14 @@ def tile_attend_gkl_w_kb_kernel(tc, xT, w_words, w_scales, y, wt, kb, xm, offs, 
             nc.vector.quantize_mx(out=g_codes[h][:, cols].bitcast(E5M2), scales=g_plane[h][:, cols], in_=grouped[:])
 
         add_bias(0)
-        for t in range(PACK - 1):
+        for t in range(2):
             add_bias(t + 1)
             exp_row(t)
+        add_bias(3)
         invert(0)
-        exp_row(PACK - 1)
+        exp_row(2)
+        weigh(0)
+        exp_row(3)
         for t in range(PACK):
             nc.gpsimd.tensor_scalar(wy[:, t, :], y_sb[t], wt_sb[:, t : t + 1], 0.0, ALU.mult, ALU.add)
 
@@ -268,7 +271,9 @@ def tile_attend_gkl_w_kb_kernel(tc, xT, w_words, w_scales, y, wt, kb, xm, offs, 
         triple = [P, 3 * K_PASS]
         group_xm(0, keep.tile(triple, BF16, name="xm_grouped0", align_bytes=64), [on_scalar] * 3)
         group_xm(3, keep.tile([P, K_PASS], BF16, name="xm_grouped3", tag="neg_z1", align_bytes=64), [on_scalar])
-        for t in range(last):
+        invert(1)
+        gradient(0, halves[0], e[0], coef[0])
+        for t in range(1, last):
             weigh(t)
             invert(t + 1)
             gradient(t, halves[0], e[t], coef[t])
@@ -285,7 +290,7 @@ def tile_attend_gkl_w_kb_kernel(tc, xT, w_words, w_scales, y, wt, kb, xm, offs, 
             quantize_g(0, quarters[q], low_grouped[q])
         quantize_xm(
             0,
-            keep.tile([P, 3 * P], U32, name="xm_codes0", tag="sums3", align_bytes=64),
+            keep.tile([P, 3 * P], U32, name="xm_codes0", tag="sums1", align_bytes=64),
             keep.tile([P, 3 * P], U8, name="xm_plane0", align_bytes=64),
             3,
         )

@@ -57,8 +57,6 @@ def tile_attend_gkl_w_kb_kernel(tc, xT, w_words, w_scales, y, wt, kb, xm, offs, 
         kb_pool = keep.tile([P, T], F32, name="kb_pool", align_bytes=64)
         nc.scalar.dma_start(kb_pool[P - 1 : P, :], kb[0:1, :])
         nc.vector.memset(kb_pool[0 : P - 1, :], 0.0)
-        wt_sb = keep.tile([P, PACK], F32, name="wt_sb", align_bytes=64)
-        nc.scalar.dma_start(wt_sb[:], wt[0].rearrange("(p t) one -> p (t one)", t=PACK))
         windows = [keep.tile([P, T], F32, name=f"window{k}", align_bytes=64) for k in range(2)]
         for win in windows:
             nc.vector.memset(win[:], 0.0)
@@ -91,11 +89,13 @@ def tile_attend_gkl_w_kb_kernel(tc, xT, w_words, w_scales, y, wt, kb, xm, offs, 
         for c in range(N // P):
             nc.tensor.transpose(acc[0][:, c * P : (c + 1) * P], kb_g[:, c * P : (c + 1) * P], identity[:])
 
+        wt_sb = keep.tile([P, PACK], F32, name="wt_sb", tag="kb_g", align_bytes=64)
+        nc.scalar.dma_start(wt_sb[:], wt[0].rearrange("(p t) one -> p (t one)", t=PACK))
         x_q = {}
 
-        def group_x(grouped, raw, m0, count, first, copy):
-            dst = grouped[:].rearrange("p (t m j) -> p m j t", t=PACK, j=PACK)[:, first : first + count]
-            src = raw[:].rearrange("p j (m t) -> p m j t", t=PACK)[:, m0 : m0 + count]
+        def group_x(grouped, raw, m0, count, first, copy, tiles=slice(0, PACK)):
+            dst = grouped[:].rearrange("p (t m j) -> p m j t", t=PACK, j=PACK)[:, first : first + count, :, tiles]
+            src = raw[:].rearrange("p j (m t) -> p m j t", t=PACK)[:, m0 : m0 + count, :, tiles]
             copy(dst, src)
 
         def quantize_x(grouped, o, t0, count, tag=None):
@@ -152,8 +152,10 @@ def tile_attend_gkl_w_kb_kernel(tc, xT, w_words, w_scales, y, wt, kb, xm, offs, 
         grouped1 = late.tile([P, PACK * K_PASS], BF16, name="x_grouped1", align_bytes=64, offset=0)
         for u, on_scalar in enumerate(X_ON_SCALAR):
             first = u * P // 2
-            group_x(grouped1, x_raw[1, u], 0, on_scalar, first, nc.scalar.copy)
-            group_x(grouped1, x_raw[1, u], on_scalar, P // 2 - on_scalar, first + on_scalar, nc.vector.tensor_copy)
+            for tiles in (slice(0, half), slice(half, PACK)) if u else (slice(0, PACK),):
+                group_x(grouped1, x_raw[1, u], 0, on_scalar, first, nc.scalar.copy, tiles)
+                rest = P // 2 - on_scalar
+                group_x(grouped1, x_raw[1, u], on_scalar, rest, first + on_scalar, nc.vector.tensor_copy, tiles)
         load_xm(1, "x10")
         for t in range(half):
             quantize_x(grouped1[:, t * K_PASS : (t + 1) * K_PASS], 1, t, 1)

@@ -80,6 +80,8 @@ def tile_attend_gkl_w_kb_kernel(tc, xT, w_words, w_scales, y, wt, kb, xm, offs, 
         nc.sync.dma_start(word_pool[:], w_words[0].rearrange("p n t -> p (n t)").bitcast(I32))
         load_x(1, 0)
         load_x(1, 1)
+        wt_sb = keep.tile([P, PACK], F32, name="wt_sb", align_bytes=64)
+        nc.sync.dma_start(wt_sb[:], wt[0].rearrange("(p t) one -> p (t one)", t=PACK))
         plane1 = keep.tile([P, N // 4], I32, name="plane1", align_bytes=64)
         nc.vector.memset(plane1[:], 0)
 
@@ -89,8 +91,6 @@ def tile_attend_gkl_w_kb_kernel(tc, xT, w_words, w_scales, y, wt, kb, xm, offs, 
         for c in range(N // P):
             nc.tensor.transpose(acc[0][:, c * P : (c + 1) * P], kb_g[:, c * P : (c + 1) * P], identity[:])
 
-        wt_sb = keep.tile([P, PACK], F32, name="wt_sb", tag="kb_g", align_bytes=64)
-        nc.scalar.dma_start(wt_sb[:], wt[0].rearrange("(p t) one -> p (t one)", t=PACK))
         x_q = {}
 
         def group_x(grouped, raw, m0, count, first, copy, tiles=slice(0, PACK)):

from contextlib import ExitStack

import concourse.mybir as mybir
from concourse.masks import make_identity

F32 = mybir.dt.float32
BF16 = mybir.dt.bfloat16
I32 = mybir.dt.int32
U32 = mybir.dt.uint32
U16 = mybir.dt.uint16
U8 = mybir.dt.uint8
E4M3 = mybir.dt.float8_e4m3fn_x4
E5M2 = mybir.dt.float8_e5m2_x4
E2M1 = mybir.dt.float4_e2m1fn_x4
ALU = mybir.AluOpType
ACT = mybir.ActivationFunctionType
AX = mybir.AxisListType

P = 128
PACK = 4
K_PASS = P * PACK
N, T, D, R = 512, 2048, 1024, 512
PASSES = D // K_PASS
QUADRANT = 32
SCALE_ROWS = 4
SPREAD = 8
BLOCKS = D // P
X_LOADS = (1, 2)
X0_ON_SCALAR = 32
X_ON_SCALAR = (40, 20)
RUN = 4
HALF = N // 2

ROW = 4 * T
WINDOWS = 5
SHARED = 2 * ROW + 4096
BEHIND = SHARED + ROW + 7168
FIRST_LATE = 2

FLOPS = 2 * 2 * R * D * N


def tile_attend_gkl_w_kb_kernel(tc, xT, w_words, w_scales, y, wt, kb, xm, offs, out):
    nc = tc.nc
    with ExitStack() as ctx:
        keep = ctx.enter_context(tc.tile_pool(name="keep", bufs=1))
        late = ctx.enter_context(tc.tile_pool(name="late", bufs=1))
        psum = ctx.enter_context(tc.psum_pool(name="psum", bufs=1))

        offsets = keep.tile([P, N // 16], U16, name="offsets")
        nc.sync.dma_start(offsets[:], offs)

        scale_pool = keep.tile([P, T // 4], I32, name="scale_pool", tag="y", align_bytes=64)
        nc.gpsimd.memset(scale_pool[:], 0)
        identity = keep.tile([P, P], F32, name="identity")
        make_identity(nc, identity[:])
        kb_pool = keep.tile([P, T], F32, name="kb_pool", align_bytes=64)
        nc.scalar.dma_start(kb_pool[P - 1 : P, :], kb[0:1, :])
        nc.vector.memset(kb_pool[0 : P - 1, :], 0.0)
        windows = [keep.tile([P, T], F32, name=f"window{k}", align_bytes=64) for k in range(2)]
        for win in windows:
            nc.vector.memset(win[:], 0.0)
        x_raw = {}

        def load_x(o, u):
            rows = xT[0, K_PASS * o : K_PASS * (o + 1), :].rearrange("(p j) r -> p j r", j=PACK)
            width = R // X_LOADS[o]
            raw = keep.tile([P, PACK, width], F32, name=f"x_raw{o}{u}", tag=f"x{o}{u}", align_bytes=64)
            nc.sync.dma_start(raw[:], rows[:, :, u * width : (u + 1) * width])
            x_raw[o, u] = raw

        load_x(0, 0)
        for q in (0, 2, 1, 3):
            nc.sync.dma_start(
                scale_pool[QUADRANT * q : QUADRANT * q + SCALE_ROWS, :],
                w_scales.bitcast(I32)[0, SCALE_ROWS * q : SCALE_ROWS * (q + 1), :],
            )
        nc.sync.dma_start(scale_pool[SCALE_ROWS:P:SPREAD, :], w_scales.bitcast(I32)[1])
        word_pool = keep.tile([P, T], I32, name="word_pool", tag="xm0", align_bytes=64)
        nc.sync.dma_start(word_pool[:], w_words[0].rearrange("p n t -> p (n t)").bitcast(I32))
        load_x(1, 0)
        load_x(1, 1)
        wt_sb = keep.tile([P, PACK], F32, name="wt_sb", align_bytes=64)
        nc.sync.dma_start(wt_sb[:], wt[0].rearrange("(p t) one -> p (t one)", t=PACK))
        plane1 = keep.tile([P, N // 4], I32, name="plane1", align_bytes=64)
        nc.vector.memset(plane1[:], 0)

        kb_g = keep.tile([P, N], F32, name="kb_g", align_bytes=64)
        nc.scalar.activation(kb_g[:], kb_pool[:].indirect(offsets[:]), ACT.Copy)
        acc = [psum.tile([P, N], F32, name=f"acc{k}") for k in range(4)]
        for c in range(N // P):
            nc.tensor.transpose(acc[0][:, c * P : (c + 1) * P], kb_g[:, c * P : (c + 1) * P], identity[:])

        x_q = {}

        def group_x(grouped, raw, m0, count, first, copy, tiles=slice(0, PACK)):
            dst = grouped[:].rearrange("p (t m j) -> p m j t", t=PACK, j=PACK)[:, first : first + count, :, tiles]
            src = raw[:].rearrange("p j (m t) -> p m j t", t=PACK)[:, m0 : m0 + count, :, tiles]
            copy(dst, src)

        def quantize_x(grouped, o, t0, count, tag=None):
            codes = keep.tile([P, count * P], U32, name=f"x_codes{o}{t0}", tag=tag or f"x_codes{o}{t0}", align_bytes=64)
            plane = keep.tile([P, count * P], U8, name=f"x_plane{o}{t0}", align_bytes=64)
            nc.vector.quantize_mx(out=codes[:].bitcast(E4M3), scales=plane[:], in_=grouped)
            for u in range(count):
                x_q[o, t0 + u] = (codes[:, u * P : (u + 1) * P], plane[:, u * P : (u + 1) * P])

        half = PACK // 2
        grouped0 = keep.tile([P, PACK * K_PASS], BF16, name="x_grouped0", tag="x_grouped0", align_bytes=64)
        group_x(grouped0, x_raw[0, 0], 0, X0_ON_SCALAR, 0, nc.scalar.copy)
        group_x(grouped0, x_raw[0, 0], X0_ON_SCALAR, P - X0_ON_SCALAR, X0_ON_SCALAR, nc.vector.tensor_copy)
        kb_col = keep.tile([P, N // P], F32, name="kb_col", align_bytes=64)
        nc.scalar.copy(kb_col[:], acc[0][:, P - 1 : N : P])
        for c in range(N // P):
            nc.tensor.transpose(acc[1][:, c * P : (c + 1) * P], kb_col[:, c : c + 1].to_broadcast([P, P]), identity[:])
        kb_all = keep.tile([P, N], F32, name="kb_all")
        nc.scalar.copy(kb_all[:], acc[1][:])

        both = keep.tile([P, N], U8, name="both", align_bytes=64)
        nc.vector.tensor_copy(both[:], scale_pool[:].bitcast(U8).indirect(offsets[:]))
        for first in range(0, P, QUADRANT):
            rows = both[first + SCALE_ROWS : first + QUADRANT : SPREAD, :]
            nc.sync.dma_start(plane1[first : first + SCALE_ROWS, :], rows.bitcast(I32))
        w_planes = [both[:], plane1[:].bitcast(U8)]
        halves = (slice(0, HALF), slice(HALF, N))
        y_sb = []

        def load_y(h, tag):
            raw = keep.tile([P, half, N], F32, name=f"y_sb{h}", tag=tag, align_bytes=64)
            nc.sync.dma_start(raw[:], y[0].rearrange("(p t) i -> p t i", t=PACK)[:, h * half : (h + 1) * half])
            y_sb.extend(raw[:, u, :] for u in range(half))

        xm_raw = []

        def load_xm(blocks, tag):
            d0 = len(xm_raw) * P
            raw = keep.tile([P, PACK, blocks * P], F32, name=f"xm_raw{d0}", tag=tag, align_bytes=64)
            nc.sync.dma_start(raw[:], xm[0, :, d0 : d0 + blocks * P].rearrange("(p t) d -> p t d", t=PACK))
            xm_raw.extend(raw[:, :, u * P : (u + 1) * P] for u in range(blocks))

        load_xm(3, "y")
        quantize_x(grouped0[:], 0, 0, PACK)

        pairs = keep.tile([P, N], U32, name="pairs", tag="pairs", align_bytes=64)
        nc.vector.tensor_copy(pairs[:], word_pool[:].bitcast(U32).indirect(offsets[:]))
        load_y(0, "xm0")
        w_codes = keep.tile([P, PASSES * 2 * N], U8, name="w_codes", tag="w_codes", align_bytes=64)
        for o in range(PASSES):
            nc.vector.tensor_copy(w_codes[:].bitcast(U16)[:, o * N : (o + 1) * N], pairs[:].bitcast(U16)[:, o::PASSES])

        load_y(1, "pairs")
        grouped1 = late.tile([P, PACK * K_PASS], BF16, name="x_grouped1", align_bytes=64, offset=0)
        for u, on_scalar in enumerate(X_ON_SCALAR):
            first = u * P // 2
            for tiles in (slice(0, half), slice(half, PACK)) if u else (slice(0, PACK),):
                group_x(grouped1, x_raw[1, u], 0, on_scalar, first, nc.scalar.copy, tiles)
                rest = P // 2 - on_scalar
                group_x(grouped1, x_raw[1, u], on_scalar, rest, first + on_scalar, nc.vector.tensor_copy, tiles)
        load_xm(1, "x10")
        for t in range(half):
            quantize_x(grouped1[:, t * K_PASS : (t + 1) * K_PASS], 1, t, 1)
        quantize_x(grouped1[:, half * K_PASS :], 1, half, half)

        scores = [psum.tile([P, N], F32, name=f"scores{t}", tag=f"scores{t}") for t in range(PACK)]
        for t in range(PACK):
            order = range(PASSES) if t < FIRST_LATE else range(PASSES - 1, -1, -1)
            for step, o in enumerate(order):
                codes, plane = x_q[o, t]
                nc.tensor.matmul_mx(
                    out=scores[t][:],
                    lhsT=codes.bitcast(E4M3),
                    lhsT_scale=plane,
                    rhs=w_codes[:, o * 2 * N : (o + 1) * 2 * N].bitcast(E2M1),
                    rhs_scale=w_planes[o],
                    start=(step == 0),
                    stop=(step == PASSES - 1),
                )

        load_xm(4, "x11")

        neg_z = [keep.tile([P, N], F32, name=f"neg_z{t}", tag=f"neg_z{t}", align_bytes=64) for t in range(PACK - 1)]
        neg_z.append(late.tile([P, N], F32, name="neg_z3", align_bytes=64, offset=SHARED + 3072))
        neg_m = [keep.tile([P, 1], F32, name=f"neg_m{t}", align_bytes=64) for t in range(PACK)]
        e = [keep.tile([P, N], F32, name=f"e{t}", tag=f"e{t}", align_bytes=64) for t in range(PACK)]
        wy = keep.tile([P, PACK, N], F32, name="wy", align_bytes=64)
        sums = [keep.tile([P, 1], F32, name=f"sums{t}", tag=f"sums{t}", align_bytes=64) for t in range(PACK)]
        inv = [keep.tile([P, 1], F32, name=f"inv{t}") for t in range(PACK)]
        coef = [keep.tile([P, 1], F32, name=f"coef{t}") for t in range(PACK)]
        g_rows = [keep.tile([P, PACK, HALF], BF16, name="g_rows0", tag="g_rows0", align_bytes=64)]

        def add_bias(t):
            nc.vector.scalar_tensor_tensor(neg_z[t][:], scores[t][:], -1.0, kb_all[:], ALU.mult, ALU.subtract)

        def exp_row(t):
            nc.vector.tensor_reduce(neg_m[t][:], neg_z[t][:], AX.X, ALU.min)
            nc.scalar.activation(
                e[t][:], neg_z[t][:], ACT.Exp, bias=neg_m[t][:], scale=-1.0,
                accum_out=sums[t][:],
            )

        def invert(t):
            nc.vector.reciprocal(inv[t][:], sums[t][:])

        def weigh(t):
            nc.vector.tensor_scalar(coef[t][:], inv[t][:], wt_sb[:, t : t + 1], None, ALU.mult)

        def gradient(t, cols, numerator, factor):
            nc.vector.scalar_tensor_tensor(
                g_rows[0][:, t, cols], numerator[:, cols], factor[:], wy[:, t, cols], ALU.mult, ALU.subtract
            )

        xm_grouped = {}

        def group_xm(first, grouped, copies):
            for u, copy in enumerate(copies):
                b = first + u
                copy(
                    grouped[:, u * K_PASS : (u + 1) * K_PASS].rearrange("p (c i t) -> p c t i", i=RUN, t=PACK),
                    xm_raw[b].rearrange("p t (c i) -> p c t i", i=RUN),
                )
                xm_grouped[b] = (grouped, u)

        xm_q = {}

        def quantize_xm(first, codes, plane, count=2):
            grouped, u = xm_grouped[first]
            nc.vector.quantize_mx(
                out=codes[:].bitcast(E4M3), scales=plane[:], in_=grouped[:, u * K_PASS : (u + count) * K_PASS]
            )
            for u in range(count):
                xm_q[first + u] = (codes[:, u * P : (u + 1) * P], plane[:, u * P : (u + 1) * P])

        quarters = (slice(0, P), slice(P, HALF))
        low_grouped = [
            late.tile([P, K_PASS], BF16, name="low_grouped0", align_bytes=64, offset=2 * ROW - K_PASS),
            late.tile([P, K_PASS], BF16, name="low_grouped1", align_bytes=64, offset=ROW),
        ]
        high_grouped = late.tile([P, HALF * PACK], BF16, name="high_grouped", align_bytes=64, offset=2 * ROW - K_PASS)
        g_codes = [keep.tile([P, HALF], U32, name=f"g_codes{h}", align_bytes=64) for h in range(2)]
        g_plane = [keep.tile([P, HALF], U8, name=f"g_plane{h}", tag=f"g_plane{h}", align_bytes=64) for h in range(2)]

        def interleave(q):
            nc.vector.tensor_copy(
                low_grouped[q][:].rearrange("p (c i t) -> p c t i", i=RUN, t=PACK),
                g_rows[0][:, :, quarters[q]].rearrange("p t (c i) -> p c t i", i=RUN),
            )

        def quantize_g(h, cols, grouped):
            nc.vector.quantize_mx(out=g_codes[h][:, cols].bitcast(E5M2), scales=g_plane[h][:, cols], in_=grouped[:])

        add_bias(0)
        for t in range(2):
            add_bias(t + 1)
            exp_row(t)
        add_bias(3)
        invert(0)
        exp_row(2)
        weigh(0)
        exp_row(3)
        for t in range(PACK):
            nc.gpsimd.tensor_scalar(wy[:, t, :], y_sb[t], wt_sb[:, t : t + 1], 0.0, ALU.mult, ALU.add)

        def zero_late(k, offset):
            win = late.tile([P, T], F32, name=f"window{k}", align_bytes=64, offset=offset)
            nc.gpsimd.memset(win[:], 0.0)
            windows.append(win)

        zero_late(2, 0)
        on_scalar, on_vector = nc.scalar.copy, nc.vector.tensor_copy
        last = PACK - 1
        weighed = late.tile([P, HALF], F32, name="weighed", align_bytes=64, offset=BEHIND + 2560)
        nc.scalar.activation(weighed[:], e[last][:, halves[0]], ACT.Copy, scale=wt_sb[:, last : last + 1])
        triple = [P, 3 * K_PASS]
        group_xm(0, keep.tile(triple, BF16, name="xm_grouped0", align_bytes=64), [on_scalar] * 3)
        group_xm(3, keep.tile([P, K_PASS], BF16, name="xm_grouped3", tag="neg_z1", align_bytes=64), [on_scalar])
        invert(1)
        gradient(0, halves[0], e[0], coef[0])
        for t in range(1, last):
            weigh(t)
            invert(t + 1)
            gradient(t, halves[0], e[t], coef[t])
        for q in range(2):
            gradient(last, quarters[q], weighed, inv[last])
        weigh(last)
        for q in range(2):
            interleave(q)
        scaled = late.tile([P, PACK, HALF], F32, name="scaled", align_bytes=64, offset=SHARED)
        for t in range(PACK):
            nc.scalar.activation(scaled[:, t, :], e[t][:, halves[1]], ACT.Copy, scale=coef[t][:])
        group_xm(4, late.tile([P, K_PASS], BF16, name="xm_grouped4", align_bytes=64, offset=BEHIND + 2560), [on_scalar])
        for q in range(2):
            quantize_g(0, quarters[q], low_grouped[q])
        quantize_xm(
            0,
            keep.tile([P, 3 * P], U32, name="xm_codes0", tag="sums1", align_bytes=64),
            keep.tile([P, 3 * P], U8, name="xm_plane0", align_bytes=64),
            3,
        )
        nc.vector.tensor_tensor(
            high_grouped[:].rearrange("p (c i t) -> p c t i", i=2, t=PACK),
            scaled[:].rearrange("p t (c i) -> p c t i", i=2),
            wy[:, :, halves[1]].rearrange("p t (c i) -> p c t i", i=2),
            ALU.subtract,
        )
        quantize_g(1, slice(0, HALF), high_grouped)
        for b in (3, 4):
            quantize_xm(
                b,
                late.tile([P, P], U32, name=f"xm_codes{b}", align_bytes=64, offset=ROW + (b - 3) * 4 * P),
                keep.tile([P, P], U8, name=f"xm_plane{b}", align_bytes=64),
                1,
            )

        def multiply(b, h, bank, cols=slice(0, HALF)):
            codes, plane = xm_q[b]
            nc.tensor.matmul_mx(
                out=bank,
                lhsT=codes.bitcast(E4M3),
                lhsT_scale=plane,
                rhs=g_codes[h][:, cols].bitcast(E5M2),
                rhs_scale=g_plane[h][:, cols],
                start=True,
                stop=True,
            )

        banks = {0: acc[0], 1: acc[2], 2: acc[3], 7: acc[0]}
        for t in range(PACK):
            banks[3 + t] = psum.tile([P, N], F32, name=f"bank{3 + t}", tag=f"scores{t}")
        quarter_banks = (acc[0], banks[6])
        dense = {}

        def half_tile(b, h, place):
            offset = SHARED + ROW + 8 * N + place * 4 * HALF
            dense[b, h] = late.tile([P, HALF], F32, name=f"dense{b}{h}", align_bytes=64, offset=offset)

        def empty_half(b, h, place, columns=None):
            half_tile(b, h, place)
            nc.scalar.copy(dense[b, h][:], banks[b][:, halves[h]] if columns is None else columns)

        def scatter_half(b, h):
            entries = offsets[:, h * HALF // 16 : (h + 1) * HALF // 16]
            nc.scalar.activation(windows[b % WINDOWS][:].indirect(entries), dense[b, h][:], ACT.Copy)

        def store(b):
            nc.sync.dma_start(out[b * P : (b + 1) * P, :], windows[b % WINDOWS][:])

        def multiply_whole(b):
            for h in range(2):
                multiply(b, h, banks[b][:, halves[h]])

        def empty_whole(b, offset, copy):
            dense[b] = late.tile([P, N], F32, name=f"dense{b}", align_bytes=64, offset=SHARED + ROW + offset)
            copy(dense[b][:], banks[b][:])

        def place_on_vector(b):
            nc.vector.tensor_copy(windows[b % WINDOWS][:].indirect(offsets[:]), dense[b][:])
            store(b)

        half_tile(0, 0, 0)
        for q in range(2):
            multiply(0, 0, quarter_banks[q][:, :P], quarters[q])
            nc.scalar.copy(dense[0, 0][:, quarters[q]], quarter_banks[q][:, :P])
        scatter_half(0, 0)
        multiply(1, 0, banks[1][:, :HALF])
        empty_half(1, 0, 1)
        dense[0, 1] = late.tile([P, HALF], F32, name="dense01", align_bytes=64, offset=SHARED + ROW + 4 * N)
        dense[2] = late.tile([P, N], F32, name="dense2", align_bytes=64, offset=SHARED + ROW)
        multiply(2, 0, banks[2][:, :HALF])
        nc.vector.tensor_copy(dense[2][:, :HALF], banks[2][:, :HALF])
        multiply(0, 1, acc[1][:, :HALF])
        multiply(2, 1, banks[5][:, HALF:])
        multiply(1, 1, banks[1][:, HALF:])
        nc.vector.tensor_copy(dense[0, 1][:], acc[1][:, :HALF])
        nc.vector.tensor_copy(dense[2][:, HALF:], banks[5][:, HALF:])
        multiply(3, 0, acc[1][:, HALF:])
        multiply(3, 1, banks[3][:, HALF:])
        multiply_whole(4)
        nc.vector.tensor_copy(windows[0][:].indirect(offsets[:, HALF // 16 :]), dense[0, 1][:])
        store(0)
        zero_late(3, BEHIND + 3072)
        xm_grouped5 = late.tile(triple, BF16, name="xm_grouped5", align_bytes=64, offset=BEHIND)
        for u in range(3):
            nc.gpsimd.tensor_scalar(
                xm_grouped5[:, u * K_PASS : (u + 1) * K_PASS].rearrange("p (d t) -> p d t", t=PACK),
                xm_raw[5 + u].rearrange("p t d -> p d t"),
                1.0, 0.0, ALU.mult, ALU.add,
            )
        xm_grouped[5] = (xm_grouped5, 0)
        windows.append(keep.tile([P, T], F32, name="window4", tag="x11", align_bytes=64))
        nc.gpsimd.memset(windows[4][:], 0.0)
        scatter_half(1, 0)
        empty_half(1, 1, 0)
        empty_half(3, 0, 2, acc[1][:, HALF:])
        scatter_half(1, 1)
        store(1)
        place_on_vector(2)
        empty_whole(4, 4 * N, on_vector)
        quantize_xm(
            5,
            keep.tile([P, 3 * P], U32, name="xm_codes5", align_bytes=64),
            keep.tile([P, 3 * P], U8, name="xm_plane5", align_bytes=64),
            3,
        )
        for b in range(5, BLOCKS):
            multiply_whole(b)
        empty_half(3, 1, 1)
        scatter_half(3, 0)
        scatter_half(3, 1)
        store(3)
        place_on_vector(4)
        empty_half(5, 0, 0)
        empty_half(5, 1, 2)
        scatter_half(5, 0)
        empty_half(7, 0, 1)
        scatter_half(5, 1)
        store(5)
        empty_whole(6, 2 * N, on_vector)
        dense[7, 1] = late.tile([P, HALF], F32, name="dense71", align_bytes=64, offset=SHARED + ROW + 6 * N)
        nc.vector.tensor_copy(dense[7, 1][:], banks[7][:, HALF:])
        place_on_vector(6)
        scatter_half(7, 0)
        scatter_half(7, 1)
        store(7)
